import numpy as np, ml_dtypes
CORES = [2,3,42,43,82,83,122,123]
N = 8
BF = ml_dtypes.bfloat16
V, H, M, CAP, R = 2048, 128, 1, 32, 3
L = M * H
def lanes(t, r):
    c = (M * (N * t + r) + np.arange(M)) & 15
    return (16 * np.arange(H)[None, :] + c[:, None]).reshape(-1)
def pack(b, x, lm):
    return {"nb": np.ascontiguousarray(b.reshape(N, 128, V)).astype(np.float32), "xs": np.ascontiguousarray(x.reshape(N, 128, V)).astype(np.float32).astype(BF),
            "lim": np.ascontiguousarray(lm.reshape(N, 128, 1)).astype(np.int32)}
def parts(rng):
    dens = rng.choice(np.array([0.08, 0.25, 0.5, 0.8]), (N, 8, 1, V)); u = rng.random((N, 8, 16, V))
    h = np.minimum((V * u * u).astype(np.int64), V - 1)
    pool = rng.integers(V // 4, V, (8, 12)); known = pool[np.arange(8)[None, :, None, None], rng.integers(0, 12, (N, 8, 16, V))]
    h = np.where(rng.random((N, 8, 16, V)) < 0.35, known, h)
    b = np.where(rng.random((N, 8, 16, V)) < dens, h, V)
    top = np.where(rng.random((N, 8, 1, V)) < 0.02, 256, rng.choice(np.array([4, 16, 40, 64]), (N, 8, 1, V)))
    x = (top * rng.random((N, 8, 16, V))).astype(np.int64)
    lm = rng.permutation(np.array([6, 16, 28, 45, 70, 110, 180, 300]))[None, :, None] + rng.integers(0, 8, (N, 8, 16))
    return b, x, lm
def late(rng, b, x, lm, g):
    E = np.stack([np.append(rng.permutation(lanes(0, r)[:-1]), lanes(0, r)[-1])[-26:] for r in range(N)])
    C = np.stack([np.append(rng.permutation(lanes(1, r)[:-1]), lanes(1, r)[-1])[-14:] for r in range(N)])
    D = np.stack([rng.permutation(np.setdiff1d(lanes(2, r), E[r]))[:4] for r in range(N)])
    low = E[:, :12]; own = E[:, 12:18]; top = E[:, 18:]; lows = low.reshape(-1)
    pool = np.setdiff1d(np.arange(V), np.concatenate([E.reshape(-1), C.reshape(-1), D.reshape(-1)]))
    b[:, g] = rng.choice(pool, (N, 16, V)); x[:, g] = rng.integers(128, 256, (N, 16, V)); lm[:, g] = rng.integers(600, 1600, (N, 16))
    for r in range(N):
        b[r, g][:, E[r]] = V; b[r, g][:, C[r, :3]] = V
    for r in range(N):
        z = rng.permutation(pool)[:12]; x[r, g][:, z] = 255; x[r, g][rng.integers(0, 16, 12), z] = 254
        b[r, g][rng.integers(0, 16, 12), low[r]] = z
        p = rng.integers(0, 16, 8); b[r, g][p, top[r]] = rng.choice(pool, 8); b[r, g][(p + rng.integers(1, 16, 8)) & 15, top[r]] = rng.choice(pool, 8)
        q = (r + 1) % N; s = C[r, :6]; k = rng.integers(0, 16, 6); j = (k + rng.integers(1, 16, 6)) & 15
        b[q, g][k, own[q]] = s; b[r, g][k, s] = s; b[r, g][j, s] = own[q]
        for i in range(8):
            n = rng.permutation(lows)[:16]; n[12 + (i & 3)] = top[q, i] if i < 4 else top[0, i]
            b[r, g][:, C[r, 6 + i]] = n
        if r < N - 1:
            for i in range(4):
                n = rng.permutation(lows)[:16]; n[int(rng.integers(0, 16))] = top[0, 4 + i]
                b[r, g][:, D[r, i]] = n
def setup_inputs(rng):
    return pack(*parts(rng))
def setup_inputs_spread(rng):
    d = rng.random((N, 8, 1, V))
    b = np.where(rng.random((N, 8, 16, V)) < d * d * d, rng.integers(0, V, (N, 8, 16, V)), V)
    x = np.minimum((np.exp2(8 * rng.random((N, 8, 1, V))) * rng.random((N, 8, 16, V))).astype(np.int64), 255)
    lm = np.minimum((np.exp2(3 + 9 * rng.random((N, 8, 1))) * (0.5 + 0.5 * rng.random((N, 8, 16)))).astype(np.int64), 4079)
    return pack(b, x, lm)
def setup_inputs_ends(rng):
    x = 255 * np.where(rng.random((N, 8, 1, V)) < 0.5, rng.integers(0, 2, (N, 8, 1, V)), rng.integers(0, 2, (N, 8, 16, V)))
    x[:, 1::2, :, :16] = 255; x[:, 1::2, :, V - 1] = 255
    mode = rng.choice(np.array([0, 0, 1, 2, 2, 2, 3, 4]), (N, 8, 1, V)); coin = rng.integers(0, 2, (N, 8, 16, V))
    v = np.arange(V)[None, :]; p = np.arange(16)[:, None]
    b = np.where(mode == 0, 0, np.where(mode == 1, V, np.where(mode == 2, coin * V, np.where(mode == 3, np.where(coin == 1, p, V - 1), rng.integers(0, V + 1, (N, 8, 16, V))))))
    b[:, 0:6:2, :, 0:16:2] = V
    b[:, 3:6:2, :, 0:16] = V; b[:, 3:6:2, 5, 0:16] = 0
    b[N - 1, 7] = np.where((v >= V - 192) & (p == ((v >> 4) & 15)), V, 0)
    big = np.array([9, 16, 8, 16, 0, 9, 12, 16])[None, :, None]
    lm = np.where(np.argsort(rng.random((N, 8, 16)), axis=2) < big, 4079, 0)
    return pack(b, x, lm)
def setup_inputs_corners(rng):
    x = rng.integers(16, 32, (N, 8, 16, V)); x[..., V - 80:V - 16] = 255; x[..., V - 16:] = 0
    pos = np.argsort(rng.random((N, 8, 16, V)), axis=2)
    many = np.where((rng.random((N, 8, 16, V)) < 0.4) | (pos < 4), rng.integers(0, V - 16, (N, 8, 16, V)), V)
    one = np.where(pos == 0, rng.integers(0, V - 80, (N, 8, 16, V)), V)
    kind = rng.choice(np.array([0, 1, 2, 2]), (N, 8, 1, V)); counts = (CAP, CAP + 1, L, CAP - 1, 1, 0, CAP, 2)
    for q in range(N):
        v = lanes(0, q)
        for g in range(8):
            n = counts[(g + 3 * q) % 8]; o = rng.permutation(L)
            kind[q, g, 0, v[o[:n]]] = 0 if g % 4 == 2 else rng.integers(0, 2, n)
            kind[q, g, 0, v[o[n:]]] = rng.integers(1, 3, L - n) if g % 4 == 2 else 2
    b = np.where(kind == 0, V, np.where(kind == 1, one, many))
    lm = 40 + rng.integers(0, 8, (N, 8, 16)); o = np.argsort(rng.random((N, 8, 16)), axis=2)
    lm[:, 1::2] = np.where(o[:, 1::2] < 9, lm[:, 1::2], 0); lm[:, 2::4] = np.where(o[:, 2::4] < 8, lm[:, 2::4], 0)
    return pack(b, x, lm)
def setup_inputs_crowd(rng):
    b, x, lm = parts(rng)
    b[:, :4] = np.where(rng.random((N, 4, 16, V)) < 0.1, rng.integers(V - 128, V, (N, 4, 16, V)), V); b[:, :4, 0, :] = 0
    v = np.arange(V)
    for t in range(16 // (N * M)):
        c = (M * (N * t + N - 1)) & 15
        b[:, 1:4:2, 0, np.flatnonzero(((v & 15) == c) & ((v >> 4) % CAP == CAP - 1))] = V
    lm[:, :4] = 4079; x[:, :2] = 255
    b[:, 4:] = np.where(b[:, 4:] < V, rng.choice(np.array([0, 1, 18, 40, V - 1]), (N, 4, 16, V)), V); b[:, 4:, :, :48] = V
    return pack(b, x, lm)
def setup_inputs_alike(rng):
    b, x, lm = parts(rng)
    u = rng.random((N, 8, 3, V)); few = np.minimum((V * u * u).astype(np.int64), V - 1)
    few[:, :, 0] = np.where(rng.random((N, 8, V)) < 0.15, np.arange(V), few[:, :, 0])
    pool = rng.integers(V // 2, V, (8, 4)); few[:, :, 2] = pool[np.arange(8)[None, :, None], rng.integers(0, 4, (N, 8, V))]
    which = np.minimum(rng.integers(0, 3, (N, 8, 16, V)), rng.integers(0, 3, (N, 8, 1, V)))
    b = np.where(rng.random((N, 8, 16, V)) < rng.choice(np.array([0.4, 0.8, 1.0]), (N, 8, 1, V)), np.take_along_axis(few, which, 2), V)
    lm = np.minimum(4 * lm, 4079)
    late(rng, b, x, lm, int(rng.integers(0, 8)))
    return pack(b, x, lm)
def check_inputs(d):
    bad = []
    for k, lo, hi in (("nb", 0, V), ("xs", 0, 255), ("lim", 0, 4079)):
        a = np.asarray(d[k]).astype(np.float64)
        if not np.all((a >= lo) & (a <= hi)): bad.append("range of " + k)
        elif not np.all(a == np.floor(a)): bad.append("whole numbers in " + k)
    return bad
def reference(nb, xs, lim):
    b = nb.astype(np.int32).reshape(N, 8, 16, V); x = xs.astype(np.float32).astype(np.int32).reshape(N, 8, 16, V)
    lm = lim.astype(np.int64).reshape(N, 8, 16, 1)
    J = np.tile(np.arange(V), (8, 1)); gone = np.zeros((8, V), bool)
    A = [0] * N; g8 = np.arange(8)[:, None, None]
    for t in range(R):
        new = []
        for r in range(N):
            v = lanes(t, r); q = b[r][:, :, v]
            has = q < V; u = np.where(has, q, 0)
            n = J[g8, u]; elem = has & gone[g8, u]; var = has & ~elem
            at = n.reshape(8, 1, 16 * L)
            Q = np.take_along_axis(b[r], at, 2).reshape(8, 16, 16, L); X = np.take_along_axis(x[r], at, 2).reshape(8, 16, 16, L)
            ek = elem[:, None]
            cov = var & np.any((Q == q[:, :, None, :]) & ek, axis=2)
            unc = var & ~cov
            deg = np.sum(np.where(unc[:, None], X, 0), axis=2) + np.max(np.where(ek, X, 0), axis=2)
            live = ~gone[:, v]
            hit = live & (np.sum(deg <= lm[r] + (A[r] & 7), axis=1) >= 9)
            piv = hit & (np.add.accumulate(hit.astype(np.int64), axis=1) <= CAP)
            col = np.minimum(np.where(unc & (q != v), q, V), np.min(np.where(ek & (Q != v), Q, V), axis=2))
            S = np.where(elem, np.sum(X, axis=1), -1); k = np.argmax(S, axis=1)
            e = np.take_along_axis(n, k[:, None, :], 1)[:, 0, :]
            b[r][:, :, v] = np.where(cov & (live & ~piv)[:, None, :], V, q)
            new.append((v, piv, col, np.minimum(deg, 255), e, piv & np.any(elem, axis=1)))
        for g in range(8):
            es = []; vs = []
            for v, piv, col, sz, e, cl in new:
                w = np.flatnonzero(piv[g]); b[:, g][:, :, v[w]] = col[g][:, w]; x[:, g][:, :, v[w]] = sz[g][:, w]; gone[g, v[w]] = True
                w = np.flatnonzero(cl[g]); es.append(e[g][w]); vs.append(v[w])
            ue, ui = np.unique(np.concatenate(es), return_index=True)
            J[g, ue] = np.concatenate(vs)[ui]
            J[g] = J[g][J[g]]
        A = [int(np.sum(a[1])) for a in new]
    return {"yn": b.reshape(N, 128, V).astype(np.float32), "yx": x.reshape(N, 128, V).astype(np.float32).astype(BF), "yj": np.stack([J] * N).astype(np.float32)}

@@ -1,0 +1,490 @@
+from concourse.bass import DstId, RemoteDMATransfer
+from concourse.mybir import AluOpType, AxisListType, ActivationFunctionType
+
+W = 2368
+F, B, I, U = "float32", "bfloat16", "int32", "uint16"
+SCRATCH = {}
+for _names, _w, _d in (
+        ("NX", 2 * W, F), ("NB JT", W, F), ("XS", W, B), ("SA EQ XG XV MX RSM", 2048, B), ("SAF QR YJ", 2048, F),
+        ("RSTB Q2 KS CC NS", 512, F), ("KC X2 MM RST", 512, B), ("ONEB IDB I4 BO BO32 TRI HR HT PV PVB", 128, B), ("CMP", 256, B),
+        ("IDF BOF TQ UA UN THR DQ", 128, F), ("SB", 256, F), ("WTS PR", 2, B), ("KB MB", 64, B), ("K4", 32, B),
+        ("PI PA LIMI AI AM", 1, I), ("PF LIMA", 1, F), ("COL", 8, F), ("CA CB CM CV IO16", 16, F),
+        ("LT VT0 VT1 QT0 QT1 QT2 QX0 QX1 QX2 QC OWN SZ", 136, F), ("OQ0 OQ1 OQ2 UL JL", 128, U),
+        ("IO32 D2 QM OP NM OH PD TM TM2 TL TL2 JE", 32, F), ("IO64 MF ED EM DX R32", 64, F), ("LW UW", 2, U), ("EP L16", 32, U), ("KI K5", 32, I),
+        ("NV0 NV1 NV2 SV0 SV1 SV5", 256, U), ("OF0 OF1 OF5 OE3", 16, U), ("OE4", 32, U)):
+    for _n in _names.split():
+        SCRATCH[_n] = ("sbuf", [128, _w], _d)
+for _b in range(6):
+    SCRATCH["LD%d" % _b] = ("sbuf", [128, 8, 104], U)
+for _b in range(8):
+    SCRATCH["P%d" % _b] = ("psum", [128, 512], F)
+SEMAPHORES = ["ev", "et", "ea", "eg", "d_x", "d_n0", "d_n1", "d_n2", "d_l", "o_n", "o_x", "o_j0", "o_j1"]
+SEMAPHORES += ["a%d_%d" % (m, r) for m in range(6) for r in range(8)] + ["l%d" % m for m in range(6)]
+VOFF, SIZES, NAMES, EOFF2, EOFF, VREP = 0, 2, 34, 66, 68, 70
+SPAN = [(0, 66), (0, 66), (34, 66), (68, 102), (66, 102), (0, 34)]
+
+
+def rank_program(g, core, T, topo):
+    rank = T.rank_of(core)
+    if rank is None:
+        return
+    A = AluOpType
+    IDN = ActivationFunctionType.Identity
+    Q = {"v": g.vector, "t": g.tensor, "a": g.scalar, "g": g, "s": g.sync}
+    cnt, wr, rd, nloc = {}, {}, {}, {}
+    known = {q: {} for q in Q}
+
+    def bank(k):
+        return k[0] == "P" and k[1:].isdigit()
+
+    def pre(q, R, Wk):
+        evs = []
+        for k in R:
+            evs += wr.get(k, [])
+            if bank(k):
+                evs += [e for e in rd.get(k, []) if e[0] != q]
+        for k in Wk:
+            part = q == "t" or k[0] == "+"
+            k = k.lstrip("+")
+            evs += [e for e in wr.get(k, []) if not part or e[0] != q] + rd.get(k, [])
+        top = {}
+        for e in evs:
+            top[e[1]] = max(top.get(e[1], 0), e[2])
+        for e in sorted(evs, key=lambda e: -len(e[3])):
+            if top[e[1]] == e[2] and known[q].get(e[1], 0) < e[2]:
+                Q[q].wait_ge(T.sem[e[1]], e[2])
+                for s, n in e[3].items():
+                    known[q][s] = max(known[q].get(s, 0), n)
+                known[q][e[1]] = e[2]
+
+    def post(q, by, sem, n, R, Wk):
+        ck = dict(known[by])
+        ck[sem] = n
+        ev = (q, sem, n, ck)
+        Wk = [k.lstrip("+") for k in Wk]
+        for k in Wk:
+            wr[k] = [ev]
+            rd[k] = []
+        for k in R:
+            if k not in Wk:
+                rd[k] = [e for e in rd.get(k, []) if e[0] != q] + [ev]
+
+    def op(q, f, R, Wk):
+        R, Wk = R.split(), Wk.split()
+        pre(q, R, Wk)
+        cnt[q] = cnt.get(q, 0) + 1
+        f().then_inc(T.sem["e" + q], 1)
+        post(q, q, "e" + q, cnt[q], R, Wk)
+
+    def dma(q, out, in_, sem, R, Wk):
+        R, Wk = R.split(), Wk.split()
+        pre(q, R, Wk)
+        Q[q].dma_start(out, in_).then_inc(T.sem[sem], 16)
+        post(sem, q, sem, 16, R, Wk)
+
+    V = g.vector
+
+    def cp(out, in_, R, Wk):
+        op("v", lambda: V.tensor_copy(out=out, in_=in_), R, Wk)
+
+    def ts(out, in0, s1, o0, R, Wk, s2=None, o1=None):
+        if o1 is None:
+            op("v", lambda: V.tensor_scalar(out=out, in0=in0, scalar1=s1, scalar2=None, op0=o0), R, Wk)
+        else:
+            op("v", lambda: V.tensor_scalar(out=out, in0=in0, scalar1=s1, scalar2=s2, op0=o0, op1=o1), R, Wk)
+
+    def tt(out, in0, in1, o, R, Wk):
+        op("v", lambda: V.tensor_tensor(out=out, in0=in0, in1=in1, op=o), R, Wk)
+
+    def scan(out, d0, d1, init, o0, o1, R, Wk):
+        op("v", lambda: V.tensor_tensor_scan(out=out, data0=d0, data1=d1, initial=init, op0=o0, op1=o1), R, Wk)
+
+    def fill(ap, c, Wk):
+        op("v", lambda: V.memset(ap, c), "", Wk)
+
+    def mm(out, l, r, start, stop, R, Wk):
+        op("t", lambda: g.tensor.matmul(out=out, lhsT=l, rhs=r, start=start, stop=stop), R, Wk)
+
+    def act(out, in_, R, Wk, func=ActivationFunctionType.Copy, bias=0.0, scale=1.0):
+        op("a", lambda: g.scalar.activation(out=out, in_=in_, func=func, bias=bias, scale=scale), R, Wk)
+
+    def iota(out, pat, base, cm, Wk):
+        op("g", lambda: g.iota(out, pat, base, cm, allow_small_or_imprecise_dtypes=True), "", Wk)
+
+    def asel(out, in_, pat, o, fl, base, cm, R, Wk):
+        op("g", lambda: g.affine_select(out, in_, pat, o, fl, base, cm), R, Wk)
+
+    cls = [rank, 8 + rank, rank]
+    VTs = ["VT0", "VT1", "VT0"]
+    NBK = "NB0 NB1 NB2"
+    TAB = {"NB": T.NB[:, 0:W], "XS": T.XS[:, 0:W], "NE": T.NX[:, 0:W], "XE": T.NX[:, W:2 * W], "JT": T.JT[:, 0:W]}
+    NEW, XEW = T.NX[:, 0:2080], T.NX[:, W:W + 2080]
+
+    dma("s", T.NB[:, 16:1040], T.nb[:, 0:1024], "d_n0", "", "NB0")
+    dma("a", T.XS[:, 16:2064], T.xs[:, :], "d_x", "", "XS")
+    dma("s", T.NB[:, 1040:1552], T.nb[:, 1024:1536], "d_n1", "", "NB1")
+    dma("s", T.NB[:, 1552:2064], T.nb[:, 1536:2048], "d_n2", "", "NB2")
+    dma("s", T.LIMI[:, :], T.lim[:, :], "d_l", "", "LIMI")
+
+    fill(T.ONEB[:, :], 1.0, "ONEB")
+    fill(T.WTS[:, 0:1], 1.0, "+WTS")
+    fill(T.WTS[:, 1:2], 16.0, "+WTS")
+    fill(T.XS[:, 0:16], 0.0, "+XSp")
+    fill(T.XS[:, 2064:W], 0.0, "+XSp")
+    asel(T.IDB[:, :], T.ONEB[:, :], [[-1, 128]], A.is_equal, 0.0, 0, 1, "ONEB", "IDB")
+    asel(T.BO[:, :], T.ONEB[:, :], [[-16, 8], [0, 16]], A.is_ge, 0.0, 0, 1, "ONEB", "BO")
+    asel(T.BO[:, :], T.BO[:, :], [[16, 8], [0, 16]], A.is_ge, 0.0, 15, -1, "BO", "BO")
+    asel(T.TRI[:, :], T.ONEB[:, :], [[1, 128]], A.is_ge, 0.0, 0, -1, "ONEB", "TRI")
+    asel(T.WTS[:, 1:2], T.WTS[:, 1:2], [[0, 1]], A.not_equal, 384.0, -127, 1, "WTS", "WTS")
+    op("g", lambda: g.iota(T.PI[:, :], [[0, 1]], 0, 1), "", "PI")
+    iota(T.VT0[:, :], [[16, 136]], cls[0], 0, "VT0")
+    iota(T.SB[:, :], [[16, 2], [0, 8], [1, 16]], 0, 0, "SB")
+    iota(T.IO16[:, :], [[1, 16]], 0, 0, "IO16")
+    iota(T.IO32[:, :], [[0, 2], [1, 16]], 0, 0, "IO32")
+    iota(T.IO64[:, :], [[-16, 2], [1, 32]], 0, 0, "IO64")
+    iota(T.LT[:, :], [[1, 136]], 0, 0, "LT")
+    iota(T.VT1[:, :], [[16, 136]], cls[1], 0, "VT1")
+    iota(T.KC[:, :], [[0, 32], [-1, 16]], 31, 0, "KC")
+    iota(T.NX[:, 0:W], [[0, W]], 2050, 0, "NE")
+    for n in ("QT0", "QT1", "QT2"):
+        fill(T[n][:, 128:136], 2048.0, n + "p")
+    for n in ("QX0", "OWN"):
+        fill(T[n][:, 128:136], 4096.0, n + "p")
+    fill(T.SZ[:, 128:136], 0.0, "SZp")
+    fill(T.KB[:, :], 131072.0, "KB")
+    fill(T.K4[:, :], 4096.0, "K4")
+    fill(T.RST[:, :], 1.0, "RST")
+    fill(T.RST[:, 0:512:16], 0.0, "RST")
+    fill(T.R32[:, :], 1.0, "R32")
+    fill(T.R32[:, 0:64:32], 0.0, "R32")
+    fill(T.RSTB[:, :], 0.0, "RSTB")
+    fill(T.RSTB[:, 0:512:16], 8192.0, "RSTB")
+    ts(T.PA[:, :], T.PI[:, :], 15, A.bitwise_and, "PI", "PA")
+    cp(T.PF[:, :], T.PA[:, :], "PA", "PF")
+    ts(T.COL[:, 0:1], T.PF[:, :], -1.0, A.mult, "PF", "+COL", 31.0, A.add)
+    for j, b in enumerate((2080 + 32 * rank, 2096 + 32 * rank, 2336, 2352)):
+        ts(T.COL[:, j + 1:j + 2], T.PF[:, :], float(b), A.add, "PF", "+COL")
+    CODE, TRV, TRE = T.COL[:, 0:1], [T.COL[:, 1:2], T.COL[:, 2:3]], [T.COL[:, 3:4], T.COL[:, 4:5]]
+    ts(T.CB[:, :], T.IO16[:, :], T.PF[:, 0:1], A.is_equal, "IO16 PF", "CB")
+    ts(T.CM[:, :], T.IO16[:, :], T.PF[:, 0:1], A.not_equal, "IO16 PF", "CM")
+    ts(T.CV[:, :], T.CB[:, :], 2050.0, A.mult, "CB", "CV")
+    ts(T.CA[:, :], T.CB[:, :], -126976.0, A.mult, "CB", "CA", -4096.0, A.add)
+    cp(T.IDF[:, :], T.IDB[:, :], "IDB", "IDF")
+    ts(T.BO32[:, :], T.BO[:, :], 32.0, A.mult, "BO", "BO32")
+    ts(T.I4[:, :], T.IDB[:, :], 4096.0, A.mult, "IDB", "I4")
+    ts(T.D2[:, :], T.IO32[:, :], T.PF[:, 0:1], A.is_equal, "IO32 PF", "D2")
+    ts(T.MF[:, :], T.IO64[:, :], T.PF[:, 0:1], A.is_ge, "IO64 PF", "MF", 8192.0, A.mult)
+    ts(T.MB[:, :], T.MF[:, :], 4096.0, A.add, "MF", "MB")
+    cp(T.BOF[:, :], T.BO[:, :], "BO", "BOF")
+
+    def names_of(t, a, b):
+        return T.NB[:, 16 + 16 * a + cls[t]:16 + 16 * b:16]
+
+    def mine(m, a, n):
+        return T["LD%d" % m][:, rank, a:a + n]
+
+    def key(m, r):
+        return "M%d" % m if r == rank else "LD%d_%d" % (m, r)
+
+    def self_out(t):
+        n, vt, qt = "QX%d" % t, VTs[t], "QT%d" % t
+        tt(T.TQ[:, :], T[qt][:, 0:128], T[vt][:, 0:128], A.is_equal, qt + " " + vt, "TQ")
+        ts(T.TQ[:, :], T.TQ[:, :], 4096.0, A.mult, "TQ", "TQ")
+        tt(T[n][:, 0:128], T.TQ[:, :], T[qt][:, 0:128], A.max, "TQ " + qt, n)
+
+    def repeat_names(t):
+        qt = "QT%d" % t
+
+        def copies():
+            for k in range(16):
+                act(T.QR[:, k:2048:16], T.QC[:, 0:128], "QC CM CV", "+QR", func=IDN, bias=T.CV[:, k:k + 1], scale=T.CM[:, k:k + 1])
+        return [lambda: ts(T.TQ[:, :], T[qt][:, 0:128], 2048.0, A.is_equal, qt, "TQ", 2048.0, A.mult),
+                lambda: tt(T.QC[:, 0:128], T.TQ[:, :], T[qt][:, 0:128], A.add, "TQ " + qt, "QC"), copies]
+
+    def gather_sizes(q, lst, a, b):
+        f = cp if q == "v" else act
+        f(T.XV[:, 16 * a:16 * b], T.XS[:, 0:2080].indirect(T[lst[:-2]][:, a:b]), "XS XSp " + lst, "XV%d" % a)
+
+    def degrees(a, b, keys, mx):
+        o = T.P2[:, a:b]
+        if mx:
+            mm(o, T.IDB[:, :], T.MX[:, 16 * a + 15:16 * b:16], True, False, "IDB MX", "P2")
+        for k in range(16):
+            mm(o, T.IDB[:, :], T.XV[:, 16 * a + k:16 * b:16], k == 0 and not mx, k == 15, "IDB " + keys, "P2")
+
+    gaps = {}
+
+    def gap(t, at):
+        for f in gaps.get((t, at), ()):
+            f()
+
+    def select(t):
+        ts(T.HR[:, :], T.P2[:, 0:128], T.LIMA[:, 0:1], A.is_le, "P2 LIMA", "HR")
+        mm(T.P3[:, 0:128], T.HR[:, :], T.BO[:, :], True, True, "HR BO", "P3")
+        ts(T.SZ[:, 0:128], T.P2[:, 0:128], 255.0, A.min, "P2", "SZ")
+        if t:
+            tt(T.OWN[:, 0:128], T.UA[:, :], T["QX%d" % t][:, 0:128], A.max, "UA QX%d" % t, "OWN")
+        if t < 2:
+            ts(T.HT[:, :], T.P3[:, 0:128], 9.0, A.is_ge, "P3", "HT")
+        else:
+            tt(T.HT[:, :], T.P3[:, 0:128], T.THR[:, :], A.is_ge, "P3 THR", "HT")
+        for b in range(2):
+            mm(T.P4[:, 128 * b:128 * b + 128], T.TRI[:, :], T.HT[:, :], True, True, "TRI HT", "P4")
+        gap(t, "rank")
+        tt(T.CMP[:, :], T.P4[:, 0:256], T.SB[:, :], A.is_le, "P4 SB", "CMP")
+        for b in range(2):
+            mm(T.P5[:, 2 * b:2 * b + 2], T.CMP[:, 128 * b:128 * b + 128], T.WTS[:, :], True, True, "CMP WTS", "P5")
+        gap(t, "lanes")
+        cp(T.LW[:, :], T.P5[:, 0:4:2], "P5", "LW")
+
+    ahead = [0, 1, 5]
+
+    def places(t):
+        for b in range(2):
+            ts(mine(ahead[t], VOFF + b, 1), T.P5[:, 2 * b + 1:2 * b + 2], float(cls[t] + 16), A.add, "P5 COL", "+M%d" % ahead[t], TRV[b], A.min)
+
+    def at_pivots(buf):
+        return T[buf][:, 0:136].indirect(T.LW[:, :])
+
+    near = [c for c in T.cores if topo.chip(c) == topo.chip(core) and c != core]
+    far = [c for c in T.cores if topo.chip(c) != topo.chip(core)]
+    fe = topo.engines(core, far[0])
+    ne = [e for e in topo.engines(core, near[0]) if e not in fe][:2]
+
+    def send(m):
+        a, b = SPAN[m]
+        tr = []
+        for cs, es in ((far, fe), (near, ne)):
+            ids = [DstId(rid=topo.addr(c)[0], pnc=topo.addr(c)[1]) for c in cs]
+            tr.append(RemoteDMATransfer(dst_ids=ids, dma_engine_mask=sum(1 << e for e in es), remote_sem=T.sem["a%d_%d" % (m, rank)],
+                                        srcs=[mine(m, a, b - a)], dsts=[mine(m, a, b - a)] * len(cs)))
+        pre("g", ["M%d" % m], [])
+        g.remote_dma_fused(tr, local_sem=T.sem["l%d" % m])
+        nloc[m] = len(fe) + len(ne)
+        post("l%d" % m, "g", "l%d" % m, nloc[m], ["M%d" % m], [])
+        for r in range(8):
+            if r != rank:
+                wr["LD%d_%d" % (m, r)] = [("r", "a%d_%d" % (m, r), len(ne) if T.cores[r] in near else len(fe), {})]
+
+    def unpack(m, buf, a, n):
+        cp(T["%s%d" % (buf, m)][:, :], T["LD%d" % m][:, :, a:a + n], " ".join(key(m, r) for r in range(8)), "%s%d" % (buf, m))
+
+    def pivots(tab, m, val, keys, o=None):
+        o = m if o is None else o
+        cp(TAB[tab].indirect(T["OF%d" % o][:, :]), T["%s%d" % (val, m)][:, :], "OF%d %s%d" % (o, val, m), keys)
+
+    def new_j(m, n, r):
+        cp(TAB["JT"].indirect(T["OE%d" % m][:, n * r + n - 2:n * r + n]), T["LD%d" % m][:, r, VREP:VREP + 32], "OE%d %s" % (m, key(m, r)), "JT")
+
+    def update(m):
+        unpack(m, "OF", VOFF, 2)
+        unpack(m, "SV", SIZES, 32)
+        pivots("XE", m, "SV", "XE")
+        unpack(m, "NV", NAMES, 32)
+        pivots("NE", m, "NV", "NE")
+
+    def count():
+        ts(T.PR[:, :], T.P5[:, 0:4:2], 127.5, A.is_le, "P5", "PR")
+        for b in range(2):
+            mm(T.P2[:, 0:1], T.ONEB[:, :], T.PR[:, b:b + 1], b == 0, b == 1, "ONEB PR", "P2")
+        cp(T.AI[:, :], T.P2[:, 0:1], "P2", "AI")
+        ts(T.AM[:, :], T.AI[:, :], 7, A.bitwise_and, "AI", "AM")
+        tt(T.LIMA[:, :], T.AM[:, :], T.LIMI[:, :], A.add, "AM LIMI", "LIMA")
+
+    def empty_covered(t):
+        for h in range(2):
+            ts(T.UN[:, 64 * h:64 * h + 64], T["P%d" % h][:, 0:64], 0.0, A.is_lt, "P%d" % h, "+UN", 2048.0, A.mult)
+        tt(names_of(t, 0, 128), T.UN[:, :], names_of(t, 0, 128), A.max, "UN " + NBK, NBK)
+
+    def claim_keys():
+        mm(T.P6[:, :], T.BO32[:, :], T.X2[:, :], False, True, "BO32 X2", "P6")
+
+    def best_key():
+        scan(T.KS[:, :], T.RST[:, :], T.P6[:, :], 0.0, A.mult, A.max, "RST P6", "KS")
+
+    def lanes_to_pivots(t):
+        qt, oq = "QT%d" % t, "OQ%d" % t
+        for h in range(2):
+            act(T.XG[:, 1024 * h:1024 * h + 1024], XEW.indirect(T[oq][:, 64 * h:64 * h + 64]), "XE " + oq, "XG%d" % h)
+
+        def cover(a, b, k):
+            tt(T.EQ[:, 16 * a:16 * b], NEW.indirect(T[oq][:, a:b]), T.QR[:, 16 * a:16 * b], A.is_equal, "NE QR " + oq, k)
+        cover(0, 64, "EQ0")
+        cover(64, 96, "EQ1")
+        for h in range(2):
+            o = T["P%d" % h][:, 0:64]
+            mm(o, T.IDF[:, :], T[qt][:, 64 * h:64 * h + 64], True, False, "IDF " + qt, "P%d" % h)
+            mm(o, T.IDB[:, :], T.KB[:, 0:64], False, False, "IDB KB", "P%d" % h)
+        for h in range(2):
+            if h:
+                ts(T.UL[:, 0:64], T.P0[:, 0:64], 16.0, A.add, "P0", "UL_0", 2064.0, A.min)
+                cover(96, 128, "EQ2")
+            for k in range(16):
+                mm(T["P%d" % h][:, 0:64], T.SA[:, 128 * k:128 * k + 128], T.EQ[:, 1024 * h + k:1024 * h + 1024:16], False, k == 15,
+                   "SA " + ("EQ1 EQ2" if h else "EQ0"), "P%d" % h)
+        gather_sizes("a", "UL_0", 0, 64)
+        scan(T.MX[:, :], T.RSM[:, :], T.XG[:, :], 0.0, A.min, A.max, "RSM XG0 XG1", "MX")
+        ts(T.UL[:, 64:128], T.P1[:, 0:64], 16.0, A.add, "P1", "UL_1", 2064.0, A.min)
+        gather_sizes("a", "UL_1", 64, 96)
+        gather_sizes("v", "UL_1", 96, 128)
+        empty_covered(t)
+        gap(t, "degrees")
+        degrees(0, 64, "XV0", True)
+        degrees(64, 128, "XV64 XV96", True)
+        for h in range(2):
+            act(T.UA[:, 64 * h:64 * h + 64], T["P%d" % h][:, 0:64], "P%d" % h, "+UA", func=ActivationFunctionType.Abs)
+        mm(T.P6[:, :], T.IDB[:, :], T.KC[:, :], True, False, "IDB KC", "P6")
+        select(t)
+        ts(T.EP[:, :], at_pivots(qt), 16.0, A.add, "%s %sp LW" % (qt, qt), "EP")
+        act(T.Q2[:, :], NEW.indirect(T.EP[:, :]), "NE EP", "Q2")
+        act(T.X2[:, :], XEW.indirect(T.EP[:, :]), "XE EP", "X2")
+        cp(T.L16[:, :], at_pivots("LT"), "LT LW", "L16")
+        cp(mine(ahead[t], SIZES, 32), at_pivots("SZ"), "SZ SZp LW", "+M%d" % ahead[t])
+        places(t)
+        if t == 2:
+            send(5)
+        ts(T.QM[:, :], at_pivots(qt), -4080.0, A.add, "%s %sp LW" % (qt, qt), "QM")
+        cp(T.OP[:, :], at_pivots("OWN"), "OWN OWNp LW", "OP")
+        m = 4 if t == 1 else 3
+        ts(mine(m, VREP, 32), at_pivots(VTs[t]), 16.0, A.add, VTs[t] + " LW", "+M%d" % m)
+
+    def new_names(t):
+        vt = VTs[t]
+        if t == 1:
+            claim_keys()
+        tt(T.MM[:, :], T[vt][:, 0:136].indirect(T.L16[:, :]), T.Q2[:, :], A.is_equal, vt + " L16 Q2", "MM")
+        mm(T.P7[:, :], T.I4[:, :], T.MM[:, :], True, True, "I4 MM", "P7")
+        gap(t, "names")
+        tt(T.CC[:, :], T.Q2[:, :], T.P7[:, :], A.add, "Q2 P7", "CC")
+        scan(T.NS[:, :], T.RSTB[:, :], T.CC[:, :], 8192.0, A.add, A.min, "RSTB CC", "NS")
+        tt(T.NM[:, :], T.NS[:, 15:512:16], T.OP[:, :], A.min, "NS OP", "NM")
+        ts(mine(t, NAMES, 32), T.NM[:, :], 2048.0, A.min, "NM", "+M%d" % t)
+
+    def win_row(t):
+        if t == 2:
+            claim_keys()
+            best_key()
+        cp(T.KI[:, :], T.KS[:, 15:512:16], "KS", "KI")
+        ts(T.K5[:, :], T.KI[:, :], 31, A.bitwise_and, "KI", "K5")
+        ts(T.OH[:, :], T.K5[:, :], CODE, A.is_equal, "K5 COL", "OH")
+        tt(T.PD[:, :], T.OH[:, :], T.QM[:, :], A.mult, "OH QM", "PD")
+        mm(T.P3[:, 0:32], T.IDB[:, :], T.K4[:, :], True, False, "IDB K4", "P3")
+        mm(T.P3[:, 0:32], T.BOF[:, :], T.PD[:, :], False, True, "BOF PD", "P3")
+        for b in range(2 if t == 1 else 0):
+            o = T.P4[:, 32 * b:32 * b + 32]
+            mm(o, T.IDB[:, :], T.MB[:, 32 * b:32 * b + 32], True, False, "IDB MB", "P4")
+            mm(o, T.BOF[:, :], T.PD[:, :], False, True, "BOF PD", "P4")
+
+    def as_list(rk, rep, tm, tl):
+        tt(T[tm][:, :], rep, T.D2[:, :], A.mult, rk + " D2", tm)
+        scan(T[tl][:, :], T.RST[:, 0:32], T[tm][:, :], 0.0, A.mult, A.add, "RST " + tm, tl)
+
+    def claims(m, em, ek, tl):
+        col = [T[tl][:, 15:16], T[tl][:, 31:32]]
+        for b in range(2):
+            ts(T.ED[:, 32 * b:32 * b + 32], em[:, 32 * b:32 * b + 32], col[b], A.is_equal, ek + " " + tl, "+ED", 4096.0, A.mult)
+        scan(T.DX[:, :], T.R32[:, :], T.ED[:, :], 0.0, A.mult, A.max, "R32 ED", "DX")
+        for b in range(2):
+            ts(mine(m, EOFF + b, 1), T.DX[:, 32 * b + 31:32 * b + 32], col[b], A.max, "DX COL " + tl, "+M%d" % m, TRE[b], A.min)
+        if m == 4:
+            ts(mine(m, EOFF2, 2), mine(m, EOFF, 2), float(W), A.add, "M4", "+M4")
+
+    for j, (a, b) in enumerate(((0, 64), (64, 96), (96, 128))):
+        c = (a + b) // 2
+        ts(T.OQ0[:, a:b], names_of(0, a, b), 16.0, A.add, "NB%d" % j, "OQ0_%d" % j)
+        gather_sizes("a", "OQ0_%d" % j, a, c)
+        gather_sizes("v", "OQ0_%d" % j, c, b)
+        degrees(a, b, "XV%d XV%d" % (a, c), False)
+        cp(T.QT0[:, a:b], names_of(0, a, b), "NB%d" % j, "+QT0")
+    act(T.NX[:, W:2 * W], T.NX[:, 0:W], "NE", "XE", func=IDN, bias=-1.0, scale=0.0)
+    for k in range(16):
+        act(T.SA[:, 128 * k:128 * k + 128], T.IDB[:, :], "IDB CA", "+SA", scale=T.CA[:, k:k + 1])
+    self_out(0)
+    cp(T.LIMA[:, :], T.LIMI[:, :], "LIMI", "LIMA")
+    select(0)
+    ts(mine(0, NAMES, 32), at_pivots("QX0"), 2048.0, A.min, "QX0 QX0p LW", "+M0")
+    cp(mine(0, SIZES, 32), at_pivots("SZ"), "SZ SZp LW", "+M0")
+    places(0)
+    send(0)
+
+    cp(T.QT1[:, 0:128], names_of(1, 0, 128), NBK, "QT1")
+    for f in repeat_names(1):
+        f()
+    ts(T.OQ1[:, :], T.QT1[:, 0:128], 16.0, A.add, "QT1", "OQ1")
+    count()
+    ts(T.PV[:, :], T.P4[:, 0:128], 32.0, A.is_le, "P4", "PV")
+    tt(T.PVB[:, :], T.PV[:, :], T.HT[:, :], A.mult, "PV HT", "PVB")
+    mm(T.P7[:, 0:128], T.PVB[:, :], T.IDB[:, :], True, True, "PVB IDB", "P7")
+    ts(T.THR[:, :], T.PVB[:, :], 100.0, A.mult, "PVB", "THR", 9.0, A.add)
+    self_out(1)
+    ts(T.DQ[:, :], T.P7[:, 0:128], 2048.0, A.mult, "P7", "DQ")
+    tt(T.QT2[:, 0:128], T.DQ[:, :], T.QT0[:, 0:128], A.max, "DQ QT0", "QT2")
+    ts(T.OQ2[:, :], T.QT2[:, 0:128], 16.0, A.add, "QT2", "OQ2")
+    self_out(2)
+    iota(T.RSM[:, :], [[0, 128], [256, 16]], 0, 0, "RSM")
+    iota(T.JT[:, 0:2064], [[1, 2064]], 0, 0, "JT")
+    iota(T.JT[:, 2064:2072], [[0, 8]], 4096, 0, "+JT")
+
+    update(0)
+    more = repeat_names(2)
+    gaps[1, "rank"], gaps[1, "lanes"], gaps[1, "names"] = more[:1], more[1:2], [best_key, more[2]]
+    lanes_to_pivots(1)
+    new_names(1)
+    send(1)
+    win_row(1)
+    as_list("P3", T.P3[:, 0:32], "TM", "TL")
+    claims(4, T.P4, "P4", "TL")
+    send(4)
+    for k in range(16):
+        act(T.SAF[:, 128 * k:128 * k + 128], T.IDF[:, :], "IDF CB", "+SAF", scale=T.CB[:, k:k + 1])
+    count()
+    pivots("NB", 0, "NV", NBK)
+    pivots("XS", 0, "SV", "XS")
+
+    update(1)
+    unpack(4, "OE", EOFF2, 4)
+    for r in range(7, -1, -1):
+        cp(T.NX[:, 0:2 * W].indirect(T.OE4[:, 4 * r:4 * r + 4]), T.LD1[:, r, SIZES:SIZES + 64], "OE4 " + key(1, r), "NE XE")
+    todo = [lambda r=r: new_j(4, 4, r) for r in range(7, -1, -1)]
+    gaps[2, "degrees"], gaps[2, "rank"], gaps[2, "lanes"], gaps[2, "names"] = todo[:1], todo[1:2], todo[2:3], todo[3:6]
+    lanes_to_pivots(2)
+    new_names(2)
+    send(2)
+    win_row(2)
+    for f in todo[6:]:
+        f()
+    for k in range(16):
+        mm(T.P5[:, 0:128], T.SAF[:, 128 * k:128 * k + 128], T.JT[:, 16 + k:2064:16], k == 0, k == 15, "SAF JT", "P5")
+    as_list("P3", T.P3[:, 0:32], "TM", "TL")
+    ts(T.UW[:, :], T.TL[:, 15:32:16], 2064.0, A.min, "TL", "UW")
+    cp(T.JE[:, :], T.JT[:, 0:2072].indirect(T.UW[:, :]), "JT UW", "JE")
+    as_list("JE", T.JE[:, :], "TM2", "TL2")
+    for b in range(2):
+        tt(T.EM[:, 32 * b:32 * b + 32], T.JE[:, :], T.MF[:, 32 * b:32 * b + 32], A.add, "JE MF", "+EM")
+    claims(3, T.EM, "EM", "TL2")
+    send(3)
+
+    pivots("XS", 1, "SV", "XS")
+    unpack(5, "OF", VOFF, 2)
+    unpack(5, "SV", SIZES, 32)
+    pivots("XS", 5, "SV", "XS")
+    dma("s", T.yx[:, :], T.XS[:, 16:2064], "o_x", "XS", "")
+    pivots("NB", 1, "NV", NBK)
+    unpack(2, "NV", NAMES, 32)
+    pivots("NB", 2, "NV", NBK, 5)
+    dma("s", T.yn[:, :], T.NB[:, 16:2064], "o_n", NBK, "")
+    cp(T.JL[:, :], T.P5[:, 0:128], "P5", "JL")
+    unpack(3, "OE", EOFF, 2)
+    for r in range(7, -1, -1):
+        new_j(3, 2, r)
+    act(T.YJ[:, 0:1024], T.JT[:, 0:2072].indirect(T.JL[:, 0:64]), "JT JL", "YJ0", func=IDN, bias=-16.0)
+    ts(T.YJ[:, 1024:2048], T.JT[:, 0:2072].indirect(T.JL[:, 64:128]), -16.0, A.add, "JT JL", "YJ1")
+    dma("a", T.yj[:, 0:1024], T.YJ[0:128:16, 0:1024], "o_j0", "YJ0", "")
+    dma("s", T.yj[:, 1024:2048], T.YJ[0:128:16, 1024:2048], "o_j1", "YJ1", "")
+
+    for q in ("v", "t", "a", "g"):
+        g.wait_ge(T.sem["e" + q], cnt[q])
+    for s in ("d_x", "d_n0", "d_n1", "d_n2", "d_l", "o_n", "o_x", "o_j0", "o_j1"):
+        g.wait_ge(T.sem[s], 16)
+    for m in range(6):
+        g.wait_ge(T.sem["l%d" % m], nloc[m])

@@ -5,23 +5,24 @@ W = 2368
 F, B, I, U = "float32", "bfloat16", "int32", "uint16"
 SCRATCH = {}
 for _names, _w, _d in (
-        ("NX", 2 * W, F), ("NB JT", W, F), ("XS", W, B), ("SA EQ XG XV MX RSM", 2048, B), ("SAF QR YJ", 2048, F),
-        ("RSTB Q2 KS CC NS", 512, F), ("KC X2 MM RST", 512, B), ("ONEB IDB I4 BO BO32 TRI HR HT PV PVB", 128, B), ("CMP", 256, B),
-        ("IDF BOF TQ UA UN THR DQ", 128, F), ("SB", 256, F), ("WTS PR", 2, B), ("KB MB", 64, B), ("K4", 32, B),
-        ("PI PA LIMI AI AM", 1, I), ("PF LIMA", 1, F), ("COL", 8, F), ("CA CB CM CV IO16", 16, F),
+        ("NB JT NE XE JF", W, F), ("XS", W, B), ("SA EQ XG XV MX RSM", 2048, B), ("SAF QR YJ", 2048, F),
+        ("Q2 KS CC NS", 512, F), ("E2", 520, F), ("KCA KCB X2 MM RST RSTB", 512, B), ("ONEB IDB I4 BO BOK TRI HR HT PV PVB", 128, B), ("CMP", 256, B),
+        ("IDF TQ UA UN THR DQ", 128, F), ("SB SVF VF", 256, F), ("WTS PR", 2, B), ("KB", 64, B),
+        ("PI PA LIMI AI AM", 1, I), ("PF LIMA LIMH", 1, F), ("COL", 8, F), ("CA CB CM CV IO16", 16, F),
         ("LT VT0 VT1 QT0 QT1 QT2 QX0 QX1 QX2 QC OWN SZ", 136, F), ("OQ0 OQ1 OQ2 UL JL", 128, U),
-        ("IO32 D2 QM OP NM OH PD TM TM2 TL TL2 JE", 32, F), ("IO64 MF ED EM DX R32", 64, F), ("LW UW", 2, U), ("EP L16", 32, U), ("KI K5", 32, I),
-        ("NV0 NV1 NV2 SV0 SV1 SV5", 256, U), ("OF0 OF1 OF5 OE3", 16, U), ("OE4", 32, U)):
+        ("IO32 D2 OP NM TM TM2 TL TL2", 32, F), ("IO66 RL ED DX", 66, F), ("LW UW", 2, U), ("EP L16", 32, U), ("KI K5 JE", 32, I),
+        ("OF0 OF1 OF5", 16, U), ("NV0 NV1 SV", 256, U)):
     for _n in _names.split():
         SCRATCH[_n] = ("sbuf", [128, _w], _d)
 for _b in range(6):
     SCRATCH["LD%d" % _b] = ("sbuf", [128, 8, 104], U)
+SCRATCH["LD2"] = ("sbuf", [128, 256], U)
 for _b in range(8):
     SCRATCH["P%d" % _b] = ("psum", [128, 512], F)
 SEMAPHORES = ["ev", "et", "ea", "eg", "d_x", "d_n0", "d_n1", "d_n2", "d_l", "o_n", "o_x", "o_j0", "o_j1"]
 SEMAPHORES += ["a%d_%d" % (m, r) for m in range(6) for r in range(8)] + ["l%d" % m for m in range(6)]
-VOFF, SIZES, NAMES, EOFF2, EOFF, VREP = 0, 2, 34, 66, 68, 70
-SPAN = [(0, 66), (0, 66), (34, 66), (68, 102), (66, 102), (0, 34)]
+VREP, VOFF, SIZES, NAMES, EOFF = 0, 32, 34, 66, 98
+SPAN = [(32, 98), (0, 98), (66, 98), (98, 100), (98, 100), (0, 66)]
 
 
 def rank_program(g, core, T, topo):
@@ -108,6 +109,15 @@ def rank_program(g, core, T, topo):
     def act(out, in_, R, Wk, func=ActivationFunctionType.Copy, bias=0.0, scale=1.0):
         op("a", lambda: g.scalar.activation(out=out, in_=in_, func=func, bias=bias, scale=scale), R, Wk)
 
+    def silu(out, in_, R, Wk):
+        op("a", lambda: g.scalar.activation(out=out, in_=in_, func=ActivationFunctionType.Silu), R, Wk)
+
+    def weave(*chains):
+        for j in range(max(len(c) for c in chains)):
+            for c in chains:
+                if j < len(c):
+                    c[j]()
+
     def iota(out, pat, base, cm, Wk):
         op("g", lambda: g.iota(out, pat, base, cm, allow_small_or_imprecise_dtypes=True), "", Wk)
 
@@ -117,70 +127,67 @@ def rank_program(g, core, T, topo):
     cls = [rank, 8 + rank, rank]
     VTs = ["VT0", "VT1", "VT0"]
     NBK = "NB0 NB1 NB2"
-    TAB = {"NB": T.NB[:, 0:W], "XS": T.XS[:, 0:W], "NE": T.NX[:, 0:W], "XE": T.NX[:, W:2 * W], "JT": T.JT[:, 0:W]}
-    NEW, XEW = T.NX[:, 0:2080], T.NX[:, W:W + 2080]
+    TAB = {n: T[n][:, 0:W] for n in ("NB", "XS", "NE", "XE", "JT", "JF")}
+    NEW, XEW = T.NE[:, 0:2080], T.XE[:, 0:2080]
 
-    dma("s", T.NB[:, 16:1040], T.nb[:, 0:1024], "d_n0", "", "NB0")
     dma("a", T.XS[:, 16:2064], T.xs[:, :], "d_x", "", "XS")
+    dma("s", T.NB[:, 16:1040], T.nb[:, 0:1024], "d_n0", "", "NB0")
+    dma("a", T.LIMI[:, :], T.lim[:, :], "d_l", "", "LIMI")
     dma("s", T.NB[:, 1040:1552], T.nb[:, 1024:1536], "d_n1", "", "NB1")
     dma("s", T.NB[:, 1552:2064], T.nb[:, 1536:2048], "d_n2", "", "NB2")
-    dma("s", T.LIMI[:, :], T.lim[:, :], "d_l", "", "LIMI")
 
     fill(T.ONEB[:, :], 1.0, "ONEB")
     fill(T.WTS[:, 0:1], 1.0, "+WTS")
     fill(T.WTS[:, 1:2], 16.0, "+WTS")
     fill(T.XS[:, 0:16], 0.0, "+XSp")
     fill(T.XS[:, 2064:W], 0.0, "+XSp")
+    op("g", lambda: g.iota(T.PI[:, :], [[0, 1]], 0, 1), "", "PI")
     asel(T.IDB[:, :], T.ONEB[:, :], [[-1, 128]], A.is_equal, 0.0, 0, 1, "ONEB", "IDB")
+    iota(T.IO16[:, :], [[1, 16]], 0, 0, "IO16")
+    iota(T.IO32[:, :], [[0, 2], [1, 16]], 0, 0, "IO32")
+    iota(T.IO66[:, :], [[-16, 2], [1, 33]], -1, 0, "IO66")
     asel(T.BO[:, :], T.ONEB[:, :], [[-16, 8], [0, 16]], A.is_ge, 0.0, 0, 1, "ONEB", "BO")
     asel(T.BO[:, :], T.BO[:, :], [[16, 8], [0, 16]], A.is_ge, 0.0, 15, -1, "BO", "BO")
     asel(T.TRI[:, :], T.ONEB[:, :], [[1, 128]], A.is_ge, 0.0, 0, -1, "ONEB", "TRI")
     asel(T.WTS[:, 1:2], T.WTS[:, 1:2], [[0, 1]], A.not_equal, 384.0, -127, 1, "WTS", "WTS")
-    op("g", lambda: g.iota(T.PI[:, :], [[0, 1]], 0, 1), "", "PI")
     iota(T.VT0[:, :], [[16, 136]], cls[0], 0, "VT0")
-    iota(T.SB[:, :], [[16, 2], [0, 8], [1, 16]], 0, 0, "SB")
-    iota(T.IO16[:, :], [[1, 16]], 0, 0, "IO16")
-    iota(T.IO32[:, :], [[0, 2], [1, 16]], 0, 0, "IO32")
-    iota(T.IO64[:, :], [[-16, 2], [1, 32]], 0, 0, "IO64")
+    iota(T.SB[:, :], [[-16, 2], [0, 8], [-1, 16]], 31, 0, "SB")
     iota(T.LT[:, :], [[1, 136]], 0, 0, "LT")
     iota(T.VT1[:, :], [[16, 136]], cls[1], 0, "VT1")
-    iota(T.KC[:, :], [[0, 32], [-1, 16]], 31, 0, "KC")
-    iota(T.NX[:, 0:W], [[0, W]], 2050, 0, "NE")
     for n in ("QT0", "QT1", "QT2"):
         fill(T[n][:, 128:136], 2048.0, n + "p")
     for n in ("QX0", "OWN"):
         fill(T[n][:, 128:136], 4096.0, n + "p")
     fill(T.SZ[:, 128:136], 0.0, "SZp")
+    fill(T.E2[:, 512:520], 4096.0, "E2p")
+    fill(T.ED[:, :], 0.0, "ED")
     fill(T.KB[:, :], 131072.0, "KB")
-    fill(T.K4[:, :], 4096.0, "K4")
-    fill(T.RST[:, :], 1.0, "RST")
-    fill(T.RST[:, 0:512:16], 0.0, "RST")
-    fill(T.R32[:, :], 1.0, "R32")
-    fill(T.R32[:, 0:64:32], 0.0, "R32")
-    fill(T.RSTB[:, :], 0.0, "RSTB")
-    fill(T.RSTB[:, 0:512:16], 8192.0, "RSTB")
+    resets = (("RST", 512, 1.0, 0.0), ("RSTB", 512, 0.0, 8192.0), ("RSM", 2048, 256.0, 0.0))
+    for n, w, c, c0 in resets:
+        fill(T[n][:, :], c, n)
+    for n, w, c, c0 in resets:
+        fill(T[n][:, 0:w:16], c0, n)
     ts(T.PA[:, :], T.PI[:, :], 15, A.bitwise_and, "PI", "PA")
+    cp(T.IDF[:, :], T.IDB[:, :], "IDB", "IDF")
     cp(T.PF[:, :], T.PA[:, :], "PA", "PF")
-    ts(T.COL[:, 0:1], T.PF[:, :], -1.0, A.mult, "PF", "+COL", 31.0, A.add)
+    ts(T.I4[:, :], T.IDB[:, :], 4096.0, A.mult, "IDB", "I4")
     for j, b in enumerate((2080 + 32 * rank, 2096 + 32 * rank, 2336, 2352)):
-        ts(T.COL[:, j + 1:j + 2], T.PF[:, :], float(b), A.add, "PF", "+COL")
-    CODE, TRV, TRE = T.COL[:, 0:1], [T.COL[:, 1:2], T.COL[:, 2:3]], [T.COL[:, 3:4], T.COL[:, 4:5]]
+        ts(T.COL[:, j:j + 1], T.PF[:, :], float(b), A.add, "PF", "+COL")
+    TRV, TRE = [T.COL[:, 0:1], T.COL[:, 1:2]], [T.COL[:, 2:3], T.COL[:, 3:4]]
     ts(T.CB[:, :], T.IO16[:, :], T.PF[:, 0:1], A.is_equal, "IO16 PF", "CB")
     ts(T.CM[:, :], T.IO16[:, :], T.PF[:, 0:1], A.not_equal, "IO16 PF", "CM")
+    ts(T.D2[:, :], T.IO32[:, :], T.PF[:, 0:1], A.is_equal, "IO32 PF", "D2")
+    ts(T.RL[:, :], T.IO66[:, :], T.PF[:, 0:1], A.is_gt, "IO66 PF", "RL")
     ts(T.CV[:, :], T.CB[:, :], 2050.0, A.mult, "CB", "CV")
     ts(T.CA[:, :], T.CB[:, :], -126976.0, A.mult, "CB", "CA", -4096.0, A.add)
-    cp(T.IDF[:, :], T.IDB[:, :], "IDB", "IDF")
-    ts(T.BO32[:, :], T.BO[:, :], 32.0, A.mult, "BO", "BO32")
-    ts(T.I4[:, :], T.IDB[:, :], 4096.0, A.mult, "IDB", "I4")
-    ts(T.D2[:, :], T.IO32[:, :], T.PF[:, 0:1], A.is_equal, "IO32 PF", "D2")
-    ts(T.MF[:, :], T.IO64[:, :], T.PF[:, 0:1], A.is_ge, "IO64 PF", "MF", 8192.0, A.mult)
-    ts(T.MB[:, :], T.MF[:, :], 4096.0, A.add, "MF", "MB")
-    cp(T.BOF[:, :], T.BO[:, :], "BO", "BOF")
+    ts(T.BOK[:, :], T.BO[:, :], 1024.0, A.mult, "BO", "BOK")
 
     def names_of(t, a, b):
         return T.NB[:, 16 + 16 * a + cls[t]:16 + 16 * b:16]
 
     def mine(m, a, n):
+        if m == 2:
+            return T.LD2[:, 32 * rank:32 * rank + 32]
         return T["LD%d" % m][:, rank, a:a + n]
 
     def key(m, r):
@@ -188,9 +195,9 @@ def rank_program(g, core, T, topo):
 
     def self_out(t):
         n, vt, qt = "QX%d" % t, VTs[t], "QT%d" % t
-        tt(T.TQ[:, :], T[qt][:, 0:128], T[vt][:, 0:128], A.is_equal, qt + " " + vt, "TQ")
-        ts(T.TQ[:, :], T.TQ[:, :], 4096.0, A.mult, "TQ", "TQ")
-        tt(T[n][:, 0:128], T.TQ[:, :], T[qt][:, 0:128], A.max, "TQ " + qt, n)
+        return [lambda: tt(T.TQ[:, :], T[qt][:, 0:128], T[vt][:, 0:128], A.is_equal, qt + " " + vt, "TQ"),
+                lambda: ts(T.TQ[:, :], T.TQ[:, :], 4096.0, A.mult, "TQ", "TQ"),
+                lambda: tt(T[n][:, 0:128], T.TQ[:, :], T[qt][:, 0:128], A.max, "TQ " + qt, n)]
 
     def repeat_names(t):
         qt = "QT%d" % t
@@ -219,17 +226,19 @@ def rank_program(g, core, T, topo):
             f()
 
     def select(t):
-        ts(T.HR[:, :], T.P2[:, 0:128], T.LIMA[:, 0:1], A.is_le, "P2 LIMA", "HR")
+        lim = "LIMA" if t else "LIMH"
+        ts(T.HR[:, :], T.P2[:, 0:128], T[lim][:, 0:1], A.is_le, "P2 " + lim, "HR")
         mm(T.P3[:, 0:128], T.HR[:, :], T.BO[:, :], True, True, "HR BO", "P3")
         ts(T.SZ[:, 0:128], T.P2[:, 0:128], 255.0, A.min, "P2", "SZ")
-        if t:
-            tt(T.OWN[:, 0:128], T.UA[:, :], T["QX%d" % t][:, 0:128], A.max, "UA QX%d" % t, "OWN")
+        gap(t, "hits")
         if t < 2:
             ts(T.HT[:, :], T.P3[:, 0:128], 9.0, A.is_ge, "P3", "HT")
         else:
             tt(T.HT[:, :], T.P3[:, 0:128], T.THR[:, :], A.is_ge, "P3 THR", "HT")
         for b in range(2):
             mm(T.P4[:, 128 * b:128 * b + 128], T.TRI[:, :], T.HT[:, :], True, True, "TRI HT", "P4")
+        if t:
+            tt(T.OWN[:, 0:128], T.UA[:, :], T["QX%d" % t][:, 0:128], A.max, "UA QX%d" % t, "OWN")
         gap(t, "rank")
         tt(T.CMP[:, :], T.P4[:, 0:256], T.SB[:, :], A.is_le, "P4 SB", "CMP")
         for b in range(2):
@@ -246,8 +255,9 @@ def rank_program(g, core, T, topo):
     def at_pivots(buf):
         return T[buf][:, 0:136].indirect(T.LW[:, :])
 
-    near = [c for c in T.cores if topo.chip(c) == topo.chip(core) and c != core]
-    far = [c for c in T.cores if topo.chip(c) != topo.chip(core)]
+    others = T.cores[rank + 1:] + T.cores[:rank]
+    near = [c for c in others if topo.chip(c) == topo.chip(core)]
+    far = [c for c in others if topo.chip(c) != topo.chip(core)]
     fe = topo.engines(core, far[0])
     ne = [e for e in topo.engines(core, near[0]) if e not in fe][:2]
 
@@ -266,46 +276,49 @@ def rank_program(g, core, T, topo):
             if r != rank:
                 wr["LD%d_%d" % (m, r)] = [("r", "a%d_%d" % (m, r), len(ne) if T.cores[r] in near else len(fe), {})]
 
-    def unpack(m, buf, a, n):
-        cp(T["%s%d" % (buf, m)][:, :], T["LD%d" % m][:, :, a:a + n], " ".join(key(m, r) for r in range(8)), "%s%d" % (buf, m))
+    def piece(m, a, n):
+        return T["LD%d" % m][:, :, a:a + n]
 
-    def pivots(tab, m, val, keys, o=None):
-        o = m if o is None else o
-        cp(TAB[tab].indirect(T["OF%d" % o][:, :]), T["%s%d" % (val, m)][:, :], "OF%d %s%d" % (o, val, m), keys)
+    def keys(m):
+        return " ".join(key(m, r) for r in range(8))
 
-    def new_j(m, n, r):
-        cp(TAB["JT"].indirect(T["OE%d" % m][:, n * r + n - 2:n * r + n]), T["LD%d" % m][:, r, VREP:VREP + 32], "OE%d %s" % (m, key(m, r)), "JT")
+    def all_places(m):
+        cp(T["OF%d" % m][:, :], piece(m, VOFF, 2), keys(m), "OF%d" % m)
+
+    def unpack(m, buf, a):
+        cp(T[buf][:, :], piece(m, a, 32), keys(m), buf)
+
+    def pivots(tab, m, buf, wk, rk=None):
+        cp(TAB[tab].indirect(T["OF%d" % m][:, :]), T[buf][:, :], "OF%d %s" % (m, rk or buf), wk)
+
+    def won(tab, m, r):
+        return TAB[tab].indirect(T["LD%d" % m][:, r, EOFF:EOFF + 2])
 
     def update(m):
-        unpack(m, "OF", VOFF, 2)
-        unpack(m, "SV", SIZES, 32)
-        pivots("XE", m, "SV", "XE")
-        unpack(m, "NV", NAMES, 32)
-        pivots("NE", m, "NV", "NE")
+        all_places(m)
+        ts(T.SVF[:, :], piece(m, SIZES, 32), 32.0, A.add, keys(m), "SVF")
+        silu(TAB["XE"].indirect(T["OF%d" % m][:, :]), T.SVF[:, :], "SVF OF%d" % m, "XE")
+        unpack(m, "NV%d" % m, NAMES)
+        pivots("NE", m, "NV%d" % m, "NE")
 
     def count():
-        ts(T.PR[:, :], T.P5[:, 0:4:2], 127.5, A.is_le, "P5", "PR")
-        for b in range(2):
-            mm(T.P2[:, 0:1], T.ONEB[:, :], T.PR[:, b:b + 1], b == 0, b == 1, "ONEB PR", "P2")
-        cp(T.AI[:, :], T.P2[:, 0:1], "P2", "AI")
-        ts(T.AM[:, :], T.AI[:, :], 7, A.bitwise_and, "AI", "AM")
-        tt(T.LIMA[:, :], T.AM[:, :], T.LIMI[:, :], A.add, "AM LIMI", "LIMA")
+        def total():
+            ts(T.PR[:, :], T.P5[:, 0:4:2], 127.5, A.is_le, "P5", "PR")
+            for b in range(2):
+                mm(T.P2[:, 0:1], T.ONEB[:, :], T.PR[:, b:b + 1], b == 0, b == 1, "ONEB PR", "P2")
+        return [total, lambda: cp(T.AI[:, :], T.P2[:, 0:1], "P2", "AI"),
+                lambda: ts(T.AM[:, :], T.AI[:, :], 7, A.bitwise_and, "AI", "AM"),
+                lambda: tt(T.LIMA[:, :], T.AM[:, :], T.LIMH[:, :], A.add, "AM LIMH", "LIMA")]
 
     def empty_covered(t):
         for h in range(2):
             ts(T.UN[:, 64 * h:64 * h + 64], T["P%d" % h][:, 0:64], 0.0, A.is_lt, "P%d" % h, "+UN", 2048.0, A.mult)
         tt(names_of(t, 0, 128), T.UN[:, :], names_of(t, 0, 128), A.max, "UN " + NBK, NBK)
 
-    def claim_keys():
-        mm(T.P6[:, :], T.BO32[:, :], T.X2[:, :], False, True, "BO32 X2", "P6")
-
-    def best_key():
-        scan(T.KS[:, :], T.RST[:, :], T.P6[:, :], 0.0, A.mult, A.max, "RST P6", "KS")
-
     def lanes_to_pivots(t):
         qt, oq = "QT%d" % t, "OQ%d" % t
         for h in range(2):
-            act(T.XG[:, 1024 * h:1024 * h + 1024], XEW.indirect(T[oq][:, 64 * h:64 * h + 64]), "XE " + oq, "XG%d" % h)
+            act(T.XG[:, 1024 * h:1024 * h + 1024], XEW.indirect(T[oq][:, 64 * h:64 * h + 64]), "XE " + oq, "XG%d" % h, func=IDN, bias=-32.0)
 
         def cover(a, b, k):
             tt(T.EQ[:, 16 * a:16 * b], NEW.indirect(T[oq][:, a:b]), T.QR[:, 16 * a:16 * b], A.is_equal, "NE QR " + oq, k)
@@ -315,6 +328,8 @@ def rank_program(g, core, T, topo):
             o = T["P%d" % h][:, 0:64]
             mm(o, T.IDF[:, :], T[qt][:, 64 * h:64 * h + 64], True, False, "IDF " + qt, "P%d" % h)
             mm(o, T.IDB[:, :], T.KB[:, 0:64], False, False, "IDB KB", "P%d" % h)
+        mm(T.P6[:, :], T.IDB[:, :], T.KCA[:, :], True, False, "IDB KCA", "P6")
+        mm(T.P6[:, :], T.IDB[:, :], T.KCB[:, :], False, False, "IDB KCB", "P6")
         for h in range(2):
             if h:
                 ts(T.UL[:, 0:64], T.P0[:, 0:64], 16.0, A.add, "P0", "UL_0", 2064.0, A.min)
@@ -333,61 +348,59 @@ def rank_program(g, core, T, topo):
         degrees(64, 128, "XV64 XV96", True)
         for h in range(2):
             act(T.UA[:, 64 * h:64 * h + 64], T["P%d" % h][:, 0:64], "P%d" % h, "+UA", func=ActivationFunctionType.Abs)
-        mm(T.P6[:, :], T.IDB[:, :], T.KC[:, :], True, False, "IDB KC", "P6")
+        gap(t, "select")
         select(t)
         ts(T.EP[:, :], at_pivots(qt), 16.0, A.add, "%s %sp LW" % (qt, qt), "EP")
-        act(T.Q2[:, :], NEW.indirect(T.EP[:, :]), "NE EP", "Q2")
-        act(T.X2[:, :], XEW.indirect(T.EP[:, :]), "XE EP", "X2")
+        for h in range(2):
+            act(T.Q2[:, 256 * h:256 * h + 256], NEW.indirect(T.EP[:, 16 * h:16 * h + 16]), "NE EP", "Q2_%d" % h)
+        act(T.X2[:, :], XEW.indirect(T.EP[:, :]), "XE EP", "X2", func=IDN, bias=-31.0)
+        gap(t, "roots")
+        act(T.E2[:, 0:512], T.JF[:, 0:2080].indirect(T.EP[:, :]), "JF EP", "E2", func=IDN, bias=-16.0)
         cp(T.L16[:, :], at_pivots("LT"), "LT LW", "L16")
         cp(mine(ahead[t], SIZES, 32), at_pivots("SZ"), "SZ SZp LW", "+M%d" % ahead[t])
         places(t)
+        ts(mine(ahead[t], VREP, 32), at_pivots(VTs[t]), 16.0, A.add, VTs[t] + " LW", "+M%d" % ahead[t])
         if t == 2:
             send(5)
-        ts(T.QM[:, :], at_pivots(qt), -4080.0, A.add, "%s %sp LW" % (qt, qt), "QM")
-        cp(T.OP[:, :], at_pivots("OWN"), "OWN OWNp LW", "OP")
-        m = 4 if t == 1 else 3
-        ts(mine(m, VREP, 32), at_pivots(VTs[t]), 16.0, A.add, VTs[t] + " LW", "+M%d" % m)
 
     def new_names(t):
-        vt = VTs[t]
-        if t == 1:
-            claim_keys()
-        tt(T.MM[:, :], T[vt][:, 0:136].indirect(T.L16[:, :]), T.Q2[:, :], A.is_equal, vt + " L16 Q2", "MM")
-        mm(T.P7[:, :], T.I4[:, :], T.MM[:, :], True, True, "I4 MM", "P7")
-        gap(t, "names")
-        tt(T.CC[:, :], T.Q2[:, :], T.P7[:, :], A.add, "Q2 P7", "CC")
-        scan(T.NS[:, :], T.RSTB[:, :], T.CC[:, :], 8192.0, A.add, A.min, "RSTB CC", "NS")
-        tt(T.NM[:, :], T.NS[:, 15:512:16], T.OP[:, :], A.min, "NS OP", "NM")
+        vt, half, pb = VTs[t], [slice(0, 256), slice(256, 512)], ["P7", "P3"]
+        for h in range(2):
+            tt(T.MM[:, half[h]], T[vt][:, 0:136].indirect(T.L16[:, 16 * h:16 * h + 16]), T.Q2[:, half[h]], A.is_equal, "%s L16 Q2_%d" % (vt, h), "MM%d" % h)
+            mm(T[pb[h]][:, 0:256], T.I4[:, :], T.MM[:, half[h]], True, True, "I4 MM%d" % h, pb[h])
+        mm(T.P6[:, :], T.BOK[:, :], T.X2[:, :], False, True, "BOK X2", "P6")
+        cp(T.OP[:, :], at_pivots("OWN"), "OWN OWNp LW", "OP")
+        for h in range(2):
+            tt(T.CC[:, half[h]], T.Q2[:, half[h]], T[pb[h]][:, 0:256], A.add, "Q2_%d %s" % (h, pb[h]), "CC%d" % h)
+        for h in range(2):
+            scan(T.NS[:, half[h]], T.RSTB[:, 0:256], T.CC[:, half[h]], 8192.0, A.add, A.min, "RSTB CC%d" % h, "NS%d" % h)
+        tt(T.NM[:, :], T.NS[:, 15:512:16], T.OP[:, :], A.min, "NS0 NS1 OP", "NM")
         ts(mine(t, NAMES, 32), T.NM[:, :], 2048.0, A.min, "NM", "+M%d" % t)
 
-    def win_row(t):
-        if t == 2:
-            claim_keys()
-            best_key()
-        cp(T.KI[:, :], T.KS[:, 15:512:16], "KS", "KI")
-        ts(T.K5[:, :], T.KI[:, :], 31, A.bitwise_and, "KI", "K5")
-        ts(T.OH[:, :], T.K5[:, :], CODE, A.is_equal, "K5 COL", "OH")
-        tt(T.PD[:, :], T.OH[:, :], T.QM[:, :], A.mult, "OH QM", "PD")
-        mm(T.P3[:, 0:32], T.IDB[:, :], T.K4[:, :], True, False, "IDB K4", "P3")
-        mm(T.P3[:, 0:32], T.BOF[:, :], T.PD[:, :], False, True, "BOF PD", "P3")
-        for b in range(2 if t == 1 else 0):
-            o = T.P4[:, 32 * b:32 * b + 32]
-            mm(o, T.IDB[:, :], T.MB[:, 32 * b:32 * b + 32], True, False, "IDB MB", "P4")
-            mm(o, T.BOF[:, :], T.PD[:, :], False, True, "BOF PD", "P4")
+    def as_list(rk, tm, tl):
+        return [lambda: tt(T[tm][:, :], T[rk][:, :], T.D2[:, :], A.mult, rk + " D2", tm),
+                lambda: scan(T[tl][:, :], T.RST[:, 0:32], T[tm][:, :], 0.0, A.mult, A.add, "RST " + tm, tl)]
 
-    def as_list(rk, rep, tm, tl):
-        tt(T[tm][:, :], rep, T.D2[:, :], A.mult, rk + " D2", tm)
-        scan(T[tl][:, :], T.RST[:, 0:32], T[tm][:, :], 0.0, A.mult, A.add, "RST " + tm, tl)
+    def claims(m):
+        col = [T.TL2[:, 15:16], T.TL2[:, 31:32]]
 
-    def claims(m, em, ek, tl):
-        col = [T[tl][:, 15:16], T[tl][:, 31:32]]
-        for b in range(2):
-            ts(T.ED[:, 32 * b:32 * b + 32], em[:, 32 * b:32 * b + 32], col[b], A.is_equal, ek + " " + tl, "+ED", 4096.0, A.mult)
-        scan(T.DX[:, :], T.R32[:, :], T.ED[:, :], 0.0, A.mult, A.max, "R32 ED", "DX")
-        for b in range(2):
-            ts(mine(m, EOFF + b, 1), T.DX[:, 32 * b + 31:32 * b + 32], col[b], A.max, "DX COL " + tl, "+M%d" % m, TRE[b], A.min)
-        if m == 4:
-            ts(mine(m, EOFF2, 2), mine(m, EOFF, 2), float(W), A.add, "M4", "+M4")
+        def same():
+            for b in range(2):
+                ts(T.ED[:, 33 * b:33 * b + 32], T.JE[:, :], col[b], A.is_equal, "JE TL2", "+ED", 4096.0, A.mult)
+
+        def out():
+            for b in range(2):
+                ts(mine(m, EOFF + b, 1), T.DX[:, 33 * b + 32:33 * b + 33], col[b], A.max, "DX COL TL2", "+M%d" % m, TRE[b], A.min)
+        return ([lambda: scan(T.KS[:, :], T.RST[:, :], T.P6[:, :], 0.0, A.mult, A.max, "RST P6", "KS"),
+                 lambda: cp(T.KI[:, :], T.KS[:, 15:512:16], "KS", "KI"),
+                 lambda: ts(T.K5[:, :], T.KI[:, :], 1023, A.bitwise_and, "KI", "K5")] + as_list("K5", "TM", "TL") +
+                [lambda: ts(T.UW[:, :], T.TL[:, 15:32:16], -1.0, A.mult, "TL", "UW", 512.0, A.add),
+                 lambda: cp(T.JE[:, :], T.E2[:, :].indirect(T.UW[:, :]), "E2 E2p UW", "JE")] + as_list("JE", "TM2", "TL2") +
+                [same, lambda: scan(T.DX[:, :], T.RL[:, :], T.ED[:, :], 0.0, A.mult, A.max, "RL ED", "DX"), out])
+
+    def select_row(ks):
+        for k in ks:
+            act(T.SAF[:, 128 * k:128 * k + 128], T.IDF[:, :], "IDF CB", "SAF%d" % k, scale=T.CB[:, k:k + 1])
 
     for j, (a, b) in enumerate(((0, 64), (64, 96), (96, 128))):
         c = (a + b) // 2
@@ -396,89 +409,82 @@ def rank_program(g, core, T, topo):
         gather_sizes("v", "OQ0_%d" % j, c, b)
         degrees(a, b, "XV%d XV%d" % (a, c), False)
         cp(T.QT0[:, a:b], names_of(0, a, b), "NB%d" % j, "+QT0")
-    act(T.NX[:, W:2 * W], T.NX[:, 0:W], "NE", "XE", func=IDN, bias=-1.0, scale=0.0)
-    for k in range(16):
-        act(T.SA[:, 128 * k:128 * k + 128], T.IDB[:, :], "IDB CA", "+SA", scale=T.CA[:, k:k + 1])
-    self_out(0)
-    cp(T.LIMA[:, :], T.LIMI[:, :], "LIMI", "LIMA")
+    act(T.XE[:, 0:2080], T.XS[:, 0:2080], "XS XSp", "XE", func=ActivationFunctionType.Silu, bias=30.0, scale=0.0)
+    ts(T.LIMH[:, :], T.LIMI[:, :], 0.5, A.add, "LIMI", "LIMH")
+    own0 = self_out(0)
+    own0[0]()
+    gaps[0, "hits"], gaps[0, "rank"] = own0[1:2], own0[2:3]
     select(0)
     ts(mine(0, NAMES, 32), at_pivots("QX0"), 2048.0, A.min, "QX0 QX0p LW", "+M0")
     cp(mine(0, SIZES, 32), at_pivots("SZ"), "SZ SZp LW", "+M0")
     places(0)
     send(0)
 
+    iota(T.NE[:, 0:2080], [[0, 2080]], 2050, 0, "NE")
+    iota(T.KCA[:, :], [[-16, 32], [0, 16]], 496, 0, "KCA")
+    iota(T.KCB[:, :], [[0, 32], [-1, 16]], 16, 0, "KCB")
+    iota(T.JF[:, 0:2080], [[1, 2080]], 16, 0, "JF")
     cp(T.QT1[:, 0:128], names_of(1, 0, 128), NBK, "QT1")
     for f in repeat_names(1):
         f()
+    select_row(range(8))
     ts(T.OQ1[:, :], T.QT1[:, 0:128], 16.0, A.add, "QT1", "OQ1")
-    count()
+    for k in range(16):
+        ts(T.SA[:, 128 * k:128 * k + 128], T.IDB[:, :], T.CA[:, k:k + 1], A.mult, "IDB CA", "+SA")
     ts(T.PV[:, :], T.P4[:, 0:128], 32.0, A.is_le, "P4", "PV")
     tt(T.PVB[:, :], T.PV[:, :], T.HT[:, :], A.mult, "PV HT", "PVB")
     mm(T.P7[:, 0:128], T.PVB[:, :], T.IDB[:, :], True, True, "PVB IDB", "P7")
     ts(T.THR[:, :], T.PVB[:, :], 100.0, A.mult, "PVB", "THR", 9.0, A.add)
-    self_out(1)
+    weave(count(), self_out(1))
     ts(T.DQ[:, :], T.P7[:, 0:128], 2048.0, A.mult, "P7", "DQ")
     tt(T.QT2[:, 0:128], T.DQ[:, :], T.QT0[:, 0:128], A.max, "DQ QT0", "QT2")
     ts(T.OQ2[:, :], T.QT2[:, 0:128], 16.0, A.add, "QT2", "OQ2")
-    self_out(2)
-    iota(T.RSM[:, :], [[0, 128], [256, 16]], 0, 0, "RSM")
-    iota(T.JT[:, 0:2064], [[1, 2064]], 0, 0, "JT")
-    iota(T.JT[:, 2064:2072], [[0, 8]], 4096, 0, "+JT")
+    weave(self_out(2))
 
     update(0)
     more = repeat_names(2)
-    gaps[1, "rank"], gaps[1, "lanes"], gaps[1, "names"] = more[:1], more[1:2], [best_key, more[2]]
+    gaps[1, "degrees"], gaps[1, "lanes"] = more[:1], more[1:2]
     lanes_to_pivots(1)
+    more[2]()
     new_names(1)
     send(1)
-    win_row(1)
-    as_list("P3", T.P3[:, 0:32], "TM", "TL")
-    claims(4, T.P4, "P4", "TL")
+    weave(claims(4), count())
     send(4)
-    for k in range(16):
-        act(T.SAF[:, 128 * k:128 * k + 128], T.IDF[:, :], "IDF CB", "+SAF", scale=T.CB[:, k:k + 1])
-    count()
-    pivots("NB", 0, "NV", NBK)
+    iota(T.JT[:, 0:2064], [[1, 2064]], 0, 0, "JT")
+    select_row(range(8, 16))
+    unpack(0, "SV", SIZES)
+    pivots("NB", 0, "NV0", NBK)
     pivots("XS", 0, "SV", "XS")
 
     update(1)
-    unpack(4, "OE", EOFF2, 4)
+    ts(T.VF[:, :], piece(1, VREP, 32), 16.0, A.add, keys(1), "VF")
+    unpack(1, "SV", SIZES)
     for r in range(7, -1, -1):
-        cp(T.NX[:, 0:2 * W].indirect(T.OE4[:, 4 * r:4 * r + 4]), T.LD1[:, r, SIZES:SIZES + 64], "OE4 " + key(1, r), "NE XE")
-    todo = [lambda r=r: new_j(4, 4, r) for r in range(7, -1, -1)]
-    gaps[2, "degrees"], gaps[2, "rank"], gaps[2, "lanes"], gaps[2, "names"] = todo[:1], todo[1:2], todo[2:3], todo[3:6]
+        cp(won("NE", 4, r), T.LD1[:, r, NAMES:NAMES + 32], "%s %s" % (key(4, r), key(1, r)), "NE")
+        silu(won("XE", 4, r), T.SVF[:, 32 * r:32 * r + 32], "SVF " + key(4, r), "XE")
+    todo = [lambda r=r: silu(won("JF", 4, r), T.VF[:, 32 * r:32 * r + 32], "VF " + key(4, r), "JF") for r in range(7, -1, -1)]
+    gaps[2, "select"], gaps[2, "roots"] = todo[:5], todo[5:]
     lanes_to_pivots(2)
     new_names(2)
     send(2)
-    win_row(2)
-    for f in todo[6:]:
-        f()
     for k in range(16):
-        mm(T.P5[:, 0:128], T.SAF[:, 128 * k:128 * k + 128], T.JT[:, 16 + k:2064:16], k == 0, k == 15, "SAF JT", "P5")
-    as_list("P3", T.P3[:, 0:32], "TM", "TL")
-    ts(T.UW[:, :], T.TL[:, 15:32:16], 2064.0, A.min, "TL", "UW")
-    cp(T.JE[:, :], T.JT[:, 0:2072].indirect(T.UW[:, :]), "JT UW", "JE")
-    as_list("JE", T.JE[:, :], "TM2", "TL2")
-    for b in range(2):
-        tt(T.EM[:, 32 * b:32 * b + 32], T.JE[:, :], T.MF[:, 32 * b:32 * b + 32], A.add, "JE MF", "+EM")
-    claims(3, T.EM, "EM", "TL2")
+        mm(T.P5[:, 0:128], T.SAF[:, 128 * k:128 * k + 128], T.JF[:, 16 + k:2064:16], k == 0, k == 15, "SAF%d JF" % k, "P5")
+    weave(claims(3))
     send(3)
 
     pivots("XS", 1, "SV", "XS")
-    unpack(5, "OF", VOFF, 2)
-    unpack(5, "SV", SIZES, 32)
+    all_places(5)
+    unpack(5, "SV", SIZES)
     pivots("XS", 5, "SV", "XS")
     dma("s", T.yx[:, :], T.XS[:, 16:2064], "o_x", "XS", "")
-    pivots("NB", 1, "NV", NBK)
-    unpack(2, "NV", NAMES, 32)
-    pivots("NB", 2, "NV", NBK, 5)
+    pivots("NB", 1, "NV1", NBK)
+    pivots("NB", 5, "LD2", NBK, keys(2))
     dma("s", T.yn[:, :], T.NB[:, 16:2064], "o_n", NBK, "")
-    cp(T.JL[:, :], T.P5[:, 0:128], "P5", "JL")
-    unpack(3, "OE", EOFF, 2)
+    ts(T.JL[:, :], T.P5[:, 0:128], -15.75, A.add, "P5", "JL")
     for r in range(7, -1, -1):
-        new_j(3, 2, r)
-    act(T.YJ[:, 0:1024], T.JT[:, 0:2072].indirect(T.JL[:, 0:64]), "JT JL", "YJ0", func=IDN, bias=-16.0)
-    ts(T.YJ[:, 1024:2048], T.JT[:, 0:2072].indirect(T.JL[:, 64:128]), -16.0, A.add, "JT JL", "YJ1")
+        cp(won("JT", 3, r), T.LD5[:, r, VREP:VREP + 32], "%s %s" % (key(3, r), key(5, r)), "JT")
+    act(T.YJ[:, 0:1024], T.JT[:, 0:2064].indirect(T.JL[:, 0:64]), "JT JL", "YJ0", func=IDN, bias=-16.0)
+    ts(T.YJ[:, 1024:2048], T.JT[:, 0:2064].indirect(T.JL[:, 64:128]), -16.0, A.add, "JT JL", "YJ1")
     dma("a", T.yj[:, 0:1024], T.YJ[0:128:16, 0:1024], "o_j0", "YJ0", "")
     dma("s", T.yj[:, 1024:2048], T.YJ[0:128:16, 1024:2048], "o_j1", "YJ1", "")
 

@@ -5,24 +5,24 @@ W = 2368
 F, B, I, U = "float32", "bfloat16", "int32", "uint16"
 SCRATCH = {}
 for _names, _w, _d in (
-        ("NB JT NE XE JF", W, F), ("XS", W, B), ("SA EQ XG XV MX RSM", 2048, B), ("SAF QR YJ", 2048, F),
-        ("Q2 KS CC NS", 512, F), ("E2", 520, F), ("KCA KCB X2 MM RST RSTB", 512, B), ("ONEB IDB I4 BO BOK TRI HR HT PV PVB", 128, B), ("CMP", 256, B),
-        ("IDF TQ UA UN THR DQ", 128, F), ("SB SVF VF", 256, F), ("WTS PR", 2, B), ("KB", 64, B),
-        ("PI PA LIMI AI AM", 1, I), ("PF LIMA LIMH", 1, F), ("COL", 8, F), ("CA CB CM CV IO16", 16, F),
-        ("LT VT0 VT1 QT0 QT1 QT2 QX0 QX1 QX2 QC OWN SZ", 136, F), ("OQ0 OQ1 OQ2 UL JL", 128, U),
-        ("IO32 D2 OP NM TM TM2 TL TL2", 32, F), ("IO66 RL ED DX", 66, F), ("LW UW", 2, U), ("EP L16", 32, U), ("KI K5 JE", 32, I),
+        ("NB JT NE XE JF", W, F), ("XS", W, B), ("SA SK EQ XG XV MX RSM", 2048, B), ("SAF QR YJ", 2048, F),
+        ("Q2 CC NS", 512, F), ("E2", 520, F), ("X2 MM", 512, B), ("RSTB", 256, B), ("ONEB IDB I4 BO TRI HR HT PV PVB KB1 KB2", 128, B), ("CMP", 256, B),
+        ("IDF TQ UA UN THR", 128, F), ("SB SVF VF VJ", 256, F), ("WTS PR", 2, B),
+        ("PI PA LIMI AI AM", 1, I), ("PF P32 LIMA LIMH", 1, F), ("COL BOK", 8, F), ("CA CB CM CV IO16", 16, F),
+        ("LT VT0 VT1 QT0 QT1 QX0 QX1 OWN SZ", 136, F), ("OQ0 OQ1 UL JL", 128, U),
+        ("IO32 D2 OP NM TM TL KC KS RST RSK", 32, F), ("IO66 RL ED DX", 66, F), ("LW UW", 2, U), ("EP EK L16", 32, U), ("KI K5", 2, I), ("JE", 32, I),
         ("OF0 OF1 OF5", 16, U), ("NV0 NV1 SV", 256, U)):
     for _n in _names.split():
         SCRATCH[_n] = ("sbuf", [128, _w], _d)
 for _b in range(6):
-    SCRATCH["LD%d" % _b] = ("sbuf", [128, 8, 104], U)
+    SCRATCH["LD%d" % _b] = ("sbuf", [128, 8, 72], U)
 SCRATCH["LD2"] = ("sbuf", [128, 256], U)
 for _b in range(8):
     SCRATCH["P%d" % _b] = ("psum", [128, 512], F)
 SEMAPHORES = ["ev", "et", "ea", "eg", "d_x", "d_n0", "d_n1", "d_n2", "d_l", "o_n", "o_x", "o_j0", "o_j1"]
 SEMAPHORES += ["a%d_%d" % (m, r) for m in range(6) for r in range(8)] + ["l%d" % m for m in range(6)]
-VREP, VOFF, SIZES, NAMES, EOFF = 0, 32, 34, 66, 98
-SPAN = [(32, 98), (0, 98), (66, 98), (98, 100), (98, 100), (0, 66)]
+VOFF, SIZES, NAMES, EOFF = 0, 2, 34, 66
+SPAN = [(0, 66), (0, 66), (34, 66), (66, 68), (66, 68), (0, 34)]
 
 
 def rank_program(g, core, T, topo):
@@ -137,6 +137,9 @@ def rank_program(g, core, T, topo):
     dma("s", T.NB[:, 1552:2064], T.nb[:, 1536:2048], "d_n2", "", "NB2")
 
     fill(T.ONEB[:, :], 1.0, "ONEB")
+    fill(T.SK[:, :], 0.0, "SK")
+    for a, b, src in ((0, 128, "ONEB"), (128, 2080, "SK")):
+        act(T.XE[:, a:b], T[src][:, 0:b - a], src, "+XE", func=ActivationFunctionType.Silu, bias=30.0, scale=0.0)
     fill(T.WTS[:, 0:1], 1.0, "+WTS")
     fill(T.WTS[:, 1:2], 16.0, "+WTS")
     fill(T.XS[:, 0:16], 0.0, "+XSp")
@@ -154,15 +157,16 @@ def rank_program(g, core, T, topo):
     iota(T.SB[:, :], [[-16, 2], [0, 8], [-1, 16]], 31, 0, "SB")
     iota(T.LT[:, :], [[1, 136]], 0, 0, "LT")
     iota(T.VT1[:, :], [[16, 136]], cls[1], 0, "VT1")
-    for n in ("QT0", "QT1", "QT2"):
+    iota(T.NE[:, 0:1040], [[0, 1040]], 2050, 0, "NEa")
+    for n in ("QT0", "QT1"):
         fill(T[n][:, 128:136], 2048.0, n + "p")
     for n in ("QX0", "OWN"):
         fill(T[n][:, 128:136], 4096.0, n + "p")
     fill(T.SZ[:, 128:136], 0.0, "SZp")
     fill(T.E2[:, 512:520], 4096.0, "E2p")
     fill(T.ED[:, :], 0.0, "ED")
-    fill(T.KB[:, :], 131072.0, "KB")
-    resets = (("RST", 512, 1.0, 0.0), ("RSTB", 512, 0.0, 8192.0), ("RSM", 2048, 256.0, 0.0))
+    fill(T.KB1[:, :], 131072.0, "KB1")
+    resets = (("RST", 32, 1.0, 0.0), ("RSK", 32, -8388608.0, 512.0), ("RSTB", 256, 0.0, 8192.0))
     for n, w, c, c0 in resets:
         fill(T[n][:, :], c, n)
     for n, w, c, c0 in resets:
@@ -180,15 +184,43 @@ def rank_program(g, core, T, topo):
     ts(T.RL[:, :], T.IO66[:, :], T.PF[:, 0:1], A.is_gt, "IO66 PF", "RL")
     ts(T.CV[:, :], T.CB[:, :], 2050.0, A.mult, "CB", "CV")
     ts(T.CA[:, :], T.CB[:, :], -126976.0, A.mult, "CB", "CA", -4096.0, A.add)
-    ts(T.BOK[:, :], T.BO[:, :], 1024.0, A.mult, "BO", "BOK")
+    ts(T.BOK[:, :], T.BO[:, 0:128:16], -1024.0, A.mult, "BO", "BOK")
+    ts(T.P32[:, :], T.PF[:, :], 32.0, A.mult, "PF", "PX")
+
+    def count_rows(ks):
+        for k in ks:
+            ts(T.SA[:, 128 * k:128 * k + 128], T.IDB[:, :], T.CA[:, k:k + 1], A.mult, "IDB CA", "+SA")
+    count_rows(range(8))
 
     def names_of(t, a, b):
         return T.NB[:, 16 + 16 * a + cls[t]:16 + 16 * b:16]
 
-    def mine(m, a, n):
+    chips = []
+    for r, c in enumerate(T.cores):
+        if chips and topo.chip(T.cores[chips[-1][0]]) == topo.chip(c):
+            chips[-1].append(r)
+        else:
+            chips.append([r])
+
+    def far(r):
+        i = [r in c for c in chips].index(True)
+        j = chips[i].index(r)
+        return [x for c in chips[i + 1:] + chips[:i] for x in c[j:] + c[:j]]
+
+    def slot(d, r):
+        return 0 if r == d else 2 + far(r).index(d) if d in far(r) else 1
+
+    near = [r for r in range(8) if r != rank and r not in far(rank)]
+    fe = topo.engines(core, T.cores[far(rank)[0]])
+    ne = [e for e in topo.engines(core, T.cores[near[0]]) if e not in fe][:2]
+
+    def msg(m, j, a, n):
         if m == 2:
-            return T.LD2[:, 32 * rank:32 * rank + 32]
-        return T["LD%d" % m][:, rank, a:a + n]
+            return T.LD2[:, 32 * j:32 * j + 32]
+        return T["LD%d" % m][:, j, a:a + n]
+
+    def mine(m, a, n):
+        return msg(m, 0, a, n)
 
     def key(m, r):
         return "M%d" % m if r == rank else "LD%d_%d" % (m, r)
@@ -199,14 +231,9 @@ def rank_program(g, core, T, topo):
                 lambda: ts(T.TQ[:, :], T.TQ[:, :], 4096.0, A.mult, "TQ", "TQ"),
                 lambda: tt(T[n][:, 0:128], T.TQ[:, :], T[qt][:, 0:128], A.max, "TQ " + qt, n)]
 
-    def repeat_names(t):
-        qt = "QT%d" % t
-
-        def copies():
-            for k in range(16):
-                act(T.QR[:, k:2048:16], T.QC[:, 0:128], "QC CM CV", "+QR", func=IDN, bias=T.CV[:, k:k + 1], scale=T.CM[:, k:k + 1])
-        return [lambda: ts(T.TQ[:, :], T[qt][:, 0:128], 2048.0, A.is_equal, qt, "TQ", 2048.0, A.mult),
-                lambda: tt(T.QC[:, 0:128], T.TQ[:, :], T[qt][:, 0:128], A.add, "TQ " + qt, "QC"), copies]
+    def repeat_names(names, rk):
+        for k in range(16):
+            act(T.QR[:, k:2048:16], names, rk + " CM CV", "+QR", func=IDN, bias=T.CV[:, k:k + 1], scale=T.CM[:, k:k + 1])
 
     def gather_sizes(q, lst, a, b):
         f = cp if q == "v" else act
@@ -238,7 +265,7 @@ def rank_program(g, core, T, topo):
         for b in range(2):
             mm(T.P4[:, 128 * b:128 * b + 128], T.TRI[:, :], T.HT[:, :], True, True, "TRI HT", "P4")
         if t:
-            tt(T.OWN[:, 0:128], T.UA[:, :], T["QX%d" % t][:, 0:128], A.max, "UA QX%d" % t, "OWN")
+            tt(T.OWN[:, 0:128], T.UA[:, :], T["QX%d" % (t % 2)][:, 0:128], A.max, "UA QX%d" % (t % 2), "OWN")
         gap(t, "rank")
         tt(T.CMP[:, :], T.P4[:, 0:256], T.SB[:, :], A.is_le, "P4 SB", "CMP")
         for b in range(2):
@@ -255,51 +282,53 @@ def rank_program(g, core, T, topo):
     def at_pivots(buf):
         return T[buf][:, 0:136].indirect(T.LW[:, :])
 
-    others = T.cores[rank + 1:] + T.cores[:rank]
-    near = [c for c in others if topo.chip(c) == topo.chip(core)]
-    far = [c for c in others if topo.chip(c) != topo.chip(core)]
-    fe = topo.engines(core, far[0])
-    ne = [e for e in topo.engines(core, near[0]) if e not in fe][:2]
-
     def send(m):
         a, b = SPAN[m]
         tr = []
-        for cs, es in ((far, fe), (near, ne)):
-            ids = [DstId(rid=topo.addr(c)[0], pnc=topo.addr(c)[1]) for c in cs]
+        for rs, es in ((far(rank), fe), (near, ne)):
+            ids = [DstId(rid=topo.addr(T.cores[r])[0], pnc=topo.addr(T.cores[r])[1]) for r in rs]
             tr.append(RemoteDMATransfer(dst_ids=ids, dma_engine_mask=sum(1 << e for e in es), remote_sem=T.sem["a%d_%d" % (m, rank)],
-                                        srcs=[mine(m, a, b - a)], dsts=[mine(m, a, b - a)] * len(cs)))
+                                        srcs=[mine(m, a, b - a)], dsts=[msg(m, slot(r, rank), a, b - a) for r in rs]))
         pre("g", ["M%d" % m], [])
         g.remote_dma_fused(tr, local_sem=T.sem["l%d" % m])
         nloc[m] = len(fe) + len(ne)
         post("l%d" % m, "g", "l%d" % m, nloc[m], ["M%d" % m], [])
         for r in range(8):
             if r != rank:
-                wr["LD%d_%d" % (m, r)] = [("r", "a%d_%d" % (m, r), len(ne) if T.cores[r] in near else len(fe), {})]
+                wr["LD%d_%d" % (m, r)] = [("r", "a%d_%d" % (m, r), len(ne) if r in near else len(fe), {})]
 
-    def piece(m, a, n):
-        return T["LD%d" % m][:, :, a:a + n]
+    ALL, EARLY, LATE = (0, 8), (0, 6), (6, 8)
 
-    def keys(m):
-        return " ".join(key(m, r) for r in range(8))
+    def keys(m, part):
+        return " ".join(key(m, r) for r in range(8) if part[0] <= slot(rank, r) < part[1])
 
-    def all_places(m):
-        cp(T["OF%d" % m][:, :], piece(m, VOFF, 2), keys(m), "OF%d" % m)
+    def parts(buf, part):
+        return " ".join("%s_%d" % (buf, p[0]) for p in (EARLY, LATE) if part[0] <= p[0] < part[1])
 
-    def unpack(m, buf, a):
-        cp(T[buf][:, :], piece(m, a, 32), keys(m), buf)
+    def unpack(m, buf, a, n, part, add=None):
+        out, in_ = T[buf][:, n * part[0]:n * part[1]], T["LD%d" % m][:, part[0]:part[1], a:a + n]
+        if add is None:
+            cp(out, in_, keys(m, part), parts(buf, part))
+        else:
+            ts(out, in_, add, A.add, keys(m, part), parts(buf, part))
 
-    def pivots(tab, m, buf, wk, rk=None):
-        cp(TAB[tab].indirect(T["OF%d" % m][:, :]), T[buf][:, :], "OF%d %s" % (m, rk or buf), wk)
+    def at_places(tab, m, part):
+        return TAB[tab].indirect(T["OF%d" % m][:, 2 * part[0]:2 * part[1]])
 
-    def won(tab, m, r):
-        return TAB[tab].indirect(T["LD%d" % m][:, r, EOFF:EOFF + 2])
+    def pivots(f, tab, m, buf, wk, part=ALL, rk=None):
+        f(at_places(tab, m, part), T[buf][:, 32 * part[0]:32 * part[1]], parts("OF%d" % m, part) + " " + (rk or parts(buf, part)), wk)
+
+    def won(f, tab, m, r, buf):
+        j = slot(rank, r)
+        f(TAB[tab].indirect(msg(m, j, EOFF, 2)), T[buf][:, 32 * j:32 * j + 32], parts(buf, ALL) + " " + key(m, r), tab)
 
     def update(m):
-        all_places(m)
-        ts(T.SVF[:, :], piece(m, SIZES, 32), 32.0, A.add, keys(m), "SVF")
-        silu(TAB["XE"].indirect(T["OF%d" % m][:, :]), T.SVF[:, :], "SVF OF%d" % m, "XE")
-        unpack(m, "NV%d" % m, NAMES)
-        pivots("NE", m, "NV%d" % m, "NE")
+        for part in (EARLY, LATE):
+            unpack(m, "OF%d" % m, VOFF, 2, part)
+            unpack(m, "SVF", SIZES, 32, part, 32.0)
+            unpack(m, "NV%d" % m, NAMES, 32, part)
+            pivots(silu, "XE", m, "SVF", "XE", part)
+            pivots(cp, "NE", m, "NV%d" % m, "NE", part)
 
     def count():
         def total():
@@ -316,20 +345,20 @@ def rank_program(g, core, T, topo):
         tt(names_of(t, 0, 128), T.UN[:, :], names_of(t, 0, 128), A.max, "UN " + NBK, NBK)
 
     def lanes_to_pivots(t):
-        qt, oq = "QT%d" % t, "OQ%d" % t
+        qt, oq, kb = "QT%d" % (t % 2), "OQ%d" % (t % 2), "KB%d" % t
+        ok = "OQ1" if t == 1 else "OQ0_0 OQ0_1 OQ0_2"
         for h in range(2):
-            act(T.XG[:, 1024 * h:1024 * h + 1024], XEW.indirect(T[oq][:, 64 * h:64 * h + 64]), "XE " + oq, "XG%d" % h, func=IDN, bias=-32.0)
+            act(T.XG[:, 1024 * h:1024 * h + 1024], XEW.indirect(T[oq][:, 64 * h:64 * h + 64]), "XE " + ok, "XG%d" % h, func=IDN, bias=-32.0)
 
         def cover(a, b, k):
-            tt(T.EQ[:, 16 * a:16 * b], NEW.indirect(T[oq][:, a:b]), T.QR[:, 16 * a:16 * b], A.is_equal, "NE QR " + oq, k)
+            tt(T.EQ[:, 16 * a:16 * b], NEW.indirect(T[oq][:, a:b]), T.QR[:, 16 * a:16 * b], A.is_equal, "NE QR " + ok, k)
         cover(0, 64, "EQ0")
         cover(64, 96, "EQ1")
         for h in range(2):
             o = T["P%d" % h][:, 0:64]
             mm(o, T.IDF[:, :], T[qt][:, 64 * h:64 * h + 64], True, False, "IDF " + qt, "P%d" % h)
-            mm(o, T.IDB[:, :], T.KB[:, 0:64], False, False, "IDB KB", "P%d" % h)
-        mm(T.P6[:, :], T.IDB[:, :], T.KCA[:, :], True, False, "IDB KCA", "P6")
-        mm(T.P6[:, :], T.IDB[:, :], T.KCB[:, :], False, False, "IDB KCB", "P6")
+            mm(o, T.IDB[:, :], T[kb][:, 64 * h:64 * h + 64], False, False, "IDB " + kb, "P%d" % h)
+        mm(T.P6[:, 0:32], T.IDF[:, :], T.KC[:, :], True, False, "IDF KC", "P6")
         for h in range(2):
             if h:
                 ts(T.UL[:, 0:64], T.P0[:, 0:64], 16.0, A.add, "P0", "UL_0", 2064.0, A.min)
@@ -340,12 +369,11 @@ def rank_program(g, core, T, topo):
         gather_sizes("a", "UL_0", 0, 64)
         scan(T.MX[:, :], T.RSM[:, :], T.XG[:, :], 0.0, A.min, A.max, "RSM XG0 XG1", "MX")
         ts(T.UL[:, 64:128], T.P1[:, 0:64], 16.0, A.add, "P1", "UL_1", 2064.0, A.min)
-        gather_sizes("a", "UL_1", 64, 96)
-        gather_sizes("v", "UL_1", 96, 128)
+        gather_sizes("a", "UL_1", 64, 88)
+        gather_sizes("v", "UL_1", 88, 128)
         empty_covered(t)
-        gap(t, "degrees")
         degrees(0, 64, "XV0", True)
-        degrees(64, 128, "XV64 XV96", True)
+        degrees(64, 128, "XV64 XV88", True)
         for h in range(2):
             act(T.UA[:, 64 * h:64 * h + 64], T["P%d" % h][:, 0:64], "P%d" % h, "+UA", func=ActivationFunctionType.Abs)
         gap(t, "select")
@@ -353,22 +381,24 @@ def rank_program(g, core, T, topo):
         ts(T.EP[:, :], at_pivots(qt), 16.0, A.add, "%s %sp LW" % (qt, qt), "EP")
         for h in range(2):
             act(T.Q2[:, 256 * h:256 * h + 256], NEW.indirect(T.EP[:, 16 * h:16 * h + 16]), "NE EP", "Q2_%d" % h)
-        act(T.X2[:, :], XEW.indirect(T.EP[:, :]), "XE EP", "X2", func=IDN, bias=-31.0)
-        gap(t, "roots")
-        act(T.E2[:, 0:512], T.JF[:, 0:2080].indirect(T.EP[:, :]), "JF EP", "E2", func=IDN, bias=-16.0)
         cp(T.L16[:, :], at_pivots("LT"), "LT LW", "L16")
         cp(mine(ahead[t], SIZES, 32), at_pivots("SZ"), "SZ SZp LW", "+M%d" % ahead[t])
         places(t)
-        ts(mine(ahead[t], VREP, 32), at_pivots(VTs[t]), 16.0, A.add, VTs[t] + " LW", "+M%d" % ahead[t])
         if t == 2:
             send(5)
+        for b in range(2):
+            cp(T.EK[:, b:32:2], T.EP[:, 16 * b:16 * b + 16], "EP", "+EK")
+        act(T.X2[:, :], XEW.indirect(T.EK[:, :]), "XE EK", "X2", func=IDN, bias=-31.0)
+        gap(t, "roots")
+        act(T.E2[:, 0:512], T.JF[:, 0:2080].indirect(T.EK[:, :]), "JF EK", "E2", func=IDN, bias=-16.0)
 
     def new_names(t):
         vt, half, pb = VTs[t], [slice(0, 256), slice(256, 512)], ["P7", "P3"]
         for h in range(2):
             tt(T.MM[:, half[h]], T[vt][:, 0:136].indirect(T.L16[:, 16 * h:16 * h + 16]), T.Q2[:, half[h]], A.is_equal, "%s L16 Q2_%d" % (vt, h), "MM%d" % h)
             mm(T[pb[h]][:, 0:256], T.I4[:, :], T.MM[:, half[h]], True, True, "I4 MM%d" % h, pb[h])
-        mm(T.P6[:, :], T.BOK[:, :], T.X2[:, :], False, True, "BOK X2", "P6")
+        for p in range(16):
+            mm(T.P6[:, 0:32], T.SK[:, 128 * p:128 * p + 128], T.X2[:, 32 * p:32 * p + 32], False, p == 15, "SK X2", "P6")
         cp(T.OP[:, :], at_pivots("OWN"), "OWN OWNp LW", "OP")
         for h in range(2):
             tt(T.CC[:, half[h]], T.Q2[:, half[h]], T[pb[h]][:, 0:256], A.add, "Q2_%d %s" % (h, pb[h]), "CC%d" % h)
@@ -377,26 +407,24 @@ def rank_program(g, core, T, topo):
         tt(T.NM[:, :], T.NS[:, 15:512:16], T.OP[:, :], A.min, "NS0 NS1 OP", "NM")
         ts(mine(t, NAMES, 32), T.NM[:, :], 2048.0, A.min, "NM", "+M%d" % t)
 
-    def as_list(rk, tm, tl):
-        return [lambda: tt(T[tm][:, :], T[rk][:, :], T.D2[:, :], A.mult, rk + " D2", tm),
-                lambda: scan(T[tl][:, :], T.RST[:, 0:32], T[tm][:, :], 0.0, A.mult, A.add, "RST " + tm, tl)]
-
     def claims(m):
-        col = [T.TL2[:, 15:16], T.TL2[:, 31:32]]
+        col = [T.TL[:, 15:16], T.TL[:, 31:32]]
 
         def same():
             for b in range(2):
-                ts(T.ED[:, 33 * b:33 * b + 32], T.JE[:, :], col[b], A.is_equal, "JE TL2", "+ED", 4096.0, A.mult)
+                ts(T.ED[:, 33 * b:33 * b + 32], T.JE[:, :], col[b], A.is_equal, "JE TL", "+ED", 4096.0, A.mult)
 
         def out():
             for b in range(2):
-                ts(mine(m, EOFF + b, 1), T.DX[:, 33 * b + 32:33 * b + 33], col[b], A.max, "DX COL TL2", "+M%d" % m, TRE[b], A.min)
-        return ([lambda: scan(T.KS[:, :], T.RST[:, :], T.P6[:, :], 0.0, A.mult, A.max, "RST P6", "KS"),
-                 lambda: cp(T.KI[:, :], T.KS[:, 15:512:16], "KS", "KI"),
-                 lambda: ts(T.K5[:, :], T.KI[:, :], 1023, A.bitwise_and, "KI", "K5")] + as_list("K5", "TM", "TL") +
-                [lambda: ts(T.UW[:, :], T.TL[:, 15:32:16], -1.0, A.mult, "TL", "UW", 512.0, A.add),
-                 lambda: cp(T.JE[:, :], T.E2[:, :].indirect(T.UW[:, :]), "E2 E2p UW", "JE")] + as_list("JE", "TM2", "TL2") +
-                [same, lambda: scan(T.DX[:, :], T.RL[:, :], T.ED[:, :], 0.0, A.mult, A.max, "RL ED", "DX"), out])
+                ts(mine(m, EOFF + b, 1), T.DX[:, 33 * b + 32:33 * b + 33], col[b], A.max, "DX COL TL", "+M%d" % m, TRE[b], A.min)
+        return [lambda: scan(T.KS[:, :], T.RSK[:, :], T.P6[:, 0:32], 0.0, A.max, A.min, "RSK P6", "KS"),
+                lambda: cp(T.KI[:, :], T.KS[:, 15:32:16], "KS", "KI"),
+                lambda: ts(T.K5[:, :], T.KI[:, :], 1023, A.bitwise_and, "KI", "K5"),
+                lambda: cp(T.UW[:, :], T.K5[:, :], "K5", "UW"),
+                lambda: cp(T.JE[:, :], T.E2[:, :].indirect(T.UW[:, :]), "E2 E2p UW", "JE"),
+                lambda: tt(T.TM[:, :], T.JE[:, :], T.D2[:, :], A.mult, "JE D2", "TM"),
+                lambda: scan(T.TL[:, :], T.RST[:, :], T.TM[:, :], 0.0, A.mult, A.add, "RST TM", "TL"),
+                same, lambda: scan(T.DX[:, :], T.RL[:, :], T.ED[:, :], 0.0, A.mult, A.max, "RL ED", "DX"), out]
 
     def select_row(ks):
         for k in ks:
@@ -409,62 +437,57 @@ def rank_program(g, core, T, topo):
         gather_sizes("v", "OQ0_%d" % j, c, b)
         degrees(a, b, "XV%d XV%d" % (a, c), False)
         cp(T.QT0[:, a:b], names_of(0, a, b), "NB%d" % j, "+QT0")
-    act(T.XE[:, 0:2080], T.XS[:, 0:2080], "XS XSp", "XE", func=ActivationFunctionType.Silu, bias=30.0, scale=0.0)
-    ts(T.LIMH[:, :], T.LIMI[:, :], 0.5, A.add, "LIMI", "LIMH")
+        if j == 1:
+            ts(T.LIMH[:, :], T.LIMI[:, :], 0.5, A.add, "LIMI", "LIMH")
+    act(T.NE[:, 1040:2080], T.XS[:, 0:1040], "XS XSp", "NEb", func=IDN, bias=2050.0, scale=0.0)
+    repeat_names(names_of(1, 0, 128), NBK)
+    select_row(range(8))
     own0 = self_out(0)
-    own0[0]()
-    gaps[0, "hits"], gaps[0, "rank"] = own0[1:2], own0[2:3]
+    weave(own0[:2])
+    gaps[0, "rank"] = own0[2:]
+    gaps[0, "lanes"] = [lambda: cp(T.QT1[:, 0:128], names_of(1, 0, 128), NBK, "QT1")]
     select(0)
     ts(mine(0, NAMES, 32), at_pivots("QX0"), 2048.0, A.min, "QX0 QX0p LW", "+M0")
     cp(mine(0, SIZES, 32), at_pivots("SZ"), "SZ SZp LW", "+M0")
     places(0)
     send(0)
 
-    iota(T.NE[:, 0:2080], [[0, 2080]], 2050, 0, "NE")
-    iota(T.KCA[:, :], [[-16, 32], [0, 16]], 496, 0, "KCA")
-    iota(T.KCB[:, :], [[0, 32], [-1, 16]], 16, 0, "KCB")
-    iota(T.JF[:, 0:2080], [[1, 2080]], 16, 0, "JF")
-    cp(T.QT1[:, 0:128], names_of(1, 0, 128), NBK, "QT1")
-    for f in repeat_names(1):
-        f()
-    select_row(range(8))
+    iota(T.RSM[:, :], [[0, 128], [256, 16]], 0, 0, "RSM")
+    iota(T.JF[:, :], [[1, W]], 16, 0, "JF")
+    wr["NE"] = wr["NEa"] + wr["NEb"]
     ts(T.OQ1[:, :], T.QT1[:, 0:128], 16.0, A.add, "QT1", "OQ1")
-    for k in range(16):
-        ts(T.SA[:, 128 * k:128 * k + 128], T.IDB[:, :], T.CA[:, k:k + 1], A.mult, "IDB CA", "+SA")
+    count_rows(range(8, 16))
     ts(T.PV[:, :], T.P4[:, 0:128], 32.0, A.is_le, "P4", "PV")
     tt(T.PVB[:, :], T.PV[:, :], T.HT[:, :], A.mult, "PV HT", "PVB")
     mm(T.P7[:, 0:128], T.PVB[:, :], T.IDB[:, :], True, True, "PVB IDB", "P7")
     ts(T.THR[:, :], T.PVB[:, :], 100.0, A.mult, "PVB", "THR", 9.0, A.add)
     weave(count(), self_out(1))
-    ts(T.DQ[:, :], T.P7[:, 0:128], 2048.0, A.mult, "P7", "DQ")
-    tt(T.QT2[:, 0:128], T.DQ[:, :], T.QT0[:, 0:128], A.max, "DQ QT0", "QT2")
-    ts(T.OQ2[:, :], T.QT2[:, 0:128], 16.0, A.add, "QT2", "OQ2")
-    weave(self_out(2))
+    ts(T.KB2[:, :], T.P7[:, 0:128], 131072.0, A.mult, "P7", "KB2", 131072.0, A.add)
+    ts(T.KC[:, :], T.LT[:, 0:32], T.P32[:, 0:1], A.add, "LT PX", "KC")
+    for j in range(8):
+        ts(T.SK[:, 16 * j:16 * j + 1936:129], T.ONEB[:, 0:16], T.BOK[:, j:j + 1], A.mult, "ONEB BOK", "SK" if j == 0 else "+SK")
 
     update(0)
-    more = repeat_names(2)
-    gaps[1, "degrees"], gaps[1, "lanes"] = more[:1], more[1:2]
     lanes_to_pivots(1)
-    more[2]()
+    repeat_names(T.QT0[:, 0:128], "QT0")
     new_names(1)
     send(1)
     weave(claims(4), count())
     send(4)
-    iota(T.JT[:, 0:2064], [[1, 2064]], 0, 0, "JT")
-    select_row(range(8, 16))
-    unpack(0, "SV", SIZES)
-    pivots("NB", 0, "NV0", NBK)
-    pivots("XS", 0, "SV", "XS")
+    iota(T.JT[:, :], [[1, W]], 0, 0, "JT")
+    unpack(0, "SV", SIZES, 32, ALL)
+    pivots(cp, "NB", 0, "NV0", NBK)
+    pivots(cp, "XS", 0, "SV", "XS")
 
     update(1)
-    ts(T.VF[:, :], piece(1, VREP, 32), 16.0, A.add, keys(1), "VF")
-    unpack(1, "SV", SIZES)
     for r in range(7, -1, -1):
-        cp(won("NE", 4, r), T.LD1[:, r, NAMES:NAMES + 32], "%s %s" % (key(4, r), key(1, r)), "NE")
-        silu(won("XE", 4, r), T.SVF[:, 32 * r:32 * r + 32], "SVF " + key(4, r), "XE")
-    todo = [lambda r=r: silu(won("JF", 4, r), T.VF[:, 32 * r:32 * r + 32], "VF " + key(4, r), "JF") for r in range(7, -1, -1)]
-    gaps[2, "select"], gaps[2, "roots"] = todo[:5], todo[5:]
+        won(cp, "NE", 4, r, "NV1")
+        won(silu, "XE", 4, r, "SVF")
+    todo = [lambda: act(T.VF[:, :], at_places("JF", 1, ALL), "JF " + parts("OF1", ALL), parts("VF", ALL))]
+    todo += [lambda r=r: won(silu, "JF", 4, r, "VF") for r in range(7, -1, -1)]
+    gaps[2, "select"], gaps[2, "roots"] = todo[:6], todo[6:]
     lanes_to_pivots(2)
+    select_row(range(8, 16))
     new_names(2)
     send(2)
     for k in range(16):
@@ -472,17 +495,20 @@ def rank_program(g, core, T, topo):
     weave(claims(3))
     send(3)
 
-    pivots("XS", 1, "SV", "XS")
-    all_places(5)
-    unpack(5, "SV", SIZES)
-    pivots("XS", 5, "SV", "XS")
+    unpack(1, "SV", SIZES, 32, ALL)
+    pivots(cp, "NB", 1, "NV1", NBK)
+    pivots(cp, "XS", 1, "SV", "XS")
+    unpack(5, "OF5", VOFF, 2, ALL)
+    unpack(5, "SV", SIZES, 32, ALL)
+    act(T.VJ[:, :], at_places("JT", 5, ALL), "JT " + parts("OF5", ALL), parts("VJ", ALL))
+    pivots(cp, "XS", 5, "SV", "XS")
     dma("s", T.yx[:, :], T.XS[:, 16:2064], "o_x", "XS", "")
-    pivots("NB", 1, "NV1", NBK)
-    pivots("NB", 5, "LD2", NBK, keys(2))
+    for part in (EARLY, LATE):
+        pivots(cp, "NB", 5, "LD2", NBK, part, keys(2, part))
     dma("s", T.yn[:, :], T.NB[:, 16:2064], "o_n", NBK, "")
     ts(T.JL[:, :], T.P5[:, 0:128], -15.75, A.add, "P5", "JL")
     for r in range(7, -1, -1):
-        cp(won("JT", 3, r), T.LD5[:, r, VREP:VREP + 32], "%s %s" % (key(3, r), key(5, r)), "JT")
+        won(cp, "JT", 3, r, "VJ")
     act(T.YJ[:, 0:1024], T.JT[:, 0:2064].indirect(T.JL[:, 0:64]), "JT JL", "YJ0", func=IDN, bias=-16.0)
     ts(T.YJ[:, 1024:2048], T.JT[:, 0:2064].indirect(T.JL[:, 64:128]), -16.0, A.add, "JT JL", "YJ1")
     dma("a", T.yj[:, 0:1024], T.YJ[0:128:16, 0:1024], "o_j0", "YJ0", "")

@@ -2,27 +2,27 @@ from concourse.bass import DstId, RemoteDMATransfer
 from concourse.mybir import AluOpType, AxisListType, ActivationFunctionType
 
 W = 2368
+BIG = 12582912.0
 F, B, I, U = "float32", "bfloat16", "int32", "uint16"
 SCRATCH = {}
 for _names, _w, _d in (
-        ("NB JT NE XE JF", W, F), ("XS", W, B), ("SA SK EQ XG XV MX RSM", 2048, B), ("SAF QR YJ", 2048, F),
+        ("NB JT NE XE JF XO", W, F), ("XS", W, B), ("SA EQ XG XV MX RSM", 2048, B), ("SAF QR YJ", 2048, F), ("SK", 512, B), ("BOK", 128, B), ("KC KM KS RSK IOK IOH", 128, F), ("HT0", 128, B), ("OV", 32, F),
         ("Q2 CC NS", 512, F), ("E2", 520, F), ("X2 MM", 512, B), ("RSTB", 256, B), ("ONEB IDB I4 BO TRI HR HT PV PVB KB1 KB2", 128, B), ("CMP", 256, B),
-        ("IDF TQ UA UN THR", 128, F), ("SB SVF VF VJ", 256, F), ("WTS PR", 2, B),
-        ("PI PA LIMI AI AM", 1, I), ("PF P32 LIMA LIMH", 1, F), ("COL BOK", 8, F), ("CA CB CM CV IO16", 16, F),
-        ("LT VT0 VT1 QT0 QT1 QX0 QX1 OWN SZ", 136, F), ("OQ0 OQ1 UL JL", 128, U),
-        ("IO32 D2 OP NM TM TL KC KS RST RSK", 32, F), ("IO66 RL ED DX", 66, F), ("LW UW", 2, U), ("EP EK L16", 32, U), ("KI K5", 2, I), ("JE", 32, I),
-        ("OF0 OF1 OF5", 16, U), ("NV0 NV1 SV", 256, U)):
+        ("IDF TQ UN THR", 128, F), ("SB SF0 SF1 SF5 VF VJ", 256, F), ("WTS PR", 2, B),
+        ("PI PA PB LIMI AI AM", 1, I), ("PF PH PQ LIMA LIMH", 1, F), ("COL", 8, F), ("CA CB CM CV IO16", 16, F),
+        ("LT VT0 VT1 QT0 QT1 OWN SZ", 136, F), ("OQ0 OQ1 UL JL", 128, U),
+        ("IO32 D2 OP NM TM TL RST", 32, F), ("IO66 RL ED DX", 66, F), ("LW UW", 2, U), ("EP L16", 32, U), ("KI", 2, F), ("JE", 32, I),
+        ("OF0 OF1 OF5", 16, U), ("NV0 NV1", 256, U)):
     for _n in _names.split():
         SCRATCH[_n] = ("sbuf", [128, _w], _d)
-for _b in range(6):
+for _b in (0, 1, 3, 4, 5):
     SCRATCH["LD%d" % _b] = ("sbuf", [128, 8, 72], U)
-SCRATCH["LD2"] = ("sbuf", [128, 256], U)
 for _b in range(8):
     SCRATCH["P%d" % _b] = ("psum", [128, 512], F)
 SEMAPHORES = ["ev", "et", "ea", "eg", "d_x", "d_n0", "d_n1", "d_n2", "d_l", "o_n", "o_x", "o_j0", "o_j1"]
-SEMAPHORES += ["a%d_%d" % (m, r) for m in range(6) for r in range(8)] + ["l%d" % m for m in range(6)]
+SEMAPHORES += ["a%d_%d" % (m, r) for m in (0, 1, 3, 4, 5) for r in range(8)] + ["l%d" % m for m in (0, 1, 3, 4, 5)]
 VOFF, SIZES, NAMES, EOFF = 0, 2, 34, 66
-SPAN = [(0, 66), (0, 66), (34, 66), (66, 68), (66, 68), (0, 34)]
+SPAN = {0: (0, 66), 1: (0, 34), 4: (34, 68), 5: (0, 34), 3: (34, 68)}
 
 
 def rank_program(g, core, T, topo):
@@ -126,19 +126,19 @@ def rank_program(g, core, T, topo):
 
     cls = [rank, 8 + rank, rank]
     VTs = ["VT0", "VT1", "VT0"]
+    BLOCKS = ((0, 64), (64, 96), (96, 128))
     NBK = "NB0 NB1 NB2"
-    TAB = {n: T[n][:, 0:W] for n in ("NB", "XS", "NE", "XE", "JT", "JF")}
+    TAB = {n: T[n][:, 0:W] for n in ("NB", "XO", "NE", "XE", "JT", "JF")}
     NEW, XEW = T.NE[:, 0:2080], T.XE[:, 0:2080]
 
     dma("a", T.XS[:, 16:2064], T.xs[:, :], "d_x", "", "XS")
-    dma("s", T.NB[:, 16:1040], T.nb[:, 0:1024], "d_n0", "", "NB0")
+    for j, (a, b) in enumerate(BLOCKS):
+        dma("s", T.NB[:, 16 + 16 * a:16 + 16 * b], T.nb[:, 16 * a:16 * b], "d_n%d" % j, "", "NB%d" % j)
     dma("a", T.LIMI[:, :], T.lim[:, :], "d_l", "", "LIMI")
-    dma("s", T.NB[:, 1040:1552], T.nb[:, 1024:1536], "d_n1", "", "NB1")
-    dma("s", T.NB[:, 1552:2064], T.nb[:, 1536:2048], "d_n2", "", "NB2")
 
     fill(T.ONEB[:, :], 1.0, "ONEB")
-    fill(T.SK[:, :], 0.0, "SK")
-    for a, b, src in ((0, 128, "ONEB"), (128, 2080, "SK")):
+    fill(T.RSM[:, :], 256.0, "RSM")
+    for a, b, src in ((0, 128, "ONEB"), (128, 2080, "RSM")):
         act(T.XE[:, a:b], T[src][:, 0:b - a], src, "+XE", func=ActivationFunctionType.Silu, bias=30.0, scale=0.0)
     fill(T.WTS[:, 0:1], 1.0, "+WTS")
     fill(T.WTS[:, 1:2], 16.0, "+WTS")
@@ -155,22 +155,19 @@ def rank_program(g, core, T, topo):
     asel(T.WTS[:, 1:2], T.WTS[:, 1:2], [[0, 1]], A.not_equal, 384.0, -127, 1, "WTS", "WTS")
     iota(T.VT0[:, :], [[16, 136]], cls[0], 0, "VT0")
     iota(T.SB[:, :], [[-16, 2], [0, 8], [-1, 16]], 31, 0, "SB")
-    iota(T.LT[:, :], [[1, 136]], 0, 0, "LT")
-    iota(T.VT1[:, :], [[16, 136]], cls[1], 0, "VT1")
-    iota(T.NE[:, 0:1040], [[0, 1040]], 2050, 0, "NEa")
+    iota(T.NE[:, 0:1440], [[0, 1440]], 2050, 0, "NEa")
     for n in ("QT0", "QT1"):
         fill(T[n][:, 128:136], 2048.0, n + "p")
-    for n in ("QX0", "OWN"):
-        fill(T[n][:, 128:136], 4096.0, n + "p")
-    fill(T.SZ[:, 128:136], 0.0, "SZp")
+    fill(T.OWN[:, 128:136], 0.0, "OWNp")
+    fill(T.SZ[:, 128:136], 255.0, "SZp")
     fill(T.E2[:, 512:520], 4096.0, "E2p")
     fill(T.ED[:, :], 0.0, "ED")
     fill(T.KB1[:, :], 131072.0, "KB1")
-    resets = (("RST", 32, 1.0, 0.0), ("RSK", 32, -8388608.0, 512.0), ("RSTB", 256, 0.0, 8192.0))
-    for n, w, c, c0 in resets:
+    resets = (("RST", 32, 16, 1.0, 0.0), ("RSK", 128, 64, -8388608.0, 512.0), ("RSTB", 256, 16, 0.0, 8192.0))
+    for n, w, step, c, c0 in resets:
         fill(T[n][:, :], c, n)
-    for n, w, c, c0 in resets:
-        fill(T[n][:, 0:w:16], c0, n)
+    for n, w, step, c, c0 in resets:
+        fill(T[n][:, 0:w:step], c0, n)
     ts(T.PA[:, :], T.PI[:, :], 15, A.bitwise_and, "PI", "PA")
     cp(T.IDF[:, :], T.IDB[:, :], "IDB", "IDF")
     cp(T.PF[:, :], T.PA[:, :], "PA", "PF")
@@ -184,13 +181,14 @@ def rank_program(g, core, T, topo):
     ts(T.RL[:, :], T.IO66[:, :], T.PF[:, 0:1], A.is_gt, "IO66 PF", "RL")
     ts(T.CV[:, :], T.CB[:, :], 2050.0, A.mult, "CB", "CV")
     ts(T.CA[:, :], T.CB[:, :], -126976.0, A.mult, "CB", "CA", -4096.0, A.add)
-    ts(T.BOK[:, :], T.BO[:, 0:128:16], -1024.0, A.mult, "BO", "BOK")
-    ts(T.P32[:, :], T.PF[:, :], 32.0, A.mult, "PF", "PX")
+    ts(T.BOK[:, :], T.BO[:, :], -1024.0, A.mult, "BO", "BOK")
 
     def count_rows(ks):
         for k in ks:
             ts(T.SA[:, 128 * k:128 * k + 128], T.IDB[:, :], T.CA[:, k:k + 1], A.mult, "IDB CA", "+SA")
-    count_rows(range(8))
+    weave([lambda: ts(T.PB[:, :], T.PI[:, :], 3, A.bitwise_and, "PI", "PB"), lambda: cp(T.PH[:, :], T.PB[:, :], "PB", "PH"),
+           lambda: ts(T.PQ[:, :], T.PF[:, :], T.PH[:, 0:1], A.subtract, "PF PH", "PQ", 16.0, A.mult)],
+          [lambda: count_rows(range(2)), lambda: count_rows(range(2, 4))])
 
     def names_of(t, a, b):
         return T.NB[:, 16 + 16 * a + cls[t]:16 + 16 * b:16]
@@ -205,7 +203,8 @@ def rank_program(g, core, T, topo):
     def far(r):
         i = [r in c for c in chips].index(True)
         j = chips[i].index(r)
-        return [x for c in chips[i + 1:] + chips[:i] for x in c[j:] + c[:j]]
+        later = sorted(chips[i + 1:] + chips[:i], key=lambda c: topo.same_plane(topo.chip(T.cores[r]), topo.chip(T.cores[c[0]])))
+        return [x for c in later for x in c[j:] + c[:j]]
 
     def slot(d, r):
         return 0 if r == d else 2 + far(r).index(d) if d in far(r) else 1
@@ -215,8 +214,6 @@ def rank_program(g, core, T, topo):
     ne = [e for e in topo.engines(core, T.cores[near[0]]) if e not in fe][:2]
 
     def msg(m, j, a, n):
-        if m == 2:
-            return T.LD2[:, 32 * j:32 * j + 32]
         return T["LD%d" % m][:, j, a:a + n]
 
     def mine(m, a, n):
@@ -225,14 +222,8 @@ def rank_program(g, core, T, topo):
     def key(m, r):
         return "M%d" % m if r == rank else "LD%d_%d" % (m, r)
 
-    def self_out(t):
-        n, vt, qt = "QX%d" % t, VTs[t], "QT%d" % t
-        return [lambda: tt(T.TQ[:, :], T[qt][:, 0:128], T[vt][:, 0:128], A.is_equal, qt + " " + vt, "TQ"),
-                lambda: ts(T.TQ[:, :], T.TQ[:, :], 4096.0, A.mult, "TQ", "TQ"),
-                lambda: tt(T[n][:, 0:128], T.TQ[:, :], T[qt][:, 0:128], A.max, "TQ " + qt, n)]
-
-    def repeat_names(names, rk):
-        for k in range(16):
+    def repeat_names(names, rk, ks):
+        for k in ks:
             act(T.QR[:, k:2048:16], names, rk + " CM CV", "+QR", func=IDN, bias=T.CV[:, k:k + 1], scale=T.CM[:, k:k + 1])
 
     def gather_sizes(q, lst, a, b):
@@ -241,10 +232,10 @@ def rank_program(g, core, T, topo):
 
     def degrees(a, b, keys, mx):
         o = T.P2[:, a:b]
-        if mx:
-            mm(o, T.IDB[:, :], T.MX[:, 16 * a + 15:16 * b:16], True, False, "IDB MX", "P2")
         for k in range(16):
-            mm(o, T.IDB[:, :], T.XV[:, 16 * a + k:16 * b:16], k == 0 and not mx, k == 15, "IDB " + keys, "P2")
+            mm(o, T.IDB[:, :], T.XV[:, 16 * a + k:16 * b:16], k == 0, k == 15 and not mx, "IDB " + keys, "P2")
+        if mx:
+            mm(o, T.IDB[:, :], T.MX[:, 16 * a + 15:16 * b:16], False, True, "IDB MX%d" % (a // 64), "P2")
 
     gaps = {}
 
@@ -256,22 +247,25 @@ def rank_program(g, core, T, topo):
         lim = "LIMA" if t else "LIMH"
         ts(T.HR[:, :], T.P2[:, 0:128], T[lim][:, 0:1], A.is_le, "P2 " + lim, "HR")
         mm(T.P3[:, 0:128], T.HR[:, :], T.BO[:, :], True, True, "HR BO", "P3")
-        ts(T.SZ[:, 0:128], T.P2[:, 0:128], 255.0, A.min, "P2", "SZ")
+        act(T.SZ[:, 0:128], T.P2[:, 0:128], "P2", "SZ", func=ActivationFunctionType.Relu, bias=255.0, scale=-1.0)
         gap(t, "hits")
+        ht = "HT" if t else "HT0"
         if t < 2:
-            ts(T.HT[:, :], T.P3[:, 0:128], 9.0, A.is_ge, "P3", "HT")
+            ts(T[ht][:, :], T.P3[:, 0:128], 9.0, A.is_ge, "P3", ht)
         else:
             tt(T.HT[:, :], T.P3[:, 0:128], T.THR[:, :], A.is_ge, "P3 THR", "HT")
-        for b in range(2):
-            mm(T.P4[:, 128 * b:128 * b + 128], T.TRI[:, :], T.HT[:, :], True, True, "TRI HT", "P4")
-        if t:
-            tt(T.OWN[:, 0:128], T.UA[:, :], T["QX%d" % (t % 2)][:, 0:128], A.max, "UA QX%d" % (t % 2), "OWN")
+        mm(T.P4[:, 0:128], T.TRI[:, :], T[ht][:, :], True, True, "TRI " + ht, "P4")
         gap(t, "rank")
-        tt(T.CMP[:, :], T.P4[:, 0:256], T.SB[:, :], A.is_le, "P4 SB", "CMP")
         for b in range(2):
-            mm(T.P5[:, 2 * b:2 * b + 2], T.CMP[:, 128 * b:128 * b + 128], T.WTS[:, :], True, True, "CMP WTS", "P5")
+            tt(T.CMP[:, 128 * b:128 * b + 128], T.P4[:, 0:128], T.SB[:, 128 * b:128 * b + 128], A.is_le, "P4 SB", "CMP%d" % b)
+            mm(T.P5[:, 2 * b:2 * b + 2], T.CMP[:, 128 * b:128 * b + 128], T.WTS[:, :], True, True, "CMP%d WTS" % b, "P5")
         gap(t, "lanes")
         cp(T.LW[:, :], T.P5[:, 0:4:2], "P5", "LW")
+        places(t)
+
+    def new_sizes(t):
+        ts(mine(ahead[t], SIZES, 32), at_pivots("SZ"), -1.0, A.mult, "SZ SZp LW", "+M%d" % ahead[t], 255.0, A.add)
+        send(ahead[t])
 
     ahead = [0, 1, 5]
 
@@ -297,13 +291,13 @@ def rank_program(g, core, T, topo):
             if r != rank:
                 wr["LD%d_%d" % (m, r)] = [("r", "a%d_%d" % (m, r), len(ne) if r in near else len(fe), {})]
 
-    ALL, EARLY, LATE = (0, 8), (0, 6), (6, 8)
+    ALL, EARLY, MID, LATE = (0, 8), (0, 1), (1, 4), (4, 8)
 
     def keys(m, part):
         return " ".join(key(m, r) for r in range(8) if part[0] <= slot(rank, r) < part[1])
 
     def parts(buf, part):
-        return " ".join("%s_%d" % (buf, p[0]) for p in (EARLY, LATE) if part[0] <= p[0] < part[1])
+        return " ".join("%s_%d" % (buf, j) for j in range(*part))
 
     def unpack(m, buf, a, n, part, add=None):
         out, in_ = T[buf][:, n * part[0]:n * part[1]], T["LD%d" % m][:, part[0]:part[1], a:a + n]
@@ -322,14 +316,6 @@ def rank_program(g, core, T, topo):
         j = slot(rank, r)
         f(TAB[tab].indirect(msg(m, j, EOFF, 2)), T[buf][:, 32 * j:32 * j + 32], parts(buf, ALL) + " " + key(m, r), tab)
 
-    def update(m):
-        for part in (EARLY, LATE):
-            unpack(m, "OF%d" % m, VOFF, 2, part)
-            unpack(m, "SVF", SIZES, 32, part, 32.0)
-            unpack(m, "NV%d" % m, NAMES, 32, part)
-            pivots(silu, "XE", m, "SVF", "XE", part)
-            pivots(cp, "NE", m, "NV%d" % m, "NE", part)
-
     def count():
         def total():
             ts(T.PR[:, :], T.P5[:, 0:4:2], 127.5, A.is_le, "P5", "PR")
@@ -339,76 +325,79 @@ def rank_program(g, core, T, topo):
                 lambda: ts(T.AM[:, :], T.AI[:, :], 7, A.bitwise_and, "AI", "AM"),
                 lambda: tt(T.LIMA[:, :], T.AM[:, :], T.LIMH[:, :], A.add, "AM LIMH", "LIMA")]
 
-    def empty_covered(t):
+    def own_names(t):
         for h in range(2):
-            ts(T.UN[:, 64 * h:64 * h + 64], T["P%d" % h][:, 0:64], 0.0, A.is_lt, "P%d" % h, "+UN", 2048.0, A.mult)
-        tt(names_of(t, 0, 128), T.UN[:, :], names_of(t, 0, 128), A.max, "UN " + NBK, NBK)
+            ts(T.UN[:, 64 * h:64 * h + 64], T["P%d" % h][:, 0:64], 0.0, A.is_lt, "P%d" % h, "UN%d" % h, 2048.0, A.mult)
+        for h in range(2):
+            tt(T.OWN[:, 64 * h:64 * h + 64], T["P%d" % h][:, 0:64], T.UN[:, 64 * h:64 * h + 64], A.max, "P%d UN%d" % (h, h), "+OWN")
+        tt(names_of(t, 0, 128), T.UN[:, :], names_of(t, 0, 128), A.max, "UN0 UN1 " + NBK, NBK)
+
+    def key_places():
+        mm(T.P6[:, 0:128], T.IDF[:, :], T.KC[:, :], True, False, "IDF KC", "P6")
+        mm(T.P6[:, 0:128], T.IDF[:, :], T.KM[:, :], False, False, "IDF KM", "P6")
 
     def lanes_to_pivots(t):
         qt, oq, kb = "QT%d" % (t % 2), "OQ%d" % (t % 2), "KB%d" % t
         ok = "OQ1" if t == 1 else "OQ0_0 OQ0_1 OQ0_2"
-        for h in range(2):
-            act(T.XG[:, 1024 * h:1024 * h + 1024], XEW.indirect(T[oq][:, 64 * h:64 * h + 64]), "XE " + ok, "XG%d" % h, func=IDN, bias=-32.0)
+        act(T.XG[:, :], XEW.indirect(T[oq][:, :]), "XE " + ok, "XG", func=IDN, bias=-32.0)
 
         def cover(a, b, k):
             tt(T.EQ[:, 16 * a:16 * b], NEW.indirect(T[oq][:, a:b]), T.QR[:, 16 * a:16 * b], A.is_equal, "NE QR " + ok, k)
         cover(0, 64, "EQ0")
-        cover(64, 96, "EQ1")
+        cover(64, 112, "EQ1")
         for h in range(2):
             o = T["P%d" % h][:, 0:64]
             mm(o, T.IDF[:, :], T[qt][:, 64 * h:64 * h + 64], True, False, "IDF " + qt, "P%d" % h)
             mm(o, T.IDB[:, :], T[kb][:, 64 * h:64 * h + 64], False, False, "IDB " + kb, "P%d" % h)
-        mm(T.P6[:, 0:32], T.IDF[:, :], T.KC[:, :], True, False, "IDF KC", "P6")
+        gap(t, "cover")
         for h in range(2):
             if h:
                 ts(T.UL[:, 0:64], T.P0[:, 0:64], 16.0, A.add, "P0", "UL_0", 2064.0, A.min)
-                cover(96, 128, "EQ2")
+                cover(112, 128, "EQ2")
             for k in range(16):
                 mm(T["P%d" % h][:, 0:64], T.SA[:, 128 * k:128 * k + 128], T.EQ[:, 1024 * h + k:1024 * h + 1024:16], False, k == 15,
                    "SA " + ("EQ1 EQ2" if h else "EQ0"), "P%d" % h)
-        gather_sizes("a", "UL_0", 0, 64)
-        scan(T.MX[:, :], T.RSM[:, :], T.XG[:, :], 0.0, A.min, A.max, "RSM XG0 XG1", "MX")
-        ts(T.UL[:, 64:128], T.P1[:, 0:64], 16.0, A.add, "P1", "UL_1", 2064.0, A.min)
-        gather_sizes("a", "UL_1", 64, 88)
-        gather_sizes("v", "UL_1", 88, 128)
-        empty_covered(t)
-        degrees(0, 64, "XV0", True)
-        degrees(64, 128, "XV64 XV88", True)
-        for h in range(2):
-            act(T.UA[:, 64 * h:64 * h + 64], T["P%d" % h][:, 0:64], "P%d" % h, "+UA", func=ActivationFunctionType.Abs)
+        cuts = (52, 92 + 4 * t)
+        for h, cut in enumerate(cuts):
+            if h:
+                ts(T.UL[:, 64:128], T.P1[:, 0:64], 16.0, A.add, "P1", "UL_1", 2064.0, A.min)
+            gather_sizes("a", "UL_%d" % h, 64 * h, cut)
+            gather_sizes("v", "UL_%d" % h, cut, 64 * h + 64)
+            scan(T.MX[:, 1024 * h:1024 * h + 1024], T.RSM[:, 0:1024], T.XG[:, 1024 * h:1024 * h + 1024], 0.0, A.min, A.max, "RSM XG", "MX%d" % h)
+        own_names(t)
+        for h, cut in enumerate(cuts):
+            degrees(64 * h, 64 * h + 64, "XV%d XV%d" % (64 * h, cut), True)
         gap(t, "select")
         select(t)
-        ts(T.EP[:, :], at_pivots(qt), 16.0, A.add, "%s %sp LW" % (qt, qt), "EP")
-        for h in range(2):
-            act(T.Q2[:, 256 * h:256 * h + 256], NEW.indirect(T.EP[:, 16 * h:16 * h + 16]), "NE EP", "Q2_%d" % h)
-        cp(T.L16[:, :], at_pivots("LT"), "LT LW", "L16")
-        cp(mine(ahead[t], SIZES, 32), at_pivots("SZ"), "SZ SZp LW", "+M%d" % ahead[t])
-        places(t)
-        if t == 2:
-            send(5)
-        for b in range(2):
-            cp(T.EK[:, b:32:2], T.EP[:, 16 * b:16 * b + 16], "EP", "+EK")
-        act(T.X2[:, :], XEW.indirect(T.EK[:, :]), "XE EK", "X2", func=IDN, bias=-31.0)
-        gap(t, "roots")
-        act(T.E2[:, 0:512], T.JF[:, 0:2080].indirect(T.EK[:, :]), "JF EK", "E2", func=IDN, bias=-16.0)
 
-    def new_names(t):
-        vt, half, pb = VTs[t], [slice(0, 256), slice(256, 512)], ["P7", "P3"]
-        for h in range(2):
+    def pivots_make(t, order, more):
+        qt, vt, half, pb, m = "QT%d" % (t % 2), VTs[t], [slice(0, 256), slice(256, 512)], ["P3", "P4"], [None, 4, 3][t]
+        col = [T.TL[:, 15:16], T.TL[:, 31:32]]
+
+        def names(h):
+            act(T.Q2[:, half[h]], NEW.indirect(T.EP[:, 16 * h:16 * h + 16]), "NE EP", "Q2_%d" % h)
+
+        def itself(h):
             tt(T.MM[:, half[h]], T[vt][:, 0:136].indirect(T.L16[:, 16 * h:16 * h + 16]), T.Q2[:, half[h]], A.is_equal, "%s L16 Q2_%d" % (vt, h), "MM%d" % h)
             mm(T[pb[h]][:, 0:256], T.I4[:, :], T.MM[:, half[h]], True, True, "I4 MM%d" % h, pb[h])
-        for p in range(16):
-            mm(T.P6[:, 0:32], T.SK[:, 128 * p:128 * p + 128], T.X2[:, 32 * p:32 * p + 32], False, p == 15, "SK X2", "P6")
-        cp(T.OP[:, :], at_pivots("OWN"), "OWN OWNp LW", "OP")
-        for h in range(2):
-            tt(T.CC[:, half[h]], T.Q2[:, half[h]], T[pb[h]][:, 0:256], A.add, "Q2_%d %s" % (h, pb[h]), "CC%d" % h)
-        for h in range(2):
-            scan(T.NS[:, half[h]], T.RSTB[:, 0:256], T.CC[:, half[h]], 8192.0, A.add, A.min, "RSTB CC%d" % h, "NS%d" % h)
-        tt(T.NM[:, :], T.NS[:, 15:512:16], T.OP[:, :], A.min, "NS0 NS1 OP", "NM")
-        ts(mine(t, NAMES, 32), T.NM[:, :], 2048.0, A.min, "NM", "+M%d" % t)
 
-    def claims(m):
-        col = [T.TL[:, 15:16], T.TL[:, 31:32]]
+        def large(h):
+            tt(T.CC[:, half[h]], T.Q2[:, half[h]], T[pb[h]][:, 0:256], A.add, "Q2_%d %s" % (h, pb[h]), "CC%d" % h)
+
+        def least(h):
+            scan(T.NS[:, half[h]], T.RSTB[:, 0:256], T.CC[:, half[h]], 8192.0, A.add, A.min, "RSTB CC%d" % h, "NS%d" % h)
+
+        def elements(h):
+            act(T.X2[:, half[h]], XEW.indirect(T.EP[:, 16 * h:16 * h + 16]), "XE EP", "X2_%d" % h, func=IDN, bias=-31.0)
+
+        def key_sums(h):
+            for a in range(4):
+                mm(T.P6[:, 64 * h:64 * h + 64], T.SK[:, 128 * a:128 * a + 128], T.X2[:, 256 * h + 64 * a:256 * h + 64 * a + 64], False, h == 1 and a == 3,
+                   "SK X2_%d" % h, "P6")
+
+        def place():
+            for b in range(2):
+                ts(T.UW[:, b:b + 1], T.KS[:, 64 * b + 63:64 * b + 64], T.KI[:, b:b + 1], A.subtract, "KS KI", "+UW")
 
         def same():
             for b in range(2):
@@ -417,100 +406,144 @@ def rank_program(g, core, T, topo):
         def out():
             for b in range(2):
                 ts(mine(m, EOFF + b, 1), T.DX[:, 33 * b + 32:33 * b + 33], col[b], A.max, "DX COL TL", "+M%d" % m, TRE[b], A.min)
-        return [lambda: scan(T.KS[:, :], T.RSK[:, :], T.P6[:, 0:32], 0.0, A.max, A.min, "RSK P6", "KS"),
-                lambda: cp(T.KI[:, :], T.KS[:, 15:32:16], "KS", "KI"),
-                lambda: ts(T.K5[:, :], T.KI[:, :], 1023, A.bitwise_and, "KI", "K5"),
-                lambda: cp(T.UW[:, :], T.K5[:, :], "K5", "UW"),
-                lambda: cp(T.JE[:, :], T.E2[:, :].indirect(T.UW[:, :]), "E2 E2p UW", "JE"),
-                lambda: tt(T.TM[:, :], T.JE[:, :], T.D2[:, :], A.mult, "JE D2", "TM"),
-                lambda: scan(T.TL[:, :], T.RST[:, :], T.TM[:, :], 0.0, A.mult, A.add, "RST TM", "TL"),
-                same, lambda: scan(T.DX[:, :], T.RL[:, :], T.ED[:, :], 0.0, A.mult, A.max, "RL ED", "DX"), out]
+            send(m)
+
+        step = dict(
+            EP=lambda: ts(T.EP[:, :], at_pivots(qt), 16.0, A.add, "%s %sp LW" % (qt, qt), "EP"),
+            L16=lambda: cp(T.L16[:, :], at_pivots("LT"), "LT LW", "L16"),
+            SZ=lambda: new_sizes(t), Qa=lambda: names(0), Qb=lambda: names(1), Ma=lambda: itself(0), Mb=lambda: itself(1),
+            Ca=lambda: large(0), Cb=lambda: large(1), Na=lambda: least(0), Nb=lambda: least(1),
+            OP=lambda: cp(T.OP[:, :], at_pivots("OWN"), "OWN OWNp LW", "OP"),
+            OV=lambda: tt(T.OV[:, :], at_pivots(vt), T.OP[:, :], A.is_equal, vt + " LW OP", "OV"),
+            OW=lambda: ts(T.OV[:, :], T.OV[:, :], 4096.0, A.mult, "OV", "OV"),
+            OX=lambda: tt(T.OP[:, :], T.OP[:, :], T.OV[:, :], A.max, "OP OV", "OP"),
+            NM=lambda: tt(T.NM[:, :], T.NS[:, 15:512:16], T.OP[:, :], A.min, "NS0 NS1 OP", "NM"),
+            NAMES=lambda: ts(mine(m, NAMES, 32), T.NM[:, :], 2048.0, A.min, "NM", "+M%d" % m),
+            Xa=lambda: elements(0), Xb=lambda: elements(1), Ka=lambda: key_sums(0), Kb=lambda: key_sums(1),
+            E2=lambda: act(T.E2[:, 0:512], T.JF[:, 0:2080].indirect(T.EP[:, :]), "JF EP", "E2", func=IDN, bias=-16.0),
+            KS=lambda: scan(T.KS[:, :], T.RSK[:, :], T.P6[:, 0:128], 0.0, A.max, A.min, "RSK P6", "KS"),
+            KI=lambda: ts(T.KI[:, :], T.KS[:, 63:128:64], BIG * 1024, A.add, "KS", "KI", BIG * 1024, A.subtract), UW=place,
+            JE=lambda: cp(T.JE[:, :], T.E2[:, :].indirect(T.UW[:, :]), "E2 E2p UW", "JE"),
+            TM=lambda: tt(T.TM[:, :], T.JE[:, :], T.D2[:, :], A.mult, "JE D2", "TM"),
+            TL=lambda: scan(T.TL[:, :], T.RST[:, :], T.TM[:, :], 0.0, A.mult, A.add, "RST TM", "TL"),
+            ED=same, DX=lambda: scan(T.DX[:, :], T.RL[:, :], T.ED[:, :], 0.0, A.mult, A.max, "RL ED", "DX"), CLAIMS=out, **more)
+        for name in order.split():
+            step[name]()
 
     def select_row(ks):
         for k in ks:
-            act(T.SAF[:, 128 * k:128 * k + 128], T.IDF[:, :], "IDF CB", "SAF%d" % k, scale=T.CB[:, k:k + 1])
+            asel(T.SAF[:, 128 * k:128 * k + 128], T.IDF[:, :], [[0, 8], [1, 16]], A.is_equal, 0.0, -k, 0, "IDF", "SAF%d" % k)
 
-    for j, (a, b) in enumerate(((0, 64), (64, 96), (96, 128))):
+    def sizes_out(a, b):
+        act(T.XO[:, a:b], T.XS[:, a:b], "XS", "XO_%d" % a, func=IDN, bias=32.0)
+
+    got = []
+    for j, (a, b) in enumerate(BLOCKS):
         c = (a + b) // 2
         ts(T.OQ0[:, a:b], names_of(0, a, b), 16.0, A.add, "NB%d" % j, "OQ0_%d" % j)
         gather_sizes("a", "OQ0_%d" % j, a, c)
         gather_sizes("v", "OQ0_%d" % j, c, b)
-        degrees(a, b, "XV%d XV%d" % (a, c), False)
-        cp(T.QT0[:, a:b], names_of(0, a, b), "NB%d" % j, "+QT0")
+        got += ["XV%d" % a, "XV%d" % c]
+        if b % 64 == 0:
+            degrees(b - 64, b, " ".join(got[-4:]), False)
         if j == 1:
             ts(T.LIMH[:, :], T.LIMI[:, :], 0.5, A.add, "LIMI", "LIMH")
-    act(T.NE[:, 1040:2080], T.XS[:, 0:1040], "XS XSp", "NEb", func=IDN, bias=2050.0, scale=0.0)
-    repeat_names(names_of(1, 0, 128), NBK)
-    select_row(range(8))
-    own0 = self_out(0)
-    weave(own0[:2])
-    gaps[0, "rank"] = own0[2:]
-    gaps[0, "lanes"] = [lambda: cp(T.QT1[:, 0:128], names_of(1, 0, 128), NBK, "QT1")]
+    act(T.UN[:, :], names_of(0, 0, 128), NBK, "UN0 UN1", func=IDN, bias=2048.0, scale=-1.0)
+    repeat_names(names_of(1, 0, 128), NBK, range(3))
+    tt(T.TQ[:, :], names_of(0, 0, 128), T.VT0[:, 0:128], A.not_equal, NBK + " VT0", "TQ")
+    tt(T.OWN[:, 0:128], T.TQ[:, :], T.UN[:, :], A.mult, "TQ UN0 UN1", "OWN")
+    gaps[0, "rank"] = [lambda: fill(T.RSM[:, 0:2048:16], 0.0, "RSM")]
+    gaps[0, "hits"] = [lambda: ts(T.OQ1[:, :], names_of(1, 0, 128), 16.0, A.add, NBK, "OQ1"),
+                       lambda: act(T.QT1[:, 0:128], names_of(1, 0, 128), NBK, "QT1"), lambda: repeat_names(names_of(1, 0, 128), NBK, range(3, 16))]
+    gaps[0, "lanes"] = [lambda: ts(T.PV[:, :], T.P4[:, 0:128], 32.0, A.is_le, "P4", "PV")]
     select(0)
-    ts(mine(0, NAMES, 32), at_pivots("QX0"), 2048.0, A.min, "QX0 QX0p LW", "+M0")
-    cp(mine(0, SIZES, 32), at_pivots("SZ"), "SZ SZp LW", "+M0")
-    places(0)
-    send(0)
+    ts(mine(0, NAMES, 32), at_pivots("OWN"), -1.0, A.mult, "OWN OWNp LW", "+M0", 2048.0, A.add)
+    new_sizes(0)
 
-    iota(T.RSM[:, :], [[0, 128], [256, 16]], 0, 0, "RSM")
+    iota(T.NE[:, 1440:2080], [[0, 640]], 2050, 0, "NEb")
+    iota(T.LT[:, :], [[1, 136]], 0, 0, "LT")
+    iota(T.VT1[:, :], [[16, 136]], cls[1], 0, "VT1")
+    iota(T.IOK[:, :], [[256, 2], [1, 64]], 0, 0, "IOK")
+    iota(T.IOH[:, :], [[0, 2], [1, 4], [0, 16]], 0, 0, "IOH")
+    for a in range(4):
+        asel(T.SK[:, 128 * a:128 * a + 128], T.BOK[:, :], [[0, 8], [1, 4], [0, 4]], A.is_equal, 0.0, -a, 0, "BOK", "+SK")
     iota(T.JF[:, :], [[1, W]], 16, 0, "JF")
     wr["NE"] = wr["NEa"] + wr["NEb"]
-    ts(T.OQ1[:, :], T.QT1[:, 0:128], 16.0, A.add, "QT1", "OQ1")
-    count_rows(range(8, 16))
-    ts(T.PV[:, :], T.P4[:, 0:128], 32.0, A.is_le, "P4", "PV")
-    tt(T.PVB[:, :], T.PV[:, :], T.HT[:, :], A.mult, "PV HT", "PVB")
-    mm(T.P7[:, 0:128], T.PVB[:, :], T.IDB[:, :], True, True, "PVB IDB", "P7")
-    ts(T.THR[:, :], T.PVB[:, :], 100.0, A.mult, "PVB", "THR", 9.0, A.add)
-    weave(count(), self_out(1))
-    ts(T.KB2[:, :], T.P7[:, 0:128], 131072.0, A.mult, "P7", "KB2", 131072.0, A.add)
-    ts(T.KC[:, :], T.LT[:, 0:32], T.P32[:, 0:1], A.add, "LT PX", "KC")
-    for j in range(8):
-        ts(T.SK[:, 16 * j:16 * j + 1936:129], T.ONEB[:, 0:16], T.BOK[:, j:j + 1], A.mult, "ONEB BOK", "SK" if j == 0 else "+SK")
+    sizes_out(16, 1040)
+    weave(count(), [lambda: count_rows(range(4, 8)), lambda: count_rows(range(8, 12)), lambda: count_rows(range(12, 16))])
+    cp(T.QT0[:, 0:128], names_of(0, 0, 128), NBK, "QT0")
+    ts(T.XO[:, 1040:2064], T.XS[:, 1040:2064], 32.0, A.add, "XS", "XO_1040")
+    wr["XO"] = wr["XO_16"] + wr["XO_1040"]
 
-    update(0)
+    for part in (EARLY, MID, LATE):
+        unpack(0, "OF0", VOFF, 2, part)
+        unpack(0, "NV0", NAMES, 32, part)
+        unpack(0, "SF0", SIZES, 32, part, 32.0)
+        pivots(silu, "XE", 0, "SF0", "XE", part)
+        pivots(cp, "NE", 0, "NV0", "NE", part)
+    gaps[1, "select"] = [lambda: repeat_names(T.QT0[:, 0:128], "QT0", range(2))]
+    gaps[1, "hits"] = [lambda: pivots(silu, "XO", 0, "SF0", "XO"), lambda: tt(T.PVB[:, :], T.PV[:, :], T.HT0[:, :], A.mult, "PV HT0", "PVB")]
+    gaps[1, "rank"] = [lambda: ts(T.KM[:, :], T.IOH[:, :], T.PH[:, 0:1], A.not_equal, "IOH PH", "KM", 8388608.0, A.mult)]
+    gaps[1, "lanes"] = [lambda: ts(T.KC[:, :], T.IOK[:, :], T.PQ[:, 0:1], A.add, "IOK PQ", "KC")]
     lanes_to_pivots(1)
-    repeat_names(T.QT0[:, 0:128], "QT0")
-    new_names(1)
-    send(1)
-    weave(claims(4), count())
-    send(4)
-    iota(T.JT[:, :], [[1, W]], 0, 0, "JT")
-    unpack(0, "SV", SIZES, 32, ALL)
+    key_places()
+    mm(T.P7[:, 0:128], T.PVB[:, :], T.IDB[:, :], True, True, "PVB IDB", "P7")
+    more = dict(zip(("A0", "A1", "A2", "A3"), count()), MORE=lambda: repeat_names(T.QT0[:, 0:128], "QT0", range(2, 16)),
+                THR=lambda: ts(T.THR[:, :], T.PVB[:, :], 100.0, A.mult, "PVB", "THR", 9.0, A.add),
+                KB2=lambda: ts(T.KB2[:, :], T.P7[:, 0:128], 131072.0, A.mult, "P7", "KB2", 131072.0, A.add))
+    pivots_make(1, "EP Qa Qb OP L16 OV SZ OW Xa Xb E2 Ma Mb OX Ka Kb MORE Ca Cb Na KS Nb KI NM UW NAMES JE A0 TM TL ED A1 DX A2 CLAIMS A3 KB2 THR", more)
+    select_row(range(4))
+    iota(T.JT[:, :], [[1, W]], 16, 0, "JT")
+    select_row(range(4, 16))
+
+    unpack(1, "OF1", VOFF, 2, ALL)
+    unpack(1, "SF1", SIZES, 32, ALL, 32.0)
     pivots(cp, "NB", 0, "NV0", NBK)
-    pivots(cp, "XS", 0, "SV", "XS")
-
-    update(1)
+    pivots(silu, "XE", 1, "SF1", "XE")
+    act(T.VF[:, :], at_places("JF", 1, ALL), "JF " + parts("OF1", ALL), parts("VF", ALL))
+    for part in (EARLY, MID):
+        unpack(4, "NV1", NAMES, 32, part)
+        pivots(cp, "NE", 1, "NV1", "NE", part)
     for r in range(7, -1, -1):
-        won(cp, "NE", 4, r, "NV1")
-        won(silu, "XE", 4, r, "SVF")
-    todo = [lambda: act(T.VF[:, :], at_places("JF", 1, ALL), "JF " + parts("OF1", ALL), parts("VF", ALL))]
-    todo += [lambda r=r: won(silu, "JF", 4, r, "VF") for r in range(7, -1, -1)]
-    gaps[2, "select"], gaps[2, "roots"] = todo[:6], todo[6:]
+        j = slot(rank, r)
+        cp(TAB["NE"].indirect(msg(4, j, EOFF, 2)), msg(4, j, NAMES, 32), key(4, r), "NE")
+        won(silu, "XE", 4, r, "SF1")
+        if r == 1:
+            unpack(4, "NV1", NAMES, 32, LATE)
+    pivots(cp, "NE", 1, "NV1", "NE", LATE)
+
+    def j_list(ks):
+        for k in ks:
+            mm(T.P7[:, 0:128], T.SAF[:, 128 * k:128 * k + 128], T.JF[:, 16 + k:2064:16], k == 0, k == 15, "SAF%d JF" % k, "P7")
+    gaps[2, "select"] = [lambda r=r: won(silu, "JF", 4, r, "VF") for r in range(7, -1, -1)]
+    gaps[2, "cover"] = [key_places]
     lanes_to_pivots(2)
-    select_row(range(8, 16))
-    new_names(2)
-    send(2)
-    for k in range(16):
-        mm(T.P5[:, 0:128], T.SAF[:, 128 * k:128 * k + 128], T.JF[:, 16 + k:2064:16], k == 0, k == 15, "SAF%d JF" % k, "P5")
-    weave(claims(3))
-    send(3)
+    j_list(range(2))
+    pivots_make(2, "EP Qa Qb OP L16 OV SZ OW Xa Xb E2 Ma Mb OX Ka Kb MORE Ca Cb Na KS Nb KI NM UW NAMES JE TM TL ED DX CLAIMS",
+                dict(MORE=lambda: j_list(range(2, 16))))
 
-    unpack(1, "SV", SIZES, 32, ALL)
-    pivots(cp, "NB", 1, "NV1", NBK)
-    pivots(cp, "XS", 1, "SV", "XS")
     unpack(5, "OF5", VOFF, 2, ALL)
-    unpack(5, "SV", SIZES, 32, ALL)
+    unpack(5, "SF5", SIZES, 32, ALL, 32.0)
+    pivots(cp, "NB", 1, "NV1", NBK)
+    pivots(silu, "XO", 1, "SF1", "XO")
+    pivots(silu, "XO", 5, "SF5", "XO")
+    for k in ("XSa", "XSb"):
+        wr[k], rd[k] = wr["XS"], rd["XS"]
+    act(T.XS[:, 912:2064], T.XO[:, 912:2064], "XO", "XSb", func=ActivationFunctionType.Relu, bias=-32.0002)
+    ts(T.XS[:, 16:912], T.XO[:, 16:912], -32.0002, A.add, "XO", "XSa", 0.0, A.max)
+    dma("s", T.yx[:, :], T.XS[:, 16:2064], "o_x", "XSa XSb", "")
     act(T.VJ[:, :], at_places("JT", 5, ALL), "JT " + parts("OF5", ALL), parts("VJ", ALL))
-    pivots(cp, "XS", 5, "SV", "XS")
-    dma("s", T.yx[:, :], T.XS[:, 16:2064], "o_x", "XS", "")
-    for part in (EARLY, LATE):
-        pivots(cp, "NB", 5, "LD2", NBK, part, keys(2, part))
-    dma("s", T.yn[:, :], T.NB[:, 16:2064], "o_n", NBK, "")
-    ts(T.JL[:, :], T.P5[:, 0:128], -15.75, A.add, "P5", "JL")
-    for r in range(7, -1, -1):
-        won(cp, "JT", 3, r, "VJ")
-    act(T.YJ[:, 0:1024], T.JT[:, 0:2064].indirect(T.JL[:, 0:64]), "JT JL", "YJ0", func=IDN, bias=-16.0)
-    ts(T.YJ[:, 1024:2048], T.JT[:, 0:2064].indirect(T.JL[:, 64:128]), -16.0, A.add, "JT JL", "YJ1")
+    unpack(3, "NV0", NAMES, 32, (0, 4))
+    pivots(cp, "NB", 5, "NV0", NBK, (0, 4))
+
+    def last_names(j):
+        cp(at_places("NB", 5, (j, j + 1)), msg(3, j, NAMES, 32), parts("OF5", (j, j + 1)) + " " + keys(3, (j, j + 1)), NBK)
+        if j == 7:
+            dma("s", T.yn[:, :], T.NB[:, 16:2064], "o_n", NBK, "")
+    weave([lambda r=r: won(cp, "JT", 3, r, "VJ") for r in range(7, -1, -1)],
+          [lambda j=j: last_names(j) for j in range(*LATE)] + [lambda: None] * 2 + [lambda: ts(T.JL[:, :], T.P7[:, 0:128], -15.75, A.add, "P7", "JL")])
+    act(T.YJ[:, 0:1024], T.JT[:, 0:2064].indirect(T.JL[:, 0:64]), "JT JL", "YJ0", func=IDN, bias=-32.0)
+    ts(T.YJ[:, 1024:2048], T.JT[:, 0:2064].indirect(T.JL[:, 64:128]), -32.0, A.add, "JT JL", "YJ1")
     dma("a", T.yj[:, 0:1024], T.YJ[0:128:16, 0:1024], "o_j0", "YJ0", "")
     dma("s", T.yj[:, 1024:2048], T.YJ[0:128:16, 1024:2048], "o_j1", "YJ1", "")
 
@@ -518,5 +551,5 @@ def rank_program(g, core, T, topo):
         g.wait_ge(T.sem["e" + q], cnt[q])
     for s in ("d_x", "d_n0", "d_n1", "d_n2", "d_l", "o_n", "o_x", "o_j0", "o_j1"):
         g.wait_ge(T.sem[s], 16)
-    for m in range(6):
+    for m in nloc:
         g.wait_ge(T.sem["l%d" % m], nloc[m])

@@ -6,23 +6,36 @@ BIG = 12582912.0
 F, B, I, U = "float32", "bfloat16", "int32", "uint16"
 SCRATCH = {}
 for _names, _w, _d in (
-        ("NB JT NE XE JF XO", W, F), ("XS", W, B), ("SA EQ XG XV MX RSM", 2048, B), ("SAF QR YJ", 2048, F), ("SK", 512, B), ("BOK", 128, B), ("KC KM KS RSK IOK IOH", 128, F), ("HT0", 128, B), ("OV", 32, F),
-        ("Q2 CC NS", 512, F), ("E2", 520, F), ("X2 MM", 512, B), ("RSTB", 256, B), ("ONEB IDB I4 BO TRI HR HT PV PVB KB1 KB2", 128, B), ("CMP", 256, B),
-        ("IDF TQ UN THR", 128, F), ("SB SF0 SF1 SF5 VF VJ", 256, F), ("WTS PR", 2, B),
-        ("PI PA PB LIMI AI AM", 1, I), ("PF PH PQ LIMA LIMH", 1, F), ("COL", 8, F), ("CA CB CM CV IO16", 16, F),
-        ("LT VT0 VT1 QT0 QT1 OWN SZ", 136, F), ("OQ0 OQ1 UL JL", 128, U),
-        ("IO32 D2 OP NM TM TL RST", 32, F), ("IO66 RL ED DX", 66, F), ("LW UW", 2, U), ("EP L16", 32, U), ("KI", 2, F), ("JE", 32, I),
-        ("OF0 OF1 OF5", 16, U), ("NV0 NV1", 256, U)):
+        ("NB JT NE XE JF XO", W, F), ("XS", W, B), ("SA EQ XG XV MX RSM", 2048, B), ("QR", 2048, F),
+        ("Q2 NS", 512, F), ("MM", 512, B), ("RSTB", 272, B), ("CMP CKR", 256, B), ("RST", 32, B), ("ONEB IDB NID M64 BO TRI HR HT HT0 PV PVB KB1 KB2 HI0 HI1", 128, B),
+        ("IDF UN THR", 128, F), ("SB SF0 SF1 VF VJ KS RSK JM JG", 256, F), ("SAF", 2048, F), ("D16", 32, F), ("WT PR", 2, B), ("B16 WK", 16, B),
+        ("PI PA LIMI AI AM", 1, I), ("PF LIMA LIMH", 1, F), ("COL", 8, F), ("CA CB CM CV IO16 KR", 16, F),
+        ("LT VT0 VT1 VS0 VS1 QT0 QT1 OWN OWS SZ", 136, F), ("TQ0 TQ1", 128, F), ("OQ0 OQ1 UL", 128, U),
+        ("OP N1 NM TM2 TL2 GM TM TL", 32, F), ("IO66 RL ED DX", 66, F), ("LW UW", 2, U), ("EP L16", 32, U), ("JE", 32, I),
+        ("OF0 OF1 OF5 JL", 16, U), ("NV0 NV1 SV5", 256, U)):
     for _n in _names.split():
         SCRATCH[_n] = ("sbuf", [128, _w], _d)
-for _b in (0, 1, 3, 4, 5):
-    SCRATCH["LD%d" % _b] = ("sbuf", [128, 8, 72], U)
+VOFF, SIZES, NAMES = 0, 2, 34
+SPAN = {0: (0, 66), 1: (0, 34), 4: (34, 68), 5: (0, 34), 3: (34, 68)}
+CLAIM = {1: (4, 66), 2: (3, 66)}
+FLAT = ()
+N0 = 0
+for _b in SPAN:
+    SCRATCH["LD%d" % _b] = ("sbuf", [128, 256] if _b in FLAT else [128, 8, 72 if _b < 6 else 8], U)
 for _b in range(8):
     SCRATCH["P%d" % _b] = ("psum", [128, 512], F)
-SEMAPHORES = ["ev", "et", "ea", "eg", "d_x", "d_n0", "d_n1", "d_n2", "d_l", "o_n", "o_x", "o_j0", "o_j1"]
-SEMAPHORES += ["a%d_%d" % (m, r) for m in (0, 1, 3, 4, 5) for r in range(8)] + ["l%d" % m for m in (0, 1, 3, 4, 5)]
-VOFF, SIZES, NAMES, EOFF = 0, 2, 34, 66
-SPAN = {0: (0, 66), 1: (0, 34), 4: (34, 68), 5: (0, 34), 3: (34, 68)}
+SEMAPHORES = ["ev", "et", "ea", "eg", "d_x", "d_n0", "d_n1", "d_n2", "d_l", "o_n", "o_x", "o_j"]
+SEMAPHORES += ["a%d_%d" % (m, r) for m in SPAN for r in range(8)] + ["l%d" % m for m in SPAN]
+CUTS = {1: (52, 98), 2: (52, 98)}
+SPLIT = {1: 118, 2: 116}
+SUMS = (0, 5, 10, 16, 16)
+ORDER = {1: "KR EP Qa Qb OP WK PAY PL PAD SZ 1 L16 QR1 QR2 QR3 TM Ma TL Mb UW JE Na ED Nb DX N1 CLAIMS NM NAMES 4",
+         2: "KR EP Qa Qb OP WK PAY PL PAD SZ 5 L16 TM Ma TL Mb JP UW JE Na TM2 Nb TL2 N1 ED NM DX NAMES CLAIMS 3"}
+GAPS = {(1, "sizes0"): "MX0 NB0a", (1, "sizes1"): "MX1", (1, "select"): "S0 OWN NB0b XO0", (1, "hits"): "S1 OS1 QR0", (1, "rank"): "S2 UN1", (1, "lanes"): "KS",
+        (2, "sent"): "A0 NU1 A1 OF1 A2 SF1 A3 XE VF XO1", (2, "wait"): "",
+        (2, "sizes0"): "MX0 NB1a", (2, "sizes1"): "MX1", (2, "select"): "S0 OWN NB1b J7 J6 J5 J4", (2, "hits"): "S1 OS2 J3 J2 J1 J0", (2, "rank"): "S2 UN2",
+        (2, "lanes"): "KS", (3, "sent"): "NU2"}
+END = "Na Nu T7 Nb T6 T5 T4 JL T3 T2 T1 T0"
 
 
 def rank_program(g, core, T, topo):
@@ -30,7 +43,8 @@ def rank_program(g, core, T, topo):
     if rank is None:
         return
     A = AluOpType
-    IDN = ActivationFunctionType.Identity
+    FN = ActivationFunctionType
+    IDN = FN.Identity
     Q = {"v": g.vector, "t": g.tensor, "a": g.scalar, "g": g, "s": g.sync}
     cnt, wr, rd, nloc = {}, {}, {}, {}
     known = {q: {} for q in Q}
@@ -106,11 +120,11 @@ def rank_program(g, core, T, topo):
     def mm(out, l, r, start, stop, R, Wk):
         op("t", lambda: g.tensor.matmul(out=out, lhsT=l, rhs=r, start=start, stop=stop), R, Wk)
 
-    def act(out, in_, R, Wk, func=ActivationFunctionType.Copy, bias=0.0, scale=1.0):
+    def act(out, in_, R, Wk, func=FN.Copy, bias=0.0, scale=1.0):
         op("a", lambda: g.scalar.activation(out=out, in_=in_, func=func, bias=bias, scale=scale), R, Wk)
 
     def silu(out, in_, R, Wk):
-        op("a", lambda: g.scalar.activation(out=out, in_=in_, func=ActivationFunctionType.Silu), R, Wk)
+        op("a", lambda: g.scalar.activation(out=out, in_=in_, func=FN.Silu), R, Wk)
 
     def weave(*chains):
         for j in range(max(len(c) for c in chains)):
@@ -125,11 +139,11 @@ def rank_program(g, core, T, topo):
         op("g", lambda: g.affine_select(out, in_, pat, o, fl, base, cm), R, Wk)
 
     cls = [rank, 8 + rank, rank]
-    VTs = ["VT0", "VT1", "VT0"]
-    BLOCKS = ((0, 64), (64, 96), (96, 128))
+    BLOCKS = ((0, 64), (64, 104), (104, 128))
     NBK = "NB0 NB1 NB2"
-    TAB = {n: T[n][:, 0:W] for n in ("NB", "XO", "NE", "XE", "JT", "JF")}
-    NEW, XEW = T.NE[:, 0:2080], T.XE[:, 0:2080]
+    TAB = {n: T[n][:, 0:W] for n in ("NB", "XO", "XS", "NE", "XE", "JT", "JF")}
+    BY_NAME = {n: T[n][:, 16:W] for n in ("NE", "XE", "JT", "JF")}
+    NEW, XEW, JFW = T.NE[:, 0:2080], T.XE[:, 0:2080], T.JF[:, 16:2080]
 
     dma("a", T.XS[:, 16:2064], T.xs[:, :], "d_x", "", "XS")
     for j, (a, b) in enumerate(BLOCKS):
@@ -139,31 +153,29 @@ def rank_program(g, core, T, topo):
     fill(T.ONEB[:, :], 1.0, "ONEB")
     fill(T.RSM[:, :], 256.0, "RSM")
     for a, b, src in ((0, 128, "ONEB"), (128, 2080, "RSM")):
-        act(T.XE[:, a:b], T[src][:, 0:b - a], src, "+XE", func=ActivationFunctionType.Silu, bias=30.0, scale=0.0)
-    fill(T.WTS[:, 0:1], 1.0, "+WTS")
-    fill(T.WTS[:, 1:2], 16.0, "+WTS")
+        act(T.XE[:, a:b], T[src][:, 0:b - a], src, "+XE", func=FN.Silu, bias=30.0, scale=0.0)
     fill(T.XS[:, 0:16], 0.0, "+XSp")
     fill(T.XS[:, 2064:W], 0.0, "+XSp")
     op("g", lambda: g.iota(T.PI[:, :], [[0, 1]], 0, 1), "", "PI")
     asel(T.IDB[:, :], T.ONEB[:, :], [[-1, 128]], A.is_equal, 0.0, 0, 1, "ONEB", "IDB")
     iota(T.IO16[:, :], [[1, 16]], 0, 0, "IO16")
-    iota(T.IO32[:, :], [[0, 2], [1, 16]], 0, 0, "IO32")
     iota(T.IO66[:, :], [[-16, 2], [1, 33]], -1, 0, "IO66")
     asel(T.BO[:, :], T.ONEB[:, :], [[-16, 8], [0, 16]], A.is_ge, 0.0, 0, 1, "ONEB", "BO")
     asel(T.BO[:, :], T.BO[:, :], [[16, 8], [0, 16]], A.is_ge, 0.0, 15, -1, "BO", "BO")
     asel(T.TRI[:, :], T.ONEB[:, :], [[1, 128]], A.is_ge, 0.0, 0, -1, "ONEB", "TRI")
-    asel(T.WTS[:, 1:2], T.WTS[:, 1:2], [[0, 1]], A.not_equal, 384.0, -127, 1, "WTS", "WTS")
+    asel(T.TRI[:, :], T.TRI[:, :], [[-1, 128]], A.not_equal, 129.0, 0, 1, "TRI", "TRI")
+    iota(T.WT[:, 0:1], [[0, 1]], -128, 1, "+WT")
+    iota(T.WT[:, 1:2], [[0, 1]], -4096, 16, "+WT")
     iota(T.VT0[:, :], [[16, 136]], cls[0], 0, "VT0")
-    iota(T.SB[:, :], [[-16, 2], [0, 8], [-1, 16]], 31, 0, "SB")
+    iota(T.SB[:, :], [[-16, 2], [0, 8], [-1, 16]], 160, 0, "SB")
     iota(T.NE[:, 0:1440], [[0, 1440]], 2050, 0, "NEa")
     for n in ("QT0", "QT1"):
         fill(T[n][:, 128:136], 2048.0, n + "p")
-    fill(T.OWN[:, 128:136], 0.0, "OWNp")
+    for n in ("OWN", "OWS"):
+        fill(T[n][:, 128:136], 0.0, n + "p")
     fill(T.SZ[:, 128:136], 255.0, "SZp")
-    fill(T.E2[:, 512:520], 4096.0, "E2p")
-    fill(T.ED[:, :], 0.0, "ED")
     fill(T.KB1[:, :], 131072.0, "KB1")
-    resets = (("RST", 32, 16, 1.0, 0.0), ("RSK", 128, 64, -8388608.0, 512.0), ("RSTB", 256, 16, 0.0, 8192.0))
+    resets = (("RST", 32, 16, 1.0, 0.0), ("RSK", 256, 16, 16777216.0, 63.0), ("RSTB", 272, 16, 0.0, 2.0))
     for n, w, step, c, c0 in resets:
         fill(T[n][:, :], c, n)
     for n, w, step, c, c0 in resets:
@@ -171,24 +183,21 @@ def rank_program(g, core, T, topo):
     ts(T.PA[:, :], T.PI[:, :], 15, A.bitwise_and, "PI", "PA")
     cp(T.IDF[:, :], T.IDB[:, :], "IDB", "IDF")
     cp(T.PF[:, :], T.PA[:, :], "PA", "PF")
-    ts(T.I4[:, :], T.IDB[:, :], 4096.0, A.mult, "IDB", "I4")
-    for j, b in enumerate((2080 + 32 * rank, 2096 + 32 * rank, 2336, 2352)):
+    ts(T.NID[:, :], T.IDB[:, :], -1.0, A.mult, "IDB", "NID")
+    for j, b in enumerate((2080 + 32 * rank, 2096 + 32 * rank, 2320, 2336)):
         ts(T.COL[:, j:j + 1], T.PF[:, :], float(b), A.add, "PF", "+COL")
     TRV, TRE = [T.COL[:, 0:1], T.COL[:, 1:2]], [T.COL[:, 2:3], T.COL[:, 3:4]]
     ts(T.CB[:, :], T.IO16[:, :], T.PF[:, 0:1], A.is_equal, "IO16 PF", "CB")
     ts(T.CM[:, :], T.IO16[:, :], T.PF[:, 0:1], A.not_equal, "IO16 PF", "CM")
-    ts(T.D2[:, :], T.IO32[:, :], T.PF[:, 0:1], A.is_equal, "IO32 PF", "D2")
     ts(T.RL[:, :], T.IO66[:, :], T.PF[:, 0:1], A.is_gt, "IO66 PF", "RL")
     ts(T.CV[:, :], T.CB[:, :], 2050.0, A.mult, "CB", "CV")
     ts(T.CA[:, :], T.CB[:, :], -126976.0, A.mult, "CB", "CA", -4096.0, A.add)
-    ts(T.BOK[:, :], T.BO[:, :], -1024.0, A.mult, "BO", "BOK")
+    ts(T.M64[:, :], T.IDB[:, :], -64.0, A.mult, "IDB", "M64")
 
     def count_rows(ks):
         for k in ks:
             ts(T.SA[:, 128 * k:128 * k + 128], T.IDB[:, :], T.CA[:, k:k + 1], A.mult, "IDB CA", "+SA")
-    weave([lambda: ts(T.PB[:, :], T.PI[:, :], 3, A.bitwise_and, "PI", "PB"), lambda: cp(T.PH[:, :], T.PB[:, :], "PB", "PH"),
-           lambda: ts(T.PQ[:, :], T.PF[:, :], T.PH[:, 0:1], A.subtract, "PF PH", "PQ", 16.0, A.mult)],
-          [lambda: count_rows(range(2)), lambda: count_rows(range(2, 4))])
+    count_rows(range(4))
 
     def names_of(t, a, b):
         return T.NB[:, 16 + 16 * a + cls[t]:16 + 16 * b:16]
@@ -214,6 +223,8 @@ def rank_program(g, core, T, topo):
     ne = [e for e in topo.engines(core, T.cores[near[0]]) if e not in fe][:2]
 
     def msg(m, j, a, n):
+        if m in FLAT:
+            return T["LD%d" % m][:, 32 * j:32 * j + 32]
         return T["LD%d" % m][:, j, a:a + n]
 
     def mine(m, a, n):
@@ -227,8 +238,9 @@ def rank_program(g, core, T, topo):
             act(T.QR[:, k:2048:16], names, rk + " CM CV", "+QR", func=IDN, bias=T.CV[:, k:k + 1], scale=T.CM[:, k:k + 1])
 
     def gather_sizes(q, lst, a, b):
-        f = cp if q == "v" else act
-        f(T.XV[:, 16 * a:16 * b], T.XS[:, 0:2080].indirect(T[lst[:-2]][:, a:b]), "XS XSp " + lst, "XV%d" % a)
+        if a < b:
+            f = cp if q == "v" else act
+            f(T.XV[:, 16 * a:16 * b], T.XS[:, 0:2080].indirect(T[lst[:-2]][:, a:b]), "XS XSp " + lst, "XV%d" % a)
 
     def degrees(a, b, keys, mx):
         o = T.P2[:, a:b]
@@ -247,7 +259,7 @@ def rank_program(g, core, T, topo):
         lim = "LIMA" if t else "LIMH"
         ts(T.HR[:, :], T.P2[:, 0:128], T[lim][:, 0:1], A.is_le, "P2 " + lim, "HR")
         mm(T.P3[:, 0:128], T.HR[:, :], T.BO[:, :], True, True, "HR BO", "P3")
-        act(T.SZ[:, 0:128], T.P2[:, 0:128], "P2", "SZ", func=ActivationFunctionType.Relu, bias=255.0, scale=-1.0)
+        act(T.SZ[:, 0:128], T.P2[:, 0:128], "P2", "SZ", func=FN.Relu, bias=256.0 if t else 255.0, scale=-1.0)
         gap(t, "hits")
         ht = "HT" if t else "HT0"
         if t < 2:
@@ -257,21 +269,19 @@ def rank_program(g, core, T, topo):
         mm(T.P4[:, 0:128], T.TRI[:, :], T[ht][:, :], True, True, "TRI " + ht, "P4")
         gap(t, "rank")
         for b in range(2):
-            tt(T.CMP[:, 128 * b:128 * b + 128], T.P4[:, 0:128], T.SB[:, 128 * b:128 * b + 128], A.is_le, "P4 SB", "CMP%d" % b)
-            mm(T.P5[:, 2 * b:2 * b + 2], T.CMP[:, 128 * b:128 * b + 128], T.WTS[:, :], True, True, "CMP%d WTS" % b, "P5")
+            tt(T.CMP[:, 128 * b:128 * b + 128], T.P4[:, 0:128], T.SB[:, 128 * b:128 * b + 128], A.is_equal, "P4 SB", "CMP%d" % b)
+            mm(T.P5[:, 2 * b:2 * b + 2], T.CMP[:, 128 * b:128 * b + 128], T.WT[:, :], True, True, "CMP%d WT" % b, "P5")
         gap(t, "lanes")
-        cp(T.LW[:, :], T.P5[:, 0:4:2], "P5", "LW")
-        places(t)
+        ts(T.LW[:, :], T.P5[:, 0:4:2], 128.0, A.add, "P5", "LW")
 
     def new_sizes(t):
         ts(mine(ahead[t], SIZES, 32), at_pivots("SZ"), -1.0, A.mult, "SZ SZp LW", "+M%d" % ahead[t], 255.0, A.add)
-        send(ahead[t])
 
     ahead = [0, 1, 5]
 
     def places(t):
         for b in range(2):
-            ts(mine(ahead[t], VOFF + b, 1), T.P5[:, 2 * b + 1:2 * b + 2], float(cls[t] + 16), A.add, "P5 COL", "+M%d" % ahead[t], TRV[b], A.min)
+            ts(mine(ahead[t], VOFF + b, 1), T.P5[:, 2 * b + 1:2 * b + 2], float(cls[t] + 4112), A.add, "P5 COL", "+M%d" % ahead[t], TRV[b], A.min)
 
     def at_pivots(buf):
         return T[buf][:, 0:136].indirect(T.LW[:, :])
@@ -312,127 +322,137 @@ def rank_program(g, core, T, topo):
     def pivots(f, tab, m, buf, wk, part=ALL, rk=None):
         f(at_places(tab, m, part), T[buf][:, 32 * part[0]:32 * part[1]], parts("OF%d" % m, part) + " " + (rk or parts(buf, part)), wk)
 
-    def won(f, tab, m, r, buf):
-        j = slot(rank, r)
-        f(TAB[tab].indirect(msg(m, j, EOFF, 2)), T[buf][:, 32 * j:32 * j + 32], parts(buf, ALL) + " " + key(m, r), tab)
+    def won(f, tab, t, r, buf):
+        j, (m, a) = slot(rank, r), CLAIM[t]
+        f(BY_NAME[tab].indirect(msg(m, j, a, 2)), T[buf][:, 32 * j:32 * j + 32], parts(buf, ALL) + " " + key(m, r), tab)
 
     def count():
         def total():
-            ts(T.PR[:, :], T.P5[:, 0:4:2], 127.5, A.is_le, "P5", "PR")
+            ts(T.PR[:, :], T.P5[:, 0:4:2], -0.5, A.is_le, "P5", "PR")
             for b in range(2):
                 mm(T.P2[:, 0:1], T.ONEB[:, :], T.PR[:, b:b + 1], b == 0, b == 1, "ONEB PR", "P2")
         return [total, lambda: cp(T.AI[:, :], T.P2[:, 0:1], "P2", "AI"),
                 lambda: ts(T.AM[:, :], T.AI[:, :], 7, A.bitwise_and, "AI", "AM"),
-                lambda: tt(T.LIMA[:, :], T.AM[:, :], T.LIMH[:, :], A.add, "AM LIMH", "LIMA")]
+                lambda: ts(T.LIMA[:, :], T.AM[:, :], T.LIMH[:, 0:1], A.add, "AM LIMH", "LIMA", 1.0, A.add)]
 
-    def own_names(t):
+    def own_names():
         for h in range(2):
-            ts(T.UN[:, 64 * h:64 * h + 64], T["P%d" % h][:, 0:64], 0.0, A.is_lt, "P%d" % h, "UN%d" % h, 2048.0, A.mult)
-        for h in range(2):
-            tt(T.OWN[:, 64 * h:64 * h + 64], T["P%d" % h][:, 0:64], T.UN[:, 64 * h:64 * h + 64], A.max, "P%d UN%d" % (h, h), "+OWN")
-        tt(names_of(t, 0, 128), T.UN[:, :], names_of(t, 0, 128), A.max, "UN0 UN1 " + NBK, NBK)
+            act(T.OWN[:, 64 * h:64 * h + 64], T["P%d" % h][:, 0:64], "P%d" % h, "+OWN", func=FN.Abs, scale=1.0 / 4096)
 
-    def key_places():
-        mm(T.P6[:, 0:128], T.IDF[:, :], T.KC[:, :], True, False, "IDF KC", "P6")
-        mm(T.P6[:, 0:128], T.IDF[:, :], T.KM[:, :], False, False, "IDF KM", "P6")
+    def empty_covered(t):
+        def marks():
+            for h in range(2):
+                ts(T.UN[:, 64 * h:64 * h + 64], T["P%d" % h][:, 0:64], 0.0, A.is_lt, "P%d" % h, "UN%d" % h, 2048.0, A.mult)
+        return [marks, lambda: tt(names_of(t, 0, 128), T.UN[:, :], names_of(t, 0, 128), A.max, "UN0 UN1 " + NBK, NBK)]
+
+    def high_names(t):
+        act(T["HI%d" % t][:, :], T["QT%d" % t][:, 0:128], "QT%d" % t, "HI%d" % t, func=IDN, bias=191.5078125, scale=1.0 / 64)
+
+    def key_start(t):
+        hi, qt = "HI%d" % t, "QT%d" % t
+        mm(T.P6[:, 0:256], T.IDB[:, :], T.CKR[:, :], True, False, "IDB CKR", "P6")
+        mm(T.P6[:, 0:128], T[hi][:, :], T.IDB[:, :], False, False, "IDB " + hi, "P6")
+        mm(T.P6[:, 128:256], T[hi][:, :], T.M64[:, :], False, False, "M64 " + hi, "P6")
+        mm(T.P6[:, 128:256], T[qt][:, 0:128], T.IDF[:, :], False, False, "IDF " + qt, "P6")
+
+    def key_sums(ks):
+        for k in ks:
+            mm(T.P6[:, k:256:16], T.XG[:, k:2048:16], T.B16[:, :], False, k == 15, "XG B16", "P6")
+
+    def at_lists():
+        for b in range(2):
+            mm(T.P7[:, 16 * b:16 * b + 16], T.CMP[:, 128 * b:128 * b + 128], T.WK[:, :], True, True, "CMP%d WK" % b, "P7")
+
+    best = dict(KS=lambda: scan(T.KS[:, :], T.RSK[:, :], T.P6[:, 0:256], 63.0, A.min, A.max, "RSK P6", "KS"),
+                KR=lambda: ts(T.KR[:, :], T.KS[:, 15:256:16], BIG * 128, A.add, "KS", "KR", BIG * 128, A.subtract),
+                WK=lambda: tt(T.WK[:, :], T.KS[:, 15:256:16], T.KR[:, :], A.subtract, "KS KR", "WK"), PAY=at_lists)
+
+    def element_sizes(t):
+        oq = "OQ%d" % (t % 2)
+        act(T.XG[:, :], XEW.indirect(T[oq][:, :]), "XE " + ("OQ1" if t == 1 else "OQ0_0 OQ0_1 OQ0_2"), "XG", func=IDN, bias=-31.0)
 
     def lanes_to_pivots(t):
         qt, oq, kb = "QT%d" % (t % 2), "OQ%d" % (t % 2), "KB%d" % t
         ok = "OQ1" if t == 1 else "OQ0_0 OQ0_1 OQ0_2"
-        act(T.XG[:, :], XEW.indirect(T[oq][:, :]), "XE " + ok, "XG", func=IDN, bias=-32.0)
 
         def cover(a, b, k):
             tt(T.EQ[:, 16 * a:16 * b], NEW.indirect(T[oq][:, a:b]), T.QR[:, 16 * a:16 * b], A.is_equal, "NE QR " + ok, k)
         cover(0, 64, "EQ0")
-        cover(64, 112, "EQ1")
+        cover(64, SPLIT[t], "EQ1")
         for h in range(2):
             o = T["P%d" % h][:, 0:64]
             mm(o, T.IDF[:, :], T[qt][:, 64 * h:64 * h + 64], True, False, "IDF " + qt, "P%d" % h)
             mm(o, T.IDB[:, :], T[kb][:, 64 * h:64 * h + 64], False, False, "IDB " + kb, "P%d" % h)
-        gap(t, "cover")
+        gap(t, "start")
         for h in range(2):
             if h:
                 ts(T.UL[:, 0:64], T.P0[:, 0:64], 16.0, A.add, "P0", "UL_0", 2064.0, A.min)
-                cover(112, 128, "EQ2")
+                cover(SPLIT[t], 128, "EQ2")
             for k in range(16):
                 mm(T["P%d" % h][:, 0:64], T.SA[:, 128 * k:128 * k + 128], T.EQ[:, 1024 * h + k:1024 * h + 1024:16], False, k == 15,
                    "SA " + ("EQ1 EQ2" if h else "EQ0"), "P%d" % h)
-        cuts = (52, 92 + 4 * t)
+            gap(t, "cover%d" % h)
+        cuts = CUTS[t]
         for h, cut in enumerate(cuts):
             if h:
+                gap(t, "list")
                 ts(T.UL[:, 64:128], T.P1[:, 0:64], 16.0, A.add, "P1", "UL_1", 2064.0, A.min)
             gather_sizes("a", "UL_%d" % h, 64 * h, cut)
             gather_sizes("v", "UL_%d" % h, cut, 64 * h + 64)
-            scan(T.MX[:, 1024 * h:1024 * h + 1024], T.RSM[:, 0:1024], T.XG[:, 1024 * h:1024 * h + 1024], 0.0, A.min, A.max, "RSM XG", "MX%d" % h)
-        own_names(t)
+            gap(t, "sizes%d" % h)
         for h, cut in enumerate(cuts):
-            degrees(64 * h, 64 * h + 64, "XV%d XV%d" % (64 * h, cut), True)
+            degrees(64 * h, 64 * h + 64, "XV%d" % (64 * h) + (" XV%d" % cut if cut % 64 else ""), True)
         gap(t, "select")
         select(t)
 
-    def pivots_make(t, order, more):
-        qt, vt, half, pb, m = "QT%d" % (t % 2), VTs[t], [slice(0, 256), slice(256, 512)], ["P3", "P4"], [None, 4, 3][t]
-        col = [T.TL[:, 15:16], T.TL[:, 31:32]]
+    def pivots_make(t, more):
+        qt, vs, tq, half, pb = "QT%d" % (t % 2), "VS%d" % (t % 2), "TQ%d" % (t % 2), [slice(0, 256), slice(256, 512)], ["P3", "P4"]
+        mn, (mc, ca) = [None, 4, 3][t], CLAIM[t]
+        tl = "TL" if t == 1 else "TL2"
+        col = [T[tl][:, 15:16], T[tl][:, 31:32]]
 
         def names(h):
-            act(T.Q2[:, half[h]], NEW.indirect(T.EP[:, 16 * h:16 * h + 16]), "NE EP", "Q2_%d" % h)
+            act(T.Q2[:, half[h]], NEW.indirect(T.EP[:, 16 * h:16 * h + 16]), "NE EP", "Q2_%d" % h, scale=1.0 / 4096)
+            mm(T[pb[h]][:, 0:257], T.IDB[:, :], T.RSTB[:, 0:257], True, False, "IDB RSTB", pb[h])
 
         def itself(h):
-            tt(T.MM[:, half[h]], T[vt][:, 0:136].indirect(T.L16[:, 16 * h:16 * h + 16]), T.Q2[:, half[h]], A.is_equal, "%s L16 Q2_%d" % (vt, h), "MM%d" % h)
-            mm(T[pb[h]][:, 0:256], T.I4[:, :], T.MM[:, half[h]], True, True, "I4 MM%d" % h, pb[h])
-
-        def large(h):
-            tt(T.CC[:, half[h]], T.Q2[:, half[h]], T[pb[h]][:, 0:256], A.add, "Q2_%d %s" % (h, pb[h]), "CC%d" % h)
+            tt(T.MM[:, half[h]], T[vs][:, 0:136].indirect(T.L16[:, 16 * h:16 * h + 16]), T.Q2[:, half[h]], A.is_equal, "%s L16 Q2_%d" % (vs, h), "MM%d" % h)
+            mm(T[pb[h]][:, 1:257], T.IDB[:, :], T.MM[:, half[h]], False, False, "IDB MM%d" % h, pb[h])
+            mm(T[pb[h]][:, 0:256], T.NID[:, :], T.MM[:, half[h]], False, True, "NID MM%d" % h, pb[h])
 
         def least(h):
-            scan(T.NS[:, half[h]], T.RSTB[:, 0:256], T.CC[:, half[h]], 8192.0, A.add, A.min, "RSTB CC%d" % h, "NS%d" % h)
-
-        def elements(h):
-            act(T.X2[:, half[h]], XEW.indirect(T.EP[:, 16 * h:16 * h + 16]), "XE EP", "X2_%d" % h, func=IDN, bias=-31.0)
-
-        def key_sums(h):
-            for a in range(4):
-                mm(T.P6[:, 64 * h:64 * h + 64], T.SK[:, 128 * a:128 * a + 128], T.X2[:, 256 * h + 64 * a:256 * h + 64 * a + 64], False, h == 1 and a == 3,
-                   "SK X2_%d" % h, "P6")
-
-        def place():
-            for b in range(2):
-                ts(T.UW[:, b:b + 1], T.KS[:, 64 * b + 63:64 * b + 64], T.KI[:, b:b + 1], A.subtract, "KS KI", "+UW")
+            scan(T.NS[:, half[h]], T[pb[h]][:, 0:256], T.Q2[:, half[h]], 2.0, A.add, A.min, "%s Q2_%d" % (pb[h], h), "NS%d" % h)
 
         def same():
             for b in range(2):
-                ts(T.ED[:, 33 * b:33 * b + 32], T.JE[:, :], col[b], A.is_equal, "JE TL", "+ED", 4096.0, A.mult)
+                ts(T.ED[:, 33 * b:33 * b + 32], T.JE[:, :], col[b], A.is_equal, "JE " + tl, "+ED", 4096.0, A.mult)
 
         def out():
             for b in range(2):
-                ts(mine(m, EOFF + b, 1), T.DX[:, 33 * b + 32:33 * b + 33], col[b], A.max, "DX COL TL", "+M%d" % m, TRE[b], A.min)
-            send(m)
+                ts(mine(mc, ca + b, 1), T.DX[:, 33 * b + 32:33 * b + 33], col[b], A.max, "DX COL " + tl, "+M%d" % mc, TRE[b], A.min)
 
         step = dict(
             EP=lambda: ts(T.EP[:, :], at_pivots(qt), 16.0, A.add, "%s %sp LW" % (qt, qt), "EP"),
             L16=lambda: cp(T.L16[:, :], at_pivots("LT"), "LT LW", "L16"),
-            SZ=lambda: new_sizes(t), Qa=lambda: names(0), Qb=lambda: names(1), Ma=lambda: itself(0), Mb=lambda: itself(1),
-            Ca=lambda: large(0), Cb=lambda: large(1), Na=lambda: least(0), Nb=lambda: least(1),
-            OP=lambda: cp(T.OP[:, :], at_pivots("OWN"), "OWN OWNp LW", "OP"),
-            OV=lambda: tt(T.OV[:, :], at_pivots(vt), T.OP[:, :], A.is_equal, vt + " LW OP", "OV"),
-            OW=lambda: ts(T.OV[:, :], T.OV[:, :], 4096.0, A.mult, "OV", "OV"),
-            OX=lambda: tt(T.OP[:, :], T.OP[:, :], T.OV[:, :], A.max, "OP OV", "OP"),
-            NM=lambda: tt(T.NM[:, :], T.NS[:, 15:512:16], T.OP[:, :], A.min, "NS0 NS1 OP", "NM"),
-            NAMES=lambda: ts(mine(m, NAMES, 32), T.NM[:, :], 2048.0, A.min, "NM", "+M%d" % m),
-            Xa=lambda: elements(0), Xb=lambda: elements(1), Ka=lambda: key_sums(0), Kb=lambda: key_sums(1),
-            E2=lambda: act(T.E2[:, 0:512], T.JF[:, 0:2080].indirect(T.EP[:, :]), "JF EP", "E2", func=IDN, bias=-16.0),
-            KS=lambda: scan(T.KS[:, :], T.RSK[:, :], T.P6[:, 0:128], 0.0, A.max, A.min, "RSK P6", "KS"),
-            KI=lambda: ts(T.KI[:, :], T.KS[:, 63:128:64], BIG * 1024, A.add, "KS", "KI", BIG * 1024, A.subtract), UW=place,
-            JE=lambda: cp(T.JE[:, :], T.E2[:, :].indirect(T.UW[:, :]), "E2 E2p UW", "JE"),
-            TM=lambda: tt(T.TM[:, :], T.JE[:, :], T.D2[:, :], A.mult, "JE D2", "TM"),
-            TL=lambda: scan(T.TL[:, :], T.RST[:, :], T.TM[:, :], 0.0, A.mult, A.add, "RST TM", "TL"),
-            ED=same, DX=lambda: scan(T.DX[:, :], T.RL[:, :], T.ED[:, :], 0.0, A.mult, A.max, "RL ED", "DX"), CLAIMS=out, **more)
-        for name in order.split():
-            step[name]()
-
-    def select_row(ks):
-        for k in ks:
-            asel(T.SAF[:, 128 * k:128 * k + 128], T.IDF[:, :], [[0, 8], [1, 16]], A.is_equal, 0.0, -k, 0, "IDF", "SAF%d" % k)
+            PL=lambda: places(t), SZ=lambda: new_sizes(t), Qa=lambda: names(0), Qb=lambda: names(1), Ma=lambda: itself(0), Mb=lambda: itself(1),
+            Na=lambda: least(0), Nb=lambda: least(1),
+            OP=lambda: act(T.OP[:, :], at_pivots("OWS"), "OWS OWSp LW", "OP", func=IDN, bias=1.0),
+            N1=lambda: tt(T.N1[:, :], T.NS[:, 15:512:16], T.MM[:, 15:512:16], A.add, "NS0 NS1 MM0 MM1", "N1"),
+            NM=lambda: tt(T.NM[:, :], T.N1[:, :], T.OP[:, :], A.min, "N1 OP", "NM"),
+            NAMES=lambda: ts(mine(mn, NAMES, 32), T.NM[:, :], 4096.0, A.mult, "NM", "+M%d" % mn, 2048.0, A.min),
+            TM=lambda: tt(T.TM[:, :], T.P7[:, 0:32], T.GM[:, :], A.mult, "P7 GM", "TM"),
+            TL=lambda: scan(T.TL[:, :], T.RST[:, 0:32], T.TM[:, :], 0.0, A.mult, A.add, "RST TM", "TL"),
+            UW=lambda: ts(T.UW[:, :], T.TL[:, 15:32:16], 2048.0, A.min, "TL", "UW"),
+            JE=lambda: ts(T.JE[:, :], JFW.indirect(T.UW[:, :]), -32.0, A.add, "JF UW", "JE"),
+            TM2=lambda: tt(T.TM2[:, :], T.JE[:, :], T.D16[:, 0:32], A.mult, "JE D16", "TM2"),
+            TL2=lambda: scan(T.TL2[:, :], T.RST[:, 0:32], T.TM2[:, :], 0.0, A.mult, A.add, "RST TM2", "TL2"),
+            PAD=lambda: act(T.ED[:, 32:66:33], T.P5[:, 0:4:2], "P5", "EDp", func=FN.Relu, bias=4096.0, scale=4096.0),
+            ED=same, DX=lambda: scan(T.DX[:, :], T.RL[:, :], T.ED[:, :], 0.0, A.mult, A.max, "RL ED EDp", "DX"), CLAIMS=out, **more)
+        for name in ORDER[t].split():
+            if name.isdigit():
+                send(int(name))
+            else:
+                step[name]()
 
     def sizes_out(a, b):
         act(T.XO[:, a:b], T.XS[:, a:b], "XS", "XO_%d" % a, func=IDN, bias=32.0)
@@ -450,106 +470,149 @@ def rank_program(g, core, T, topo):
             ts(T.LIMH[:, :], T.LIMI[:, :], 0.5, A.add, "LIMI", "LIMH")
     act(T.UN[:, :], names_of(0, 0, 128), NBK, "UN0 UN1", func=IDN, bias=2048.0, scale=-1.0)
     repeat_names(names_of(1, 0, 128), NBK, range(3))
-    tt(T.TQ[:, :], names_of(0, 0, 128), T.VT0[:, 0:128], A.not_equal, NBK + " VT0", "TQ")
-    tt(T.OWN[:, 0:128], T.TQ[:, :], T.UN[:, :], A.mult, "TQ UN0 UN1", "OWN")
-    gaps[0, "rank"] = [lambda: fill(T.RSM[:, 0:2048:16], 0.0, "RSM")]
+    tt(T.TQ0[:, 0:128], names_of(0, 0, 128), T.VT0[:, 0:128], A.not_equal, NBK + " VT0", "TQ0")
+    tt(T.OWN[:, 0:128], T.TQ0[:, 0:128], T.UN[:, :], A.mult, "TQ0 UN0 UN1", "OWN")
+    gaps[0, "rank"] = [lambda: fill(T.RSM[:, 0:2048:16], 1.0, "RSM")]
     gaps[0, "hits"] = [lambda: ts(T.OQ1[:, :], names_of(1, 0, 128), 16.0, A.add, NBK, "OQ1"),
                        lambda: act(T.QT1[:, 0:128], names_of(1, 0, 128), NBK, "QT1"), lambda: repeat_names(names_of(1, 0, 128), NBK, range(3, 16))]
-    gaps[0, "lanes"] = [lambda: ts(T.PV[:, :], T.P4[:, 0:128], 32.0, A.is_le, "P4", "PV")]
+    gaps[0, "lanes"] = [lambda: ts(T.PV[:, :], T.P4[:, 0:128], 160.0, A.is_le, "P4", "PV")]
     select(0)
-    ts(mine(0, NAMES, 32), at_pivots("OWN"), -1.0, A.mult, "OWN OWNp LW", "+M0", 2048.0, A.add)
+    places(0)
     new_sizes(0)
+    if N0:
+        send(0)
+    ts(mine(N0, NAMES, 32), at_pivots("OWN"), -1.0, A.mult, "OWN OWNp LW", "+M%d" % N0, 2048.0, A.add)
+    send(N0)
 
     iota(T.NE[:, 1440:2080], [[0, 640]], 2050, 0, "NEb")
-    iota(T.LT[:, :], [[1, 136]], 0, 0, "LT")
+    iota(T.CKR[:, :], [[12480, 2], [0, 8], [-128, 16]], 1728, 0, "CKR")
     iota(T.VT1[:, :], [[16, 136]], cls[1], 0, "VT1")
-    iota(T.IOK[:, :], [[256, 2], [1, 64]], 0, 0, "IOK")
-    iota(T.IOH[:, :], [[0, 2], [1, 4], [0, 16]], 0, 0, "IOH")
-    for a in range(4):
-        asel(T.SK[:, 128 * a:128 * a + 128], T.BOK[:, :], [[0, 8], [1, 4], [0, 4]], A.is_equal, 0.0, -a, 0, "BOK", "+SK")
+    iota(T.LT[:, :], [[1, 136]], 0, 0, "LT")
     iota(T.JF[:, :], [[1, W]], 16, 0, "JF")
+    iota(T.JF[:, 2064:2065], [[0, 1]], 4128, 0, "JF")
+
+    def select_row(ks):
+        for k in ks:
+            asel(T.SAF[:, 128 * k:128 * k + 128], T.IDF[:, :], [[0, 8], [1, 16]], A.is_equal, 0.0, -k, 0, "IDF", "+SAF")
+    select_row(range(8))
     wr["NE"] = wr["NEa"] + wr["NEb"]
+    high_names(1)
     sizes_out(16, 1040)
     weave(count(), [lambda: count_rows(range(4, 8)), lambda: count_rows(range(8, 12)), lambda: count_rows(range(12, 16))])
+    for h in range(2):
+        ts(T.B16[:, 8 * h:8 * h + 8], T.BO[:, 0:128:16], 2048.0, A.mult, "BO", "+B16")
     cp(T.QT0[:, 0:128], names_of(0, 0, 128), NBK, "QT0")
+    key_start(1)
     ts(T.XO[:, 1040:2064], T.XS[:, 1040:2064], 32.0, A.add, "XS", "XO_1040")
     wr["XO"] = wr["XO_16"] + wr["XO_1040"]
+    for j, c in enumerate((64.0, 1.0, 64.0, 1.0)):
+        act(T.GM[:, 8 * j:8 * j + 8], T.BO[:, 0:128:16], "BO", "+GM", scale=c)
+    tt(T.PVB[:, :], T.PV[:, :], T.HT0[:, :], A.mult, "PV HT0", "PVB")
+    mm(T.P7[:, 0:128], T.PVB[:, :], T.IDB[:, :], True, True, "PVB IDB", "P7")
+    tt(T.TQ1[:, 0:128], names_of(1, 0, 128), T.VT1[:, 0:128], A.not_equal, NBK + " VT1", "TQ1")
+    act(T.THR[:, :], T.PVB[:, :], "PVB", "THR", func=IDN, bias=9.0, scale=100.0)
+    act(T.KB2[:, :], T.P7[:, 0:128], "P7", "KB2", func=IDN, bias=131072.0, scale=131072.0)
+    for h in range(2):
+        act(T.D16[:, 16 * h:16 * h + 16], T.CB[:, :], "CB", "+D16")
+    for t in (1, 0):
+        act(T["VS%d" % t][:, :], T["VT%d" % t][:, :], "VT%d" % t, "VS%d" % t, scale=1.0 / 4096)
+    high_names(0)
+
+    def landed(tab, wk, mo, mn, buf, part):
+        unpack(mn, buf, NAMES, 32, part)
+        pivots(cp, tab, mo, buf, wk, part)
 
     for part in (EARLY, MID, LATE):
         unpack(0, "OF0", VOFF, 2, part)
-        unpack(0, "NV0", NAMES, 32, part)
         unpack(0, "SF0", SIZES, 32, part, 32.0)
         pivots(silu, "XE", 0, "SF0", "XE", part)
-        pivots(cp, "NE", 0, "NV0", "NE", part)
-    gaps[1, "select"] = [lambda: repeat_names(T.QT0[:, 0:128], "QT0", range(2))]
-    gaps[1, "hits"] = [lambda: pivots(silu, "XO", 0, "SF0", "XO"), lambda: tt(T.PVB[:, :], T.PV[:, :], T.HT0[:, :], A.mult, "PV HT0", "PVB")]
-    gaps[1, "rank"] = [lambda: ts(T.KM[:, :], T.IOH[:, :], T.PH[:, 0:1], A.not_equal, "IOH PH", "KM", 8388608.0, A.mult)]
-    gaps[1, "lanes"] = [lambda: ts(T.KC[:, :], T.IOK[:, :], T.PQ[:, 0:1], A.add, "IOK PQ", "KC")]
-    lanes_to_pivots(1)
-    key_places()
-    mm(T.P7[:, 0:128], T.PVB[:, :], T.IDB[:, :], True, True, "PVB IDB", "P7")
-    more = dict(zip(("A0", "A1", "A2", "A3"), count()), MORE=lambda: repeat_names(T.QT0[:, 0:128], "QT0", range(2, 16)),
-                THR=lambda: ts(T.THR[:, :], T.PVB[:, :], 100.0, A.mult, "PVB", "THR", 9.0, A.add),
-                KB2=lambda: ts(T.KB2[:, :], T.P7[:, 0:128], 131072.0, A.mult, "P7", "KB2", 131072.0, A.add))
-    pivots_make(1, "EP Qa Qb OP L16 OV SZ OW Xa Xb E2 Ma Mb OX Ka Kb MORE Ca Cb Na KS Nb KI NM UW NAMES JE A0 TM TL ED A1 DX A2 CLAIMS A3 KB2 THR", more)
-    select_row(range(4))
-    iota(T.JT[:, :], [[1, W]], 16, 0, "JT")
-    select_row(range(4, 16))
+        landed("NE", "NE", 0, 0, "NV0", part)
+    element_sizes(1)
 
-    unpack(1, "OF1", VOFF, 2, ALL)
-    unpack(1, "SF1", SIZES, 32, ALL, 32.0)
-    pivots(cp, "NB", 0, "NV0", NBK)
-    pivots(silu, "XE", 1, "SF1", "XE")
-    act(T.VF[:, :], at_places("JF", 1, ALL), "JF " + parts("OF1", ALL), parts("VF", ALL))
+    def names_0(part):
+        pivots(cp, "NB", 0, "NV0", NBK, part)
+    of0 = parts("OF0", ALL)
+
+    def j_list():
+        act(T.JM[:, :], at_places("JF", 0, ALL), "JF " + of0, "JM")
+        for k in range(16):
+            mm(T.P0[:, 0:16], T.SAF[:, 128 * k:128 * k + 128], T.JM[:, k:256:16], k == 0, k == 15, "SAF JM", "P0")
+
+    def names_1(tab, wk, part):
+        pivots(cp, tab, 1, "NV1", wk, part)
+    job = dict(best, OWN=own_names,
+               NB0=lambda: names_0(ALL), NB1=lambda: names_1("NB", NBK, ALL),
+               NB0a=lambda: names_0((0, 2)), NB0b=lambda: names_0((2, 8)),
+               NB1a=lambda: names_1("NB", NBK, (0, 2)), NB1b=lambda: names_1("NB", NBK, (2, 8)),
+               XO0=lambda: pivots(silu, "XO", 0, "SF0", "XO"), XO1=lambda: pivots(silu, "XO", 1, "SF1", "XO"),
+               OF1=lambda: unpack(1, "OF1", VOFF, 2, ALL), SF1=lambda: unpack(1, "SF1", SIZES, 32, ALL, 32.0),
+               VF=lambda: cp(T.VF[:, :], at_places("JF", 1, ALL), "JF " + parts("OF1", ALL), parts("VF", ALL)),
+               XG=lambda: element_sizes(2), XE=lambda: pivots(silu, "XE", 1, "SF1", "XE"),
+               JP=j_list, JL=lambda: ts(T.JL[:, :], T.P0[:, 0:16], -31.75, A.add, "P0", "JL"))
+    for h in range(2):
+        job["MX%d" % h] = lambda h=h: scan(T.MX[:, 1024 * h:1024 * h + 1024], T.RSM[:, 0:1024], T.XG[:, 1024 * h:1024 * h + 1024], 1.0, A.min, A.max,
+                                           "RSM XG", "MX%d" % h)
+    for j in range(4):
+        job["S%d" % j] = lambda j=j: key_sums(range(SUMS[j], SUMS[j + 1]))
+        job["QR%d" % j] = lambda j=j: repeat_names(T.QT0[:, 0:128], "QT0", range(4 * j, 4 * j + 4))
+    for r in range(8):
+        job["J%d" % r] = lambda r=r: won(silu, "JF", 1, r, "VF")
+    for t in (1, 2):
+        job["UN%d" % t], job["NU%d" % t] = empty_covered(t)
+        job["OS%d" % t] = lambda tq="TQ%d" % (t % 2): tt(T.OWS[:, 0:128], T.OWN[:, 0:128], T[tq][:, :], A.subtract, "OWN " + tq, "OWS")
+    for j, f in enumerate(count()):
+        job["A%d" % j] = f
+    for at, names in GAPS.items():
+        gaps[at] = [job[n] for n in names.split()]
+    lanes_to_pivots(1)
+    pivots_make(1, job)
+    key_start(0)
+    iota(T.JT[:, :], [[1, W]], -16, 0, "JT")
+    select_row(range(8, 16))
+
+    gap(2, "sent")
+    for r in range(7, -1, -1):
+        won(silu, "XE", 1, r, "SF1")
+    element_sizes(2)
+    gap(2, "wait")
     for part in (EARLY, MID):
-        unpack(4, "NV1", NAMES, 32, part)
-        pivots(cp, "NE", 1, "NV1", "NE", part)
+        landed("NE", "NE", 1, 4, "NV1", part)
     for r in range(7, -1, -1):
         j = slot(rank, r)
-        cp(TAB["NE"].indirect(msg(4, j, EOFF, 2)), msg(4, j, NAMES, 32), key(4, r), "NE")
-        won(silu, "XE", 4, r, "SF1")
+        cp(BY_NAME["NE"].indirect(msg(CLAIM[1][0], j, CLAIM[1][1], 2)), msg(4, j, NAMES, 32), key(4, r) + " " + key(CLAIM[1][0], r), "NE")
         if r == 1:
             unpack(4, "NV1", NAMES, 32, LATE)
-    pivots(cp, "NE", 1, "NV1", "NE", LATE)
-
-    def j_list(ks):
-        for k in ks:
-            mm(T.P7[:, 0:128], T.SAF[:, 128 * k:128 * k + 128], T.JF[:, 16 + k:2064:16], k == 0, k == 15, "SAF%d JF" % k, "P7")
-    gaps[2, "select"] = [lambda r=r: won(silu, "JF", 4, r, "VF") for r in range(7, -1, -1)]
-    gaps[2, "cover"] = [key_places]
+    names_1("NE", "NE", LATE)
     lanes_to_pivots(2)
-    j_list(range(2))
-    pivots_make(2, "EP Qa Qb OP L16 OV SZ OW Xa Xb E2 Ma Mb OX Ka Kb MORE Ca Cb Na KS Nb KI NM UW NAMES JE TM TL ED DX CLAIMS",
-                dict(MORE=lambda: j_list(range(2, 16))))
+    pivots_make(2, job)
 
+    act(T.XS[:, 16:2064], T.XO[:, 16:2064], "XO", "XS", func=FN.Relu, bias=-32.0002)
+    gap(3, "sent")
     unpack(5, "OF5", VOFF, 2, ALL)
-    unpack(5, "SF5", SIZES, 32, ALL, 32.0)
-    pivots(cp, "NB", 1, "NV1", NBK)
-    pivots(silu, "XO", 1, "SF1", "XO")
-    pivots(silu, "XO", 5, "SF5", "XO")
-    for k in ("XSa", "XSb"):
-        wr[k], rd[k] = wr["XS"], rd["XS"]
-    act(T.XS[:, 912:2064], T.XO[:, 912:2064], "XO", "XSb", func=ActivationFunctionType.Relu, bias=-32.0002)
-    ts(T.XS[:, 16:912], T.XO[:, 16:912], -32.0002, A.add, "XO", "XSa", 0.0, A.max)
-    dma("s", T.yx[:, :], T.XS[:, 16:2064], "o_x", "XSa XSb", "")
+    unpack(5, "SV5", SIZES, 32, ALL)
     act(T.VJ[:, :], at_places("JT", 5, ALL), "JT " + parts("OF5", ALL), parts("VJ", ALL))
-    unpack(3, "NV0", NAMES, 32, (0, 4))
-    pivots(cp, "NB", 5, "NV0", NBK, (0, 4))
+    pivots(cp, "XS", 5, "SV5", "XS XSp")
+    dma("a", T.yx[:, :], T.XS[:, 16:2064], "o_x", "XS", "")
 
-    def last_names(j):
-        cp(at_places("NB", 5, (j, j + 1)), msg(3, j, NAMES, 32), parts("OF5", (j, j + 1)) + " " + keys(3, (j, j + 1)), NBK)
-        if j == 7:
-            dma("s", T.yn[:, :], T.NB[:, 16:2064], "o_n", NBK, "")
-    weave([lambda r=r: won(cp, "JT", 3, r, "VJ") for r in range(7, -1, -1)],
-          [lambda j=j: last_names(j) for j in range(*LATE)] + [lambda: None] * 2 + [lambda: ts(T.JL[:, :], T.P7[:, 0:128], -15.75, A.add, "P7", "JL")])
-    act(T.YJ[:, 0:1024], T.JT[:, 0:2064].indirect(T.JL[:, 0:64]), "JT JL", "YJ0", func=IDN, bias=-32.0)
-    ts(T.YJ[:, 1024:2048], T.JT[:, 0:2064].indirect(T.JL[:, 64:128]), -32.0, A.add, "JT JL", "YJ1")
-    dma("a", T.yj[:, 0:1024], T.YJ[0:128:16, 0:1024], "o_j0", "YJ0", "")
-    dma("s", T.yj[:, 1024:2048], T.YJ[0:128:16, 1024:2048], "o_j1", "YJ1", "")
+    job["Na"] = lambda: landed("NB", NBK, 5, 3, "NV0", (0, 4))
+    job["Nu"] = lambda: unpack(3, "NV0", NAMES, 32, LATE)
+
+    def last_names():
+        pivots(cp, "NB", 5, "NV0", NBK, LATE)
+        dma("s", T.yn[:, :], T.NB[:, 16:2064], "o_n", NBK, "")
+    job["Nb"] = last_names
+    for r in range(8):
+        job["T%d" % r] = lambda r=r: won(cp, "JT", 2, r, "VJ")
+    for n in END.split():
+        job[n]()
+    act(T.JG[:, 0:128], BY_NAME["JT"].indirect(T.JL[:, 0:8]), "JT JL", "JG0")
+    cp(T.JG[:, 128:256], BY_NAME["JT"].indirect(T.JL[:, 8:16]), "JT JL", "JG1")
+    cp(at_places("JT", 0, ALL), T.JG[:, :], "JG0 JG1 " + of0, "JT")
+    dma("a", T.yj[:, :], T.JT[0:128:16, 16:2064], "o_j", "JT", "")
 
     for q in ("v", "t", "a", "g"):
         g.wait_ge(T.sem["e" + q], cnt[q])
-    for s in ("d_x", "d_n0", "d_n1", "d_n2", "d_l", "o_n", "o_x", "o_j0", "o_j1"):
+    for s in ("d_x", "d_n0", "d_n1", "d_n2", "d_l", "o_n", "o_x", "o_j"):
         g.wait_ge(T.sem[s], 16)
     for m in nloc:
         g.wait_ge(T.sem["l%d" % m], nloc[m])

from concourse.bass import DstId, RemoteDMATransfer
from concourse.mybir import AluOpType, AxisListType, ActivationFunctionType

W = 2368
BIG = 12582912.0
F, B, I, U = "float32", "bfloat16", "int32", "uint16"
SCRATCH = {}
for _names, _w, _d in (
        ("NB JT NE XE JF XO", W, F), ("XS", W, B), ("SA EQ XG XV MX RSM", 2048, B), ("QR", 2048, F),
        ("Q2 NS", 512, F), ("MM", 512, B), ("RSTB", 272, B), ("CMP CKR", 256, B), ("RST", 32, B), ("ONEB IDB NID M64 BO TRI HR HT HT0 PV PVB KB1 KB2 HI0 HI1", 128, B),
        ("IDF UN THR", 128, F), ("SB SF0 SF1 VF VJ KS RSK JM JG", 256, F), ("SAF", 2048, F), ("D16", 32, F), ("WT PR", 2, B), ("B16 WK", 16, B),
        ("PI PA LIMI AI AM", 1, I), ("PF LIMA LIMH", 1, F), ("COL", 8, F), ("CA CB CM CV IO16 KR", 16, F),
        ("LT VT0 VT1 VS0 VS1 QT0 QT1 OWN OWS SZ", 136, F), ("TQ0 TQ1", 128, F), ("OQ0 OQ1 UL", 128, U),
        ("OP N1 NM TM2 TL2 GM TM TL", 32, F), ("IO66 RL ED DX", 66, F), ("LW UW", 2, U), ("EP L16", 32, U), ("JE", 32, I),
        ("OF0 OF1 OF5 JL", 16, U), ("NV0 NV1 SV5", 256, U)):
    for _n in _names.split():
        SCRATCH[_n] = ("sbuf", [128, _w], _d)
VOFF, SIZES, NAMES = 0, 2, 34
SPAN = {0: (0, 66), 1: (0, 34), 4: (34, 68), 5: (0, 34), 3: (34, 68)}
CLAIM = {1: (4, 66), 2: (3, 66)}
FLAT = ()
N0 = 0
for _b in SPAN:
    SCRATCH["LD%d" % _b] = ("sbuf", [128, 256] if _b in FLAT else [128, 8, 72 if _b < 6 else 8], U)
for _b in range(8):
    SCRATCH["P%d" % _b] = ("psum", [128, 512], F)
SEMAPHORES = ["ev", "et", "ea", "eg", "d_x", "d_n0", "d_n1", "d_n2", "d_l", "o_n", "o_x", "o_j"]
SEMAPHORES += ["a%d_%d" % (m, r) for m in SPAN for r in range(8)] + ["l%d" % m for m in SPAN]
CUTS = {1: (52, 98), 2: (52, 98)}
SPLIT = {1: 118, 2: 116}
SUMS = (0, 5, 10, 16, 16)
ORDER = {1: "KR EP Qa Qb OP WK PAY PL PAD SZ 1 L16 QR1 QR2 QR3 TM Ma TL Mb UW JE Na ED Nb DX N1 CLAIMS NM NAMES 4",
         2: "KR EP Qa Qb OP WK PAY PL PAD SZ 5 L16 TM Ma TL Mb JP UW JE Na TM2 Nb TL2 N1 ED NM DX NAMES CLAIMS 3"}
GAPS = {(1, "sizes0"): "MX0 NB0a", (1, "sizes1"): "MX1", (1, "select"): "S0 OWN NB0b XO0", (1, "hits"): "S1 OS1 QR0", (1, "rank"): "S2 UN1", (1, "lanes"): "KS",
        (2, "sent"): "A0 NU1 A1 OF1 A2 SF1 A3 XE VF XO1", (2, "wait"): "",
        (2, "sizes0"): "MX0 NB1a", (2, "sizes1"): "MX1", (2, "select"): "S0 OWN NB1b J7 J6 J5 J4", (2, "hits"): "S1 OS2 J3 J2 J1 J0", (2, "rank"): "S2 UN2",
        (2, "lanes"): "KS", (3, "sent"): "NU2"}
END = "Na Nu T7 Nb T6 T5 T4 JL T3 T2 T1 T0"


def rank_program(g, core, T, topo):
    rank = T.rank_of(core)
    if rank is None:
        return
    A = AluOpType
    FN = ActivationFunctionType
    IDN = FN.Identity
    Q = {"v": g.vector, "t": g.tensor, "a": g.scalar, "g": g, "s": g.sync}
    cnt, wr, rd, nloc = {}, {}, {}, {}
    known = {q: {} for q in Q}

    def bank(k):
        return k[0] == "P" and k[1:].isdigit()

    def pre(q, R, Wk):
        evs = []
        for k in R:
            evs += wr.get(k, [])
            if bank(k):
                evs += [e for e in rd.get(k, []) if e[0] != q]
        for k in Wk:
            part = q == "t" or k[0] == "+"
            k = k.lstrip("+")
            evs += [e for e in wr.get(k, []) if not part or e[0] != q] + rd.get(k, [])
        top = {}
        for e in evs:
            top[e[1]] = max(top.get(e[1], 0), e[2])
        for e in sorted(evs, key=lambda e: -len(e[3])):
            if top[e[1]] == e[2] and known[q].get(e[1], 0) < e[2]:
                Q[q].wait_ge(T.sem[e[1]], e[2])
                for s, n in e[3].items():
                    known[q][s] = max(known[q].get(s, 0), n)
                known[q][e[1]] = e[2]

    def post(q, by, sem, n, R, Wk):
        ck = dict(known[by])
        ck[sem] = n
        ev = (q, sem, n, ck)
        Wk = [k.lstrip("+") for k in Wk]
        for k in Wk:
            wr[k] = [ev]
            rd[k] = []
        for k in R:
            if k not in Wk:
                rd[k] = [e for e in rd.get(k, []) if e[0] != q] + [ev]

    def op(q, f, R, Wk):
        R, Wk = R.split(), Wk.split()
        pre(q, R, Wk)
        cnt[q] = cnt.get(q, 0) + 1
        f().then_inc(T.sem["e" + q], 1)
        post(q, q, "e" + q, cnt[q], R, Wk)

    def dma(q, out, in_, sem, R, Wk):
        R, Wk = R.split(), Wk.split()
        pre(q, R, Wk)
        Q[q].dma_start(out, in_).then_inc(T.sem[sem], 16)
        post(sem, q, sem, 16, R, Wk)

    V = g.vector

    def cp(out, in_, R, Wk):
        op("v", lambda: V.tensor_copy(out=out, in_=in_), R, Wk)

    def ts(out, in0, s1, o0, R, Wk, s2=None, o1=None):
        if o1 is None:
            op("v", lambda: V.tensor_scalar(out=out, in0=in0, scalar1=s1, scalar2=None, op0=o0), R, Wk)
        else:
            op("v", lambda: V.tensor_scalar(out=out, in0=in0, scalar1=s1, scalar2=s2, op0=o0, op1=o1), R, Wk)

    def tt(out, in0, in1, o, R, Wk):
        op("v", lambda: V.tensor_tensor(out=out, in0=in0, in1=in1, op=o), R, Wk)

    def scan(out, d0, d1, init, o0, o1, R, Wk):
        op("v", lambda: V.tensor_tensor_scan(out=out, data0=d0, data1=d1, initial=init, op0=o0, op1=o1), R, Wk)

    def fill(ap, c, Wk):
        op("v", lambda: V.memset(ap, c), "", Wk)

    def mm(out, l, r, start, stop, R, Wk):
        op("t", lambda: g.tensor.matmul(out=out, lhsT=l, rhs=r, start=start, stop=stop), R, Wk)

    def act(out, in_, R, Wk, func=FN.Copy, bias=0.0, scale=1.0):
        op("a", lambda: g.scalar.activation(out=out, in_=in_, func=func, bias=bias, scale=scale), R, Wk)

    def silu(out, in_, R, Wk):
        op("a", lambda: g.scalar.activation(out=out, in_=in_, func=FN.Silu), R, Wk)

    def weave(*chains):
        for j in range(max(len(c) for c in chains)):
            for c in chains:
                if j < len(c):
                    c[j]()

    def iota(out, pat, base, cm, Wk):
        op("g", lambda: g.iota(out, pat, base, cm, allow_small_or_imprecise_dtypes=True), "", Wk)

    def asel(out, in_, pat, o, fl, base, cm, R, Wk):
        op("g", lambda: g.affine_select(out, in_, pat, o, fl, base, cm), R, Wk)

    cls = [rank, 8 + rank, rank]
    BLOCKS = ((0, 64), (64, 104), (104, 128))
    NBK = "NB0 NB1 NB2"
    TAB = {n: T[n][:, 0:W] for n in ("NB", "XO", "XS", "NE", "XE", "JT", "JF")}
    BY_NAME = {n: T[n][:, 16:W] for n in ("NE", "XE", "JT", "JF")}
    NEW, XEW, JFW = T.NE[:, 0:2080], T.XE[:, 0:2080], T.JF[:, 16:2080]

    dma("a", T.XS[:, 16:2064], T.xs[:, :], "d_x", "", "XS")
    for j, (a, b) in enumerate(BLOCKS):
        dma("s", T.NB[:, 16 + 16 * a:16 + 16 * b], T.nb[:, 16 * a:16 * b], "d_n%d" % j, "", "NB%d" % j)
    dma("a", T.LIMI[:, :], T.lim[:, :], "d_l", "", "LIMI")

    fill(T.ONEB[:, :], 1.0, "ONEB")
    fill(T.RSM[:, :], 256.0, "RSM")
    for a, b, src in ((0, 128, "ONEB"), (128, 2080, "RSM")):
        act(T.XE[:, a:b], T[src][:, 0:b - a], src, "+XE", func=FN.Silu, bias=30.0, scale=0.0)
    fill(T.XS[:, 0:16], 0.0, "+XSp")
    fill(T.XS[:, 2064:W], 0.0, "+XSp")
    op("g", lambda: g.iota(T.PI[:, :], [[0, 1]], 0, 1), "", "PI")
    asel(T.IDB[:, :], T.ONEB[:, :], [[-1, 128]], A.is_equal, 0.0, 0, 1, "ONEB", "IDB")
    iota(T.IO16[:, :], [[1, 16]], 0, 0, "IO16")
    iota(T.IO66[:, :], [[-16, 2], [1, 33]], -1, 0, "IO66")
    asel(T.BO[:, :], T.ONEB[:, :], [[-16, 8], [0, 16]], A.is_ge, 0.0, 0, 1, "ONEB", "BO")
    asel(T.BO[:, :], T.BO[:, :], [[16, 8], [0, 16]], A.is_ge, 0.0, 15, -1, "BO", "BO")
    asel(T.TRI[:, :], T.ONEB[:, :], [[1, 128]], A.is_ge, 0.0, 0, -1, "ONEB", "TRI")
    asel(T.TRI[:, :], T.TRI[:, :], [[-1, 128]], A.not_equal, 129.0, 0, 1, "TRI", "TRI")
    iota(T.WT[:, 0:1], [[0, 1]], -128, 1, "+WT")
    iota(T.WT[:, 1:2], [[0, 1]], -4096, 16, "+WT")
    iota(T.VT0[:, :], [[16, 136]], cls[0], 0, "VT0")
    iota(T.SB[:, :], [[-16, 2], [0, 8], [-1, 16]], 160, 0, "SB")
    iota(T.NE[:, 0:1440], [[0, 1440]], 2050, 0, "NEa")
    for n in ("QT0", "QT1"):
        fill(T[n][:, 128:136], 2048.0, n + "p")
    for n in ("OWN", "OWS"):
        fill(T[n][:, 128:136], 0.0, n + "p")
    fill(T.SZ[:, 128:136], 255.0, "SZp")
    fill(T.KB1[:, :], 131072.0, "KB1")
    resets = (("RST", 32, 16, 1.0, 0.0), ("RSK", 256, 16, 16777216.0, 63.0), ("RSTB", 272, 16, 0.0, 2.0))
    for n, w, step, c, c0 in resets:
        fill(T[n][:, :], c, n)
    for n, w, step, c, c0 in resets:
        fill(T[n][:, 0:w:step], c0, n)
    ts(T.PA[:, :], T.PI[:, :], 15, A.bitwise_and, "PI", "PA")
    cp(T.IDF[:, :], T.IDB[:, :], "IDB", "IDF")
    cp(T.PF[:, :], T.PA[:, :], "PA", "PF")
    ts(T.NID[:, :], T.IDB[:, :], -1.0, A.mult, "IDB", "NID")
    for j, b in enumerate((2080 + 32 * rank, 2096 + 32 * rank, 2320, 2336)):
        ts(T.COL[:, j:j + 1], T.PF[:, :], float(b), A.add, "PF", "+COL")
    TRV, TRE = [T.COL[:, 0:1], T.COL[:, 1:2]], [T.COL[:, 2:3], T.COL[:, 3:4]]
    ts(T.CB[:, :], T.IO16[:, :], T.PF[:, 0:1], A.is_equal, "IO16 PF", "CB")
    ts(T.CM[:, :], T.IO16[:, :], T.PF[:, 0:1], A.not_equal, "IO16 PF", "CM")
    ts(T.RL[:, :], T.IO66[:, :], T.PF[:, 0:1], A.is_gt, "IO66 PF", "RL")
    ts(T.CV[:, :], T.CB[:, :], 2050.0, A.mult, "CB", "CV")
    ts(T.CA[:, :], T.CB[:, :], -126976.0, A.mult, "CB", "CA", -4096.0, A.add)
    ts(T.M64[:, :], T.IDB[:, :], -64.0, A.mult, "IDB", "M64")

    def count_rows(ks):
        for k in ks:
            ts(T.SA[:, 128 * k:128 * k + 128], T.IDB[:, :], T.CA[:, k:k + 1], A.mult, "IDB CA", "+SA")
    count_rows(range(4))

    def names_of(t, a, b):
        return T.NB[:, 16 + 16 * a + cls[t]:16 + 16 * b:16]

    chips = []
    for r, c in enumerate(T.cores):
        if chips and topo.chip(T.cores[chips[-1][0]]) == topo.chip(c):
            chips[-1].append(r)
        else:
            chips.append([r])

    def far(r):
        i = [r in c for c in chips].index(True)
        j = chips[i].index(r)
        later = sorted(chips[i + 1:] + chips[:i], key=lambda c: topo.same_plane(topo.chip(T.cores[r]), topo.chip(T.cores[c[0]])))
        return [x for c in later for x in c[j:] + c[:j]]

    def slot(d, r):
        return 0 if r == d else 2 + far(r).index(d) if d in far(r) else 1

    near = [r for r in range(8) if r != rank and r not in far(rank)]
    fe = topo.engines(core, T.cores[far(rank)[0]])
    ne = [e for e in topo.engines(core, T.cores[near[0]]) if e not in fe][:2]

    def msg(m, j, a, n):
        if m in FLAT:
            return T["LD%d" % m][:, 32 * j:32 * j + 32]
        return T["LD%d" % m][:, j, a:a + n]

    def mine(m, a, n):
        return msg(m, 0, a, n)

    def key(m, r):
        return "M%d" % m if r == rank else "LD%d_%d" % (m, r)

    def repeat_names(names, rk, ks):
        for k in ks:
            act(T.QR[:, k:2048:16], names, rk + " CM CV", "+QR", func=IDN, bias=T.CV[:, k:k + 1], scale=T.CM[:, k:k + 1])

    def gather_sizes(q, lst, a, b):
        if a < b:
            f = cp if q == "v" else act
            f(T.XV[:, 16 * a:16 * b], T.XS[:, 0:2080].indirect(T[lst[:-2]][:, a:b]), "XS XSp " + lst, "XV%d" % a)

    def degrees(a, b, keys, mx):
        o = T.P2[:, a:b]
        for k in range(16):
            mm(o, T.IDB[:, :], T.XV[:, 16 * a + k:16 * b:16], k == 0, k == 15 and not mx, "IDB " + keys, "P2")
        if mx:
            mm(o, T.IDB[:, :], T.MX[:, 16 * a + 15:16 * b:16], False, True, "IDB MX%d" % (a // 64), "P2")

    gaps = {}

    def gap(t, at):
        for f in gaps.get((t, at), ()):
            f()

    def select(t):
        lim = "LIMA" if t else "LIMH"
        ts(T.HR[:, :], T.P2[:, 0:128], T[lim][:, 0:1], A.is_le, "P2 " + lim, "HR")
        mm(T.P3[:, 0:128], T.HR[:, :], T.BO[:, :], True, True, "HR BO", "P3")
        act(T.SZ[:, 0:128], T.P2[:, 0:128], "P2", "SZ", func=FN.Relu, bias=256.0 if t else 255.0, scale=-1.0)
        gap(t, "hits")
        ht = "HT" if t else "HT0"
        if t < 2:
            ts(T[ht][:, :], T.P3[:, 0:128], 9.0, A.is_ge, "P3", ht)
        else:
            tt(T.HT[:, :], T.P3[:, 0:128], T.THR[:, :], A.is_ge, "P3 THR", "HT")
        mm(T.P4[:, 0:128], T.TRI[:, :], T[ht][:, :], True, True, "TRI " + ht, "P4")
        gap(t, "rank")
        for b in range(2):
            tt(T.CMP[:, 128 * b:128 * b + 128], T.P4[:, 0:128], T.SB[:, 128 * b:128 * b + 128], A.is_equal, "P4 SB", "CMP%d" % b)
            mm(T.P5[:, 2 * b:2 * b + 2], T.CMP[:, 128 * b:128 * b + 128], T.WT[:, :], True, True, "CMP%d WT" % b, "P5")
        gap(t, "lanes")
        ts(T.LW[:, :], T.P5[:, 0:4:2], 128.0, A.add, "P5", "LW")

    def new_sizes(t):
        ts(mine(ahead[t], SIZES, 32), at_pivots("SZ"), -1.0, A.mult, "SZ SZp LW", "+M%d" % ahead[t], 255.0, A.add)

    ahead = [0, 1, 5]

    def places(t):
        for b in range(2):
            ts(mine(ahead[t], VOFF + b, 1), T.P5[:, 2 * b + 1:2 * b + 2], float(cls[t] + 4112), A.add, "P5 COL", "+M%d" % ahead[t], TRV[b], A.min)

    def at_pivots(buf):
        return T[buf][:, 0:136].indirect(T.LW[:, :])

    def send(m):
        a, b = SPAN[m]
        tr = []
        for rs, es in ((far(rank), fe), (near, ne)):
            ids = [DstId(rid=topo.addr(T.cores[r])[0], pnc=topo.addr(T.cores[r])[1]) for r in rs]
            tr.append(RemoteDMATransfer(dst_ids=ids, dma_engine_mask=sum(1 << e for e in es), remote_sem=T.sem["a%d_%d" % (m, rank)],
                                        srcs=[mine(m, a, b - a)], dsts=[msg(m, slot(r, rank), a, b - a) for r in rs]))
        pre("g", ["M%d" % m], [])
        g.remote_dma_fused(tr, local_sem=T.sem["l%d" % m])
        nloc[m] = len(fe) + len(ne)
        post("l%d" % m, "g", "l%d" % m, nloc[m], ["M%d" % m], [])
        for r in range(8):
            if r != rank:
                wr["LD%d_%d" % (m, r)] = [("r", "a%d_%d" % (m, r), len(ne) if r in near else len(fe), {})]

    ALL, EARLY, MID, LATE = (0, 8), (0, 1), (1, 4), (4, 8)

    def keys(m, part):
        return " ".join(key(m, r) for r in range(8) if part[0] <= slot(rank, r) < part[1])

    def parts(buf, part):
        return " ".join("%s_%d" % (buf, j) for j in range(*part))

    def unpack(m, buf, a, n, part, add=None):
        out, in_ = T[buf][:, n * part[0]:n * part[1]], T["LD%d" % m][:, part[0]:part[1], a:a + n]
        if add is None:
            cp(out, in_, keys(m, part), parts(buf, part))
        else:
            ts(out, in_, add, A.add, keys(m, part), parts(buf, part))

    def at_places(tab, m, part):
        return TAB[tab].indirect(T["OF%d" % m][:, 2 * part[0]:2 * part[1]])

    def pivots(f, tab, m, buf, wk, part=ALL, rk=None):
        f(at_places(tab, m, part), T[buf][:, 32 * part[0]:32 * part[1]], parts("OF%d" % m, part) + " " + (rk or parts(buf, part)), wk)

    def won(f, tab, t, r, buf):
        j, (m, a) = slot(rank, r), CLAIM[t]
        f(BY_NAME[tab].indirect(msg(m, j, a, 2)), T[buf][:, 32 * j:32 * j + 32], parts(buf, ALL) + " " + key(m, r), tab)

    def count():
        def total():
            ts(T.PR[:, :], T.P5[:, 0:4:2], -0.5, A.is_le, "P5", "PR")
            for b in range(2):
                mm(T.P2[:, 0:1], T.ONEB[:, :], T.PR[:, b:b + 1], b == 0, b == 1, "ONEB PR", "P2")
        return [total, lambda: cp(T.AI[:, :], T.P2[:, 0:1], "P2", "AI"),
                lambda: ts(T.AM[:, :], T.AI[:, :], 7, A.bitwise_and, "AI", "AM"),
                lambda: ts(T.LIMA[:, :], T.AM[:, :], T.LIMH[:, 0:1], A.add, "AM LIMH", "LIMA", 1.0, A.add)]

    def own_names():
        for h in range(2):
            act(T.OWN[:, 64 * h:64 * h + 64], T["P%d" % h][:, 0:64], "P%d" % h, "+OWN", func=FN.Abs, scale=1.0 / 4096)

    def empty_covered(t):
        def marks():
            for h in range(2):
                ts(T.UN[:, 64 * h:64 * h + 64], T["P%d" % h][:, 0:64], 0.0, A.is_lt, "P%d" % h, "UN%d" % h, 2048.0, A.mult)
        return [marks, lambda: tt(names_of(t, 0, 128), T.UN[:, :], names_of(t, 0, 128), A.max, "UN0 UN1 " + NBK, NBK)]

    def high_names(t):
        act(T["HI%d" % t][:, :], T["QT%d" % t][:, 0:128], "QT%d" % t, "HI%d" % t, func=IDN, bias=191.5078125, scale=1.0 / 64)

    def key_start(t):
        hi, qt = "HI%d" % t, "QT%d" % t
        mm(T.P6[:, 0:256], T.IDB[:, :], T.CKR[:, :], True, False, "IDB CKR", "P6")
        mm(T.P6[:, 0:128], T[hi][:, :], T.IDB[:, :], False, False, "IDB " + hi, "P6")
        mm(T.P6[:, 128:256], T[hi][:, :], T.M64[:, :], False, False, "M64 " + hi, "P6")
        mm(T.P6[:, 128:256], T[qt][:, 0:128], T.IDF[:, :], False, False, "IDF " + qt, "P6")

    def key_sums(ks):
        for k in ks:
            mm(T.P6[:, k:256:16], T.XG[:, k:2048:16], T.B16[:, :], False, k == 15, "XG B16", "P6")

    def at_lists():
        for b in range(2):
            mm(T.P7[:, 16 * b:16 * b + 16], T.CMP[:, 128 * b:128 * b + 128], T.WK[:, :], True, True, "CMP%d WK" % b, "P7")

    best = dict(KS=lambda: scan(T.KS[:, :], T.RSK[:, :], T.P6[:, 0:256], 63.0, A.min, A.max, "RSK P6", "KS"),
                KR=lambda: ts(T.KR[:, :], T.KS[:, 15:256:16], BIG * 128, A.add, "KS", "KR", BIG * 128, A.subtract),
                WK=lambda: tt(T.WK[:, :], T.KS[:, 15:256:16], T.KR[:, :], A.subtract, "KS KR", "WK"), PAY=at_lists)

    def element_sizes(t):
        oq = "OQ%d" % (t % 2)
        act(T.XG[:, :], XEW.indirect(T[oq][:, :]), "XE " + ("OQ1" if t == 1 else "OQ0_0 OQ0_1 OQ0_2"), "XG", func=IDN, bias=-31.0)

    def lanes_to_pivots(t):
        qt, oq, kb = "QT%d" % (t % 2), "OQ%d" % (t % 2), "KB%d" % t
        ok = "OQ1" if t == 1 else "OQ0_0 OQ0_1 OQ0_2"

        def cover(a, b, k):
            tt(T.EQ[:, 16 * a:16 * b], NEW.indirect(T[oq][:, a:b]), T.QR[:, 16 * a:16 * b], A.is_equal, "NE QR " + ok, k)
        cover(0, 64, "EQ0")
        cover(64, SPLIT[t], "EQ1")
        for h in range(2):
            o = T["P%d" % h][:, 0:64]
            mm(o, T.IDF[:, :], T[qt][:, 64 * h:64 * h + 64], True, False, "IDF " + qt, "P%d" % h)
            mm(o, T.IDB[:, :], T[kb][:, 64 * h:64 * h + 64], False, False, "IDB " + kb, "P%d" % h)
        gap(t, "start")
        for h in range(2):
            if h:
                ts(T.UL[:, 0:64], T.P0[:, 0:64], 16.0, A.add, "P0", "UL_0", 2064.0, A.min)
                cover(SPLIT[t], 128, "EQ2")
            for k in range(16):
                mm(T["P%d" % h][:, 0:64], T.SA[:, 128 * k:128 * k + 128], T.EQ[:, 1024 * h + k:1024 * h + 1024:16], False, k == 15,
                   "SA " + ("EQ1 EQ2" if h else "EQ0"), "P%d" % h)
            gap(t, "cover%d" % h)
        cuts = CUTS[t]
        for h, cut in enumerate(cuts):
            if h:
                gap(t, "list")
                ts(T.UL[:, 64:128], T.P1[:, 0:64], 16.0, A.add, "P1", "UL_1", 2064.0, A.min)
            gather_sizes("a", "UL_%d" % h, 64 * h, cut)
            gather_sizes("v", "UL_%d" % h, cut, 64 * h + 64)
            gap(t, "sizes%d" % h)
        for h, cut in enumerate(cuts):
            degrees(64 * h, 64 * h + 64, "XV%d" % (64 * h) + (" XV%d" % cut if cut % 64 else ""), True)
        gap(t, "select")
        select(t)

    def pivots_make(t, more):
        qt, vs, tq, half, pb = "QT%d" % (t % 2), "VS%d" % (t % 2), "TQ%d" % (t % 2), [slice(0, 256), slice(256, 512)], ["P3", "P4"]
        mn, (mc, ca) = [None, 4, 3][t], CLAIM[t]
        tl = "TL" if t == 1 else "TL2"
        col = [T[tl][:, 15:16], T[tl][:, 31:32]]

        def names(h):
            act(T.Q2[:, half[h]], NEW.indirect(T.EP[:, 16 * h:16 * h + 16]), "NE EP", "Q2_%d" % h, scale=1.0 / 4096)
            mm(T[pb[h]][:, 0:257], T.IDB[:, :], T.RSTB[:, 0:257], True, False, "IDB RSTB", pb[h])

        def itself(h):
            tt(T.MM[:, half[h]], T[vs][:, 0:136].indirect(T.L16[:, 16 * h:16 * h + 16]), T.Q2[:, half[h]], A.is_equal, "%s L16 Q2_%d" % (vs, h), "MM%d" % h)
            mm(T[pb[h]][:, 1:257], T.IDB[:, :], T.MM[:, half[h]], False, False, "IDB MM%d" % h, pb[h])
            mm(T[pb[h]][:, 0:256], T.NID[:, :], T.MM[:, half[h]], False, True, "NID MM%d" % h, pb[h])

        def least(h):
            scan(T.NS[:, half[h]], T[pb[h]][:, 0:256], T.Q2[:, half[h]], 2.0, A.add, A.min, "%s Q2_%d" % (pb[h], h), "NS%d" % h)

        def same():
            for b in range(2):
                ts(T.ED[:, 33 * b:33 * b + 32], T.JE[:, :], col[b], A.is_equal, "JE " + tl, "+ED", 4096.0, A.mult)

        def out():
            for b in range(2):
                ts(mine(mc, ca + b, 1), T.DX[:, 33 * b + 32:33 * b + 33], col[b], A.max, "DX COL " + tl, "+M%d" % mc, TRE[b], A.min)

        step = dict(
            EP=lambda: ts(T.EP[:, :], at_pivots(qt), 16.0, A.add, "%s %sp LW" % (qt, qt), "EP"),
            L16=lambda: cp(T.L16[:, :], at_pivots("LT"), "LT LW", "L16"),
            PL=lambda: places(t), SZ=lambda: new_sizes(t), Qa=lambda: names(0), Qb=lambda: names(1), Ma=lambda: itself(0), Mb=lambda: itself(1),
            Na=lambda: least(0), Nb=lambda: least(1),
            OP=lambda: act(T.OP[:, :], at_pivots("OWS"), "OWS OWSp LW", "OP", func=IDN, bias=1.0),
            N1=lambda: tt(T.N1[:, :], T.NS[:, 15:512:16], T.MM[:, 15:512:16], A.add, "NS0 NS1 MM0 MM1", "N1"),
            NM=lambda: tt(T.NM[:, :], T.N1[:, :], T.OP[:, :], A.min, "N1 OP", "NM"),
            NAMES=lambda: ts(mine(mn, NAMES, 32), T.NM[:, :], 4096.0, A.mult, "NM", "+M%d" % mn, 2048.0, A.min),
            TM=lambda: tt(T.TM[:, :], T.P7[:, 0:32], T.GM[:, :], A.mult, "P7 GM", "TM"),
            TL=lambda: scan(T.TL[:, :], T.RST[:, 0:32], T.TM[:, :], 0.0, A.mult, A.add, "RST TM", "TL"),
            UW=lambda: ts(T.UW[:, :], T.TL[:, 15:32:16], 2048.0, A.min, "TL", "UW"),
            JE=lambda: ts(T.JE[:, :], JFW.indirect(T.UW[:, :]), -32.0, A.add, "JF UW", "JE"),
            TM2=lambda: tt(T.TM2[:, :], T.JE[:, :], T.D16[:, 0:32], A.mult, "JE D16", "TM2"),
            TL2=lambda: scan(T.TL2[:, :], T.RST[:, 0:32], T.TM2[:, :], 0.0, A.mult, A.add, "RST TM2", "TL2"),
            PAD=lambda: act(T.ED[:, 32:66:33], T.P5[:, 0:4:2], "P5", "EDp", func=FN.Relu, bias=4096.0, scale=4096.0),
            ED=same, DX=lambda: scan(T.DX[:, :], T.RL[:, :], T.ED[:, :], 0.0, A.mult, A.max, "RL ED EDp", "DX"), CLAIMS=out, **more)
        for name in ORDER[t].split():
            if name.isdigit():
                send(int(name))
            else:
                step[name]()

    def sizes_out(a, b):
        act(T.XO[:, a:b], T.XS[:, a:b], "XS", "XO_%d" % a, func=IDN, bias=32.0)

    got = []
    for j, (a, b) in enumerate(BLOCKS):
        c = (a + b) // 2
        ts(T.OQ0[:, a:b], names_of(0, a, b), 16.0, A.add, "NB%d" % j, "OQ0_%d" % j)
        gather_sizes("a", "OQ0_%d" % j, a, c)
        gather_sizes("v", "OQ0_%d" % j, c, b)
        got += ["XV%d" % a, "XV%d" % c]
        if b % 64 == 0:
            degrees(b - 64, b, " ".join(got[-4:]), False)
        if j == 1:
            ts(T.LIMH[:, :], T.LIMI[:, :], 0.5, A.add, "LIMI", "LIMH")
    act(T.UN[:, :], names_of(0, 0, 128), NBK, "UN0 UN1", func=IDN, bias=2048.0, scale=-1.0)
    repeat_names(names_of(1, 0, 128), NBK, range(3))
    tt(T.TQ0[:, 0:128], names_of(0, 0, 128), T.VT0[:, 0:128], A.not_equal, NBK + " VT0", "TQ0")
    tt(T.OWN[:, 0:128], T.TQ0[:, 0:128], T.UN[:, :], A.mult, "TQ0 UN0 UN1", "OWN")
    gaps[0, "rank"] = [lambda: fill(T.RSM[:, 0:2048:16], 1.0, "RSM")]
    gaps[0, "hits"] = [lambda: ts(T.OQ1[:, :], names_of(1, 0, 128), 16.0, A.add, NBK, "OQ1"),
                       lambda: act(T.QT1[:, 0:128], names_of(1, 0, 128), NBK, "QT1"), lambda: repeat_names(names_of(1, 0, 128), NBK, range(3, 16))]
    gaps[0, "lanes"] = [lambda: ts(T.PV[:, :], T.P4[:, 0:128], 160.0, A.is_le, "P4", "PV")]
    select(0)
    places(0)
    new_sizes(0)
    if N0:
        send(0)
    ts(mine(N0, NAMES, 32), at_pivots("OWN"), -1.0, A.mult, "OWN OWNp LW", "+M%d" % N0, 2048.0, A.add)
    send(N0)

    iota(T.NE[:, 1440:2080], [[0, 640]], 2050, 0, "NEb")
    iota(T.CKR[:, :], [[12480, 2], [0, 8], [-128, 16]], 1728, 0, "CKR")
    iota(T.VT1[:, :], [[16, 136]], cls[1], 0, "VT1")
    iota(T.LT[:, :], [[1, 136]], 0, 0, "LT")
    iota(T.JF[:, :], [[1, W]], 16, 0, "JF")
    iota(T.JF[:, 2064:2065], [[0, 1]], 4128, 0, "JF")

    def select_row(ks):
        for k in ks:
            asel(T.SAF[:, 128 * k:128 * k + 128], T.IDF[:, :], [[0, 8], [1, 16]], A.is_equal, 0.0, -k, 0, "IDF", "+SAF")
    select_row(range(8))
    wr["NE"] = wr["NEa"] + wr["NEb"]
    high_names(1)
    sizes_out(16, 1040)
    weave(count(), [lambda: count_rows(range(4, 8)), lambda: count_rows(range(8, 12)), lambda: count_rows(range(12, 16))])
    for h in range(2):
        ts(T.B16[:, 8 * h:8 * h + 8], T.BO[:, 0:128:16], 2048.0, A.mult, "BO", "+B16")
    cp(T.QT0[:, 0:128], names_of(0, 0, 128), NBK, "QT0")
    key_start(1)
    ts(T.XO[:, 1040:2064], T.XS[:, 1040:2064], 32.0, A.add, "XS", "XO_1040")
    wr["XO"] = wr["XO_16"] + wr["XO_1040"]
    for j, c in enumerate((64.0, 1.0, 64.0, 1.0)):
        act(T.GM[:, 8 * j:8 * j + 8], T.BO[:, 0:128:16], "BO", "+GM", scale=c)
    tt(T.PVB[:, :], T.PV[:, :], T.HT0[:, :], A.mult, "PV HT0", "PVB")
    mm(T.P7[:, 0:128], T.PVB[:, :], T.IDB[:, :], True, True, "PVB IDB", "P7")
    tt(T.TQ1[:, 0:128], names_of(1, 0, 128), T.VT1[:, 0:128], A.not_equal, NBK + " VT1", "TQ1")
    act(T.THR[:, :], T.PVB[:, :], "PVB", "THR", func=IDN, bias=9.0, scale=100.0)
    act(T.KB2[:, :], T.P7[:, 0:128], "P7", "KB2", func=IDN, bias=131072.0, scale=131072.0)
    for h in range(2):
        act(T.D16[:, 16 * h:16 * h + 16], T.CB[:, :], "CB", "+D16")
    for t in (1, 0):
        act(T["VS%d" % t][:, :], T["VT%d" % t][:, :], "VT%d" % t, "VS%d" % t, scale=1.0 / 4096)
    high_names(0)

    def landed(tab, wk, mo, mn, buf, part):
        unpack(mn, buf, NAMES, 32, part)
        pivots(cp, tab, mo, buf, wk, part)

    for part in (EARLY, MID, LATE):
        unpack(0, "OF0", VOFF, 2, part)
        unpack(0, "SF0", SIZES, 32, part, 32.0)
        pivots(silu, "XE", 0, "SF0", "XE", part)
        landed("NE", "NE", 0, 0, "NV0", part)
    element_sizes(1)

    def names_0(part):
        pivots(cp, "NB", 0, "NV0", NBK, part)
    of0 = parts("OF0", ALL)

    def j_list():
        act(T.JM[:, :], at_places("JF", 0, ALL), "JF " + of0, "JM")
        for k in range(16):
            mm(T.P0[:, 0:16], T.SAF[:, 128 * k:128 * k + 128], T.JM[:, k:256:16], k == 0, k == 15, "SAF JM", "P0")

    def names_1(tab, wk, part):
        pivots(cp, tab, 1, "NV1", wk, part)
    job = dict(best, OWN=own_names,
               NB0=lambda: names_0(ALL), NB1=lambda: names_1("NB", NBK, ALL),
               NB0a=lambda: names_0((0, 2)), NB0b=lambda: names_0((2, 8)),
               NB1a=lambda: names_1("NB", NBK, (0, 2)), NB1b=lambda: names_1("NB", NBK, (2, 8)),
               XO0=lambda: pivots(silu, "XO", 0, "SF0", "XO"), XO1=lambda: pivots(silu, "XO", 1, "SF1", "XO"),
               OF1=lambda: unpack(1, "OF1", VOFF, 2, ALL), SF1=lambda: unpack(1, "SF1", SIZES, 32, ALL, 32.0),
               VF=lambda: cp(T.VF[:, :], at_places("JF", 1, ALL), "JF " + parts("OF1", ALL), parts("VF", ALL)),
               XG=lambda: element_sizes(2), XE=lambda: pivots(silu, "XE", 1, "SF1", "XE"),
               JP=j_list, JL=lambda: ts(T.JL[:, :], T.P0[:, 0:16], -31.75, A.add, "P0", "JL"))
    for h in range(2):
        job["MX%d" % h] = lambda h=h: scan(T.MX[:, 1024 * h:1024 * h + 1024], T.RSM[:, 0:1024], T.XG[:, 1024 * h:1024 * h + 1024], 1.0, A.min, A.max,
                                           "RSM XG", "MX%d" % h)
    for j in range(4):
        job["S%d" % j] = lambda j=j: key_sums(range(SUMS[j], SUMS[j + 1]))
        job["QR%d" % j] = lambda j=j: repeat_names(T.QT0[:, 0:128], "QT0", range(4 * j, 4 * j + 4))
    for r in range(8):
        job["J%d" % r] = lambda r=r: won(silu, "JF", 1, r, "VF")
    for t in (1, 2):
        job["UN%d" % t], job["NU%d" % t] = empty_covered(t)
        job["OS%d" % t] = lambda tq="TQ%d" % (t % 2): tt(T.OWS[:, 0:128], T.OWN[:, 0:128], T[tq][:, :], A.subtract, "OWN " + tq, "OWS")
    for j, f in enumerate(count()):
        job["A%d" % j] = f
    for at, names in GAPS.items():
        gaps[at] = [job[n] for n in names.split()]
    lanes_to_pivots(1)
    pivots_make(1, job)
    key_start(0)
    iota(T.JT[:, :], [[1, W]], -16, 0, "JT")
    select_row(range(8, 16))

    gap(2, "sent")
    for r in range(7, -1, -1):
        won(silu, "XE", 1, r, "SF1")
    element_sizes(2)
    gap(2, "wait")
    for part in (EARLY, MID):
        landed("NE", "NE", 1, 4, "NV1", part)
    for r in range(7, -1, -1):
        j = slot(rank, r)
        cp(BY_NAME["NE"].indirect(msg(CLAIM[1][0], j, CLAIM[1][1], 2)), msg(4, j, NAMES, 32), key(4, r) + " " + key(CLAIM[1][0], r), "NE")
        if r == 1:
            unpack(4, "NV1", NAMES, 32, LATE)
    names_1("NE", "NE", LATE)
    lanes_to_pivots(2)
    pivots_make(2, job)

    act(T.XS[:, 16:2064], T.XO[:, 16:2064], "XO", "XS", func=FN.Relu, bias=-32.0002)
    gap(3, "sent")
    unpack(5, "OF5", VOFF, 2, ALL)
    unpack(5, "SV5", SIZES, 32, ALL)
    act(T.VJ[:, :], at_places("JT", 5, ALL), "JT " + parts("OF5", ALL), parts("VJ", ALL))
    pivots(cp, "XS", 5, "SV5", "XS XSp")
    dma("a", T.yx[:, :], T.XS[:, 16:2064], "o_x", "XS", "")

    job["Na"] = lambda: landed("NB", NBK, 5, 3, "NV0", (0, 4))
    job["Nu"] = lambda: unpack(3, "NV0", NAMES, 32, LATE)

    def last_names():
        pivots(cp, "NB", 5, "NV0", NBK, LATE)
        dma("s", T.yn[:, :], T.NB[:, 16:2064], "o_n", NBK, "")
    job["Nb"] = last_names
    for r in range(8):
        job["T%d" % r] = lambda r=r: won(cp, "JT", 2, r, "VJ")
    for n in END.split():
        job[n]()
    act(T.JG[:, 0:128], BY_NAME["JT"].indirect(T.JL[:, 0:8]), "JT JL", "JG0")
    cp(T.JG[:, 128:256], BY_NAME["JT"].indirect(T.JL[:, 8:16]), "JT JL", "JG1")
    cp(at_places("JT", 0, ALL), T.JG[:, :], "JG0 JG1 " + of0, "JT")
    dma("a", T.yj[:, :], T.JT[0:128:16, 16:2064], "o_j", "JT", "")

    for q in ("v", "t", "a", "g"):
        g.wait_ge(T.sem["e" + q], cnt[q])
    for s in ("d_x", "d_n0", "d_n1", "d_n2", "d_l", "o_n", "o_x", "o_j"):
        g.wait_ge(T.sem[s], 16)
    for m in nloc:
        g.wait_ge(T.sem["l%d" % m], nloc[m])
